import numpy as np, ml_dtypes
CORES = [36,164,52,180,100,228,116,244]
N = 8
import mx_ref
BF = ml_dtypes.bfloat16
def gcols(t, e):
    v = np.concatenate([t.reshape(8, 16, -1, 4), np.zeros((8, 16, 1, 4), BF)], axis=2)
    return np.ascontiguousarray(np.stack([v[g][:, e[g]] for g in range(8)])).reshape(128, -1)
def cut(t, i, w=512):
    return t[:, w * i:w * i + w]
def pick(q, e):
    c = np.concatenate([q[0].reshape(128, -1, 4), np.zeros((128, 1, 4), np.uint8)], axis=1); s = np.concatenate([q[1], np.ones((16, 1), np.uint8)], axis=1)
    return (np.ascontiguousarray(c[:, e].reshape(128, -1)), np.ascontiguousarray(s[:, e]))
def join(*qs):
    return (np.concatenate([q[0] for q in qs], axis=1), np.concatenate([q[1] for q in qs], axis=1))
def put(q, e, v):
    c, s = q[0].reshape(128, -1, 4).copy(), q[1].copy(); c[:, e] = v[0].reshape(128, -1, 4); s[:, e] = v[1]
    return (c.reshape(128, -1), s)
def pk(c, s):
    return (np.ascontiguousarray(c), mx_ref.live(s))
def emit(q):
    return q[0], q[1]
def packed(v, rng):
    q = [mx_ref.quantize(np.ascontiguousarray(v[r])) for r in range(N)]
    return np.stack([a for a, b in q]), np.stack([mx_ref.plane(b, rng) for a, b in q])
def values_of_codes():
    e, c = np.zeros((128, 128, 4), np.float32), np.zeros((128, 2, 4), np.uint8)
    e[np.arange(128), np.arange(128), 0] = 1
    c[:127, :, 0] = np.arange(256).reshape(2, 128).T[:127]
    return mx_ref.matmul(mx_ref.quantize(e.reshape(128, 512).astype(BF)), (c.reshape(128, 8), np.full((16, 2), 127, np.uint8))).T.reshape(-1).astype(np.float64)
CODE_VALUE, SCALE_VALUE = values_of_codes(), 2.0 ** (np.arange(256) - 127.0)
def decode(q):
    return (CODE_VALUE[q[0]].reshape(16, 8, -1, 4) * SCALE_VALUE[q[1]][:, None, :, None] + 0.0).reshape(128, -1).astype(np.float32)
def f(rng, *shape):
    return mx_ref.flush((rng.standard_normal(shape, dtype=np.float32) * np.exp2(rng.integers(-2, 3, shape[:-1] + (1,)))).astype(BF))
def wide(rng, *shape, cols=0):
    v = rng.standard_normal(shape, dtype=np.float32) * np.exp2(rng.integers(-12, 13, shape)).astype(np.float32)
    if cols: v *= np.repeat(np.exp2(rng.integers(-cols, cols + 1, shape[:-2] + (1, shape[-1] // 4))) * (rng.random(shape[:-2] + (1, shape[-1] // 4)) > 0.0625), 4, axis=-1).astype(np.float32)
    return mx_ref.flush(v.astype(BF))
C, S, L, R = 384, 32, 12, 2
def layer(lay, q, k):
    return np.stack([np.maximum(mx_ref.matmul(w, q), np.float32(0.0)) * np.float32(k) for w in lay], axis=2).reshape(128, -1)
def seams(e):
    e = e.reshape(N, 8, S, L)
    m, back = e[:, 0], []
    for g in range(1, 8):
        w = np.pad(m, ((0, 0), (0, 0), (1, 1)), constant_values=np.inf)
        three = np.stack([w[:, :, :-2], m, w[:, :, 2:]])
        back.append(np.argmin(three, axis=0) + np.arange(L) - 1)
        m = np.maximum(e[:, g], np.min(three, axis=0))
    p = [np.argmin(m, axis=2)]
    for b in back[::-1]: p.insert(0, np.take_along_axis(b, p[0][:, :, None], axis=2)[:, :, 0])
    return np.stack(p, axis=1) + L * np.arange(S), np.min(m, axis=2)
def edited(p, dear):
    key = np.concatenate([np.tile(2 * np.arange(C), (8, 1)), 2 * p + 1], axis=1)
    gone = np.zeros((8, C + S), bool)
    gone[:, C:] = ~dear
    np.put_along_axis(gone, p, gone[:, C:].copy(), axis=1)
    return np.argsort(np.where(gone, 2 * C, key), axis=1, kind="stable")[:, :C + S - 2 * np.count_nonzero(~dear)]
def numbers_of(rng):
    return {"x": np.array(f(rng, N, 128, 4 * C)), "u": np.array(f(rng, N, 128, 512)), "v": np.array(f(rng, N, 128, 512))}
def weights(w, rng):
    c, p = packed(np.stack([w] * N), rng)
    return {"wc": c, "ws": p}
def unit(k, rng, fill=False):
    w = np.zeros((128, 4, 128, 4), np.float32)
    i = np.arange(128)
    for b in range(4): w[i, b, i, b] = k
    if fill:
        h = np.arange(0, 128, 16)
        w[h + 2, 0, h + 2, 0] = 0
        w[h, 0, h + 2, 0] = k
    return weights(w.reshape(128, 2048).astype(BF), rng)
def setup_inputs(rng):
    return {**numbers_of(rng), **weights(f(rng, 128, 2048), rng)}
def setup_inputs_ties(rng):
    d = numbers_of(rng)
    o = rng.permutation(N)
    x = d["x"].reshape(N, 8, 16, C, 4)
    a = x[0, :, :8, :3].copy()
    a[:, :, 2] = 0
    for r in range(N):
        for g in range(8):
            k = np.zeros(C, int) if r == o[0] else np.minimum(rng.permutation(C) % 4, 2)
            x[r, g, :8] = a[g][:, k]
    x[o[1], :, :8] = 0
    u = d["u"].reshape(N, 8, 16, 128, 4)
    w = np.array(f(rng, 128, 2048)).reshape(8, 16, 4, 8, 16, 4)
    for g in range(8):
        a = u[0, g, :8, 16 * g].copy()
        u[:, :, :, 16 * g] = 0
        u[:, g, :8, 16 * g] = a
        a = w[g, :8, :, g, :8].copy()
        w[:, :, :, g, :8] = 0
        w[g, :8, :, g, :8] = a
    return {"x": x.reshape(N, 128, 4 * C), "u": u.reshape(N, 128, 512), "v": d["v"], **weights(w.reshape(128, 2048), rng)}
def setup_inputs_near(rng):
    d = numbers_of(rng)
    x = d["x"].astype(np.float32).reshape(N, 8, 16, C, 4)
    s = rng.integers(0, 256, (N, 8, C))
    g = ((s[..., None] >> np.arange(8)) & 1) * np.exp2(np.arange(8) - 30.0)
    x[:, :, 0] = 0
    x[:, :, 0, :, 0] = 2.0 ** -7
    x[:, :, 1:8] = rng.integers(4, 8, (N, 8, 7, C, 4)) * rng.choice([-1.0, 1.0], (N, 8, 7, C, 4)) * 2.0 ** -9
    x[:, :, 1:3] = 0
    x[:, :, 1, :, 0] = 2.0 ** -16
    x[:, :, 8] = g[..., :4]
    x[:, :, 9] = g[..., 4:]
    x[:, :, 10:] = rng.integers(4, 8, (N, 8, 6, C, 4)) * rng.choice([-1.0, 1.0], (N, 8, 6, C, 4)) * 2.0 ** -27
    k = np.where(np.arange(N) < N // 2 - 1, 1.0, 2.0 ** -30).astype(np.float32).astype(BF)
    j = L * int(rng.integers(S))
    x[int(rng.integers(N // 2 - 1)), :, 0, j:j + L, 0] = 2.0 ** 27
    u = d["u"].reshape(N, 128, 128, 4)
    u[:, :, ::16] = 0
    for h in range(0, 128, 16):
        u[:, h:h + 2, h, 0] = k[:, None]
        u[:, h + 8:h + 10, h] = k[:, None, None]
        u[N // 2 - 1, h + 2, h, 0] = k[N // 2 - 1]
    return {"x": x.reshape(N, 128, 4 * C).astype(BF), "u": u.reshape(N, 128, 512), "v": d["v"], **unit(32, rng, True)}
def setup_inputs_huge(rng):
    d = numbers_of(rng)
    x = 2.0 ** 30 * (0.85 + 0.15 * rng.random((N, 128, C, 4)))
    x[N // 2:] -= 2.0 ** 28
    c = np.stack([rng.permutation(C) % 2 * 2.0 - 1.0 for r in range(N)])
    c[rng.permutation(N) < N // 2] = -1
    x *= c[:, None, :, None]
    s = np.stack([rng.permutation(8) % 2 * 2.0 - 1.0 for r in range(N)])
    u = d["u"].reshape(N, 128, 128, 4)
    u[:, :, ::16] = (2.0 ** 30 * (1 - 0.1 * rng.random((N, 128, 8, 4))) * s[:, None, :, None]).astype(np.float32).astype(BF)
    return {"x": x.astype(np.float32).reshape(N, 128, 4 * C).astype(BF), "u": u.reshape(N, 128, 512), "v": d["v"], **unit(-16, rng)}
def setup_inputs_caps(rng):
    d = numbers_of(rng)
    x = d["x"].astype(np.float32).reshape(N, 8, 16, C, 4)
    e = 1 + rng.random((N, 8, C))
    g = np.arange(8)[:, None]
    for r in range(N):
        k, a = rng.permutation(S) % 4, rng.integers(0, L - 7, S)
        way = np.where(k == 0, a + g, np.where(k == 1, a + 7 - g, np.where(k == 2, 0, L - 1))) + L * np.arange(S)
        np.put_along_axis(e[r], way, 2.0 ** -4, axis=1)
    x[:, :, 0] = 0
    x[:, :, 0, :, 0] = e
    k = np.where(np.arange(N) < N // 2, 2.0 ** -12, 1.0)
    s = np.stack([rng.permutation(8) % 2 * 2.0 - 1.0 for r in range(N)])
    u = d["u"].reshape(N, 128, 128, 4)
    u[:, :, ::16] = 0
    for h in range(0, 128, 16): u[:, h, h, 0] = (k * s[:, h // 16]).astype(np.float32).astype(BF)
    return {"x": mx_ref.flush(x.reshape(N, 128, 4 * C).astype(BF)), "u": u.reshape(N, 128, 512), "v": d["v"], **unit(32, rng)}
def setup_inputs_spread(rng):
    d = setup_inputs(rng)
    d["x"] = wide(rng, N, 128, 4 * C, cols=6)
    return d
def check_inputs(d):
    b = []
    for k in ("x", "u", "v"):
        a = np.abs(d[k].astype(np.float32))
        if not (np.isfinite(a).all() and ((a == 0) | (a >= 2.0 ** -30) & (a <= 2.0 ** 30)).all()): b.append("a value of " + k)
    if (d["wc"] != d["wc"][:1]).any(): b.append("wc differs between ranks")
    s = [mx_ref.live(p) for p in d["ws"]]
    if any((p != s[0]).any() for p in s): b.append("ws differs between ranks")
    if (d["wc"] % 128 == 127).any(): b.append("wc: a code that is no number")
    with np.errstate(over="ignore"):
        a = np.abs(decode(pk(d["wc"][0], d["ws"][0])))
    if not ((a == 0) | (a >= 2.0 ** -30) & (a <= 2.0 ** 30)).all(): b.append("a number of W")
    return b
def reference(x, u, v, wc, ws):
    q = pk(wc[0], ws[0])
    lay = [pick(q, np.arange(128 * b, 128 * b + 128)) for b in range(4)]
    qu = [mx_ref.quantize(u[r]) for r in range(N)]
    now = [x[r] for r in range(N)]
    for t in range(R):
        held, e = [], np.zeros((N, 8, C), np.float32)
        for r in range(N):
            q = mx_ref.quantize(now[r])
            held.append(decode(q).astype(BF))
            e[r] = np.abs(mx_ref.matmul(qu[r], q)[::16])
        p, cost = seams(e)
        dear = np.ones(N * S, bool)
        dear[np.argsort(cost.reshape(-1), kind="stable")[:N * S // 2]] = False
        dear = dear.reshape(N, S)
        row = []
        for r in range(N):
            h = layer(lay, mx_ref.quantize(gcols(held[r], p[r])), 0.03125).astype(BF)
            row.append(gcols(np.concatenate([held[r], h], axis=1), edited(p[r], dear[r])))
        row = np.concatenate(row, axis=1)
        for r in range(N):
            q = mx_ref.quantize(np.ascontiguousarray(cut(row, r, 4 * C)))
            now[r] = (decode(q) + layer(lay, q, 0.015625)).astype(BF)
    y, ol = np.zeros((N, 128, C), np.float32), np.zeros((N, 8, S), np.float32)
    oc, osc = np.zeros((N, 128, 4 * C), np.uint8), np.zeros((N, 16, C), np.uint8)
    for r in range(N):
        q = mx_ref.quantize(now[r])
        y[r] = mx_ref.matmul(mx_ref.quantize(v[r]), q)
        ol[r] = p[r]
        oc[r], osc[r] = emit(q)
    return {"y": y, "ol": ol, "oc": oc, "osc": osc}

@@ -1,0 +1,634 @@
+import numpy as np
+from concourse.bass import DstId, RemoteDMATransfer
+from concourse.mybir import dt, AluOpType, AxisListType, ActivationFunctionType
+
+N, C, S, L, R = 8, 384, 32, 12, 2
+BIG = 1.0e29
+OWN = 16 * L
+HB = 64 * L
+FW = HB + 64
+PADC = 256
+PIECES = ((0, 192), (192, 384))
+F32, BF, I32, U16, MX, U8 = "float32", "bfloat16", "int32", "uint16", "float8_e4m3fn_x4", "uint8"
+
+SCRATCH = {}
+
+
+def _sb(d, shape, names):
+    for n in names.split():
+        SCRATCH[n] = ("sbuf", [128] + shape, d)
+
+
+_sb(BF, [4 * C], "xs ee xn")
+_sb(BF, [512], "us vs zt vt")
+_sb(BF, [2048], "idt")
+_sb(BF, [256], "m0 m1 ne0 ne1 sc0 sc1 sj0 sj1")
+_sb(BF, [192], "c11 fb fr")
+_sb(BF, [FW], "fw0 fw1 fw2 fw3")
+_sb(MX, [128], "uq uq2 vq vtq via0 via1")
+_sb(U8, [128], "uz uz2 vz vtz")
+_sb(MX, [512], "wq idq")
+_sb(U8, [512], "wz idz")
+_sb(MX, [C], "eq8 tq0 tq1 tq2 hq0 hq1")
+_sb(U8, [C], "ez tz0 tz1 tz2 hz0 hz1")
+_sb(I32, [1], "pi")
+_sb(I32, [4], "ints")
+_sb(U16, [8], "ul kl vo")
+_sb(U16, [26], "cl eo")
+_sb(F32, [4], "fc vf cnt sg")
+_sb(F32, [12], "m7 cmb pm land0 land1")
+_sb(F32, [16], "cc")
+_sb(F32, [26], "st w4")
+_sb(F32, [32], "th0 th1 c12 acc pt olb")
+_sb(F32, [36], "pw0 pw1")
+_sb(F32, [64], "dm ec cbb dr sig pc pdd kr the br")
+_sb(F32, [68], "npp")
+_sb(F32, [80], "ge eq")
+_sb(F32, [96], "jt pb prow")
+_sb(F32, [200], "sx")
+_sb(F32, [256], "row ct")
+_sb(F32, [288], "cg")
+_sb(F32, [C], "ys")
+_sb(F32, [4 * C], "rl")
+_sb(F32, [12, 7], "cb rr ll bi")
+_sb(F32, [12, 32], "et")
+_sb(F32, [12, 16], "ea mn")
+_sb(F32, [15, 16], "mm")
+_sb(F32, [14, 16], "tt")
+_sb(F32, [8, 12], "junk")
+_sb(F32, [4, 20], "pd")
+_sb(F32, [3, 72], "cmp")
+_sb(F32, [2, 80], "xy")
+_sb(F32, [2, 32], "bs")
+_sb(F32, [2, 48], "w2")
+_sb(F32, [2, 24], "w3")
+for _b in range(8):
+    SCRATCH["ps%d" % _b] = ("psum", [128, 512], F32)
+
+ROT = {"V": 48, "A": 32, "P": 16, "G": 8}
+NDMA = 20
+SEMAPHORES = (["%s%d" % (q.lower(), i) for q in "VAPG" for i in range(ROT[q])] + ["d%d" % i for i in range(NDMA)]
+              + ["sent"] + ["%s%d" % (n, t) for n in ("halo", "cost", "place") for t in range(R)])
+
+
+def from_left(b):
+    if 2 * b <= N:
+        return -(-S * b // (L + 1))
+    return -(-S * (N - b) // (L - 1))
+
+
+def sent_strips(r):
+    return max(([from_left(r + 1)] if r + 1 < N else []) + ([from_left(N - r)] if r > 0 else []))
+
+
+def halo_at(o):
+    a = L * sent_strips(o - 1) if o > 0 else 0
+    b = L * sent_strips(o + 1) if o + 1 < N else 0
+    return PADC - a - b, PADC - b
+
+
+def neighbours(a):
+    return [o for o in (a - 1, a + 1) if 0 <= o < N]
+
+
+def as_mask(engines):
+    m = 0
+    for e in engines:
+        m |= 1 << e
+    return m
+
+
+def helper(T, topo, a, o):
+    c = T.cores[a]
+    free = [h for h in topo.cores_of(c) if T.rank_of(h) is None and topo.die(h) == topo.die(c)
+            and all(topo.may_write(h, T.cores[x]) for x in neighbours(a))]
+    return free[0 if o < a else 1]
+
+
+def chip_engines(T, topo, a):
+    nb = neighbours(a)
+    far = [e for x in range(N) if x != a for e in topo.engines(T.cores[a], T.cores[x])]
+    es = [e for e in topo.engines(T.cores[a], helper(T, topo, a, nb[0])) if e not in far]
+    n = len(es) // len(nb)
+    return {x: es[n * k:n * k + n] for k, x in enumerate(nb)}
+
+
+def hand_on(g, core, T, topo):
+    for a in range(N):
+        for o in neighbours(a):
+            if helper(T, topo, a, o) == core:
+                w = L * sent_strips(a)
+                at = halo_at(o)[1 if o < a else 0]
+                rid, pid = topo.addr(T.cores[o], core)
+                for t in range(R):
+                    g.wait_ge(T.sem["halo%d" % t], len(chip_engines(T, topo, a)[o]))
+                    g.remote_dma_fused([RemoteDMATransfer(
+                        dst_ids=[DstId(rid=rid, pnc=pid)], dma_engine_mask=topo.mask(core, T.cores[o]),
+                        remote_sem=T.sem["halo%d" % t], src=T["via%d" % t][:, 0:w].bitcast(dt.uint8),
+                        dst=T["hq%d" % t][:, at:at + w].bitcast(dt.uint8))], local_sem=T.sem.sent)
+                g.wait_ge(T.sem.sent, R * len(topo.engines(core, T.cores[o])))
+
+
+def rank_program(g, core, T, topo):
+    r = T.rank_of(core)
+    if r is None:
+        return hand_on(g, core, T, topo)
+    Op, Act = AluOpType, ActivationFunctionType
+    ops = []
+    s_ = np.s_
+
+    def A(name, idx=None, mod=None):
+        return (name, s_[:] if idx is None else idx, mod)
+
+    def col(name, c, n=1):
+        return A(name, s_[:, c:c + n])
+
+    def ind(ap, off):
+        return (ap[0], ap[1], ("ind", off, ap[2]))
+
+    def real(ap):
+        if not isinstance(ap, tuple):
+            return ap
+        v = T[ap[0]][ap[1]]
+        mod = ap[2]
+        if mod == "u8":
+            return v.bitcast(dt.uint8)
+        if mod == "u32":
+            return v.bitcast(dt.uint32)
+        if mod is not None:
+            if mod[2] == "u32":
+                v = v.bitcast(dt.uint32)
+            return v.indirect(real(mod[1]))
+        return v
+
+    cache = {}
+
+    def foot(ap):
+        name, idx = ap[0], ap[1]
+        if name not in SCRATCH:
+            return []
+        key = (name, str(idx))
+        if key not in cache:
+            where, shape, _d = SCRATCH[name]
+            ix = idx if isinstance(idx, tuple) else (idx,)
+            parts = range(128)[ix[0]]
+            if where == "psum":
+                cache[key] = (name, 0, 128, 1)
+            else:
+                free = np.arange(int(np.prod(shape[1:]))).reshape(shape[1:])[ix[1:]].reshape(-1)
+                bits = 0
+                for e in free.tolist():
+                    bits |= 1 << e
+                cache[key] = (name, parts[0], parts[-1] + 1, bits)
+        out = [cache[key]]
+        if ap[2] is not None and ap[2][0] == "ind":
+            out += foot(ap[2][1])
+        return out
+
+    def rec(q, call, reads, writes, kind="c", sem=None, count=0):
+        rd = [f for a in reads if isinstance(a, tuple) for f in foot(a)]
+        wr = [f for a in writes for f in foot(a)]
+        ops.append({"q": q, "call": call, "rd": rd, "wr": wr, "kind": kind, "sem": sem, "count": count})
+
+    def meet(fa, fb):
+        return any(a[0] == b[0] and a[1] < b[2] and b[1] < a[2] and a[3] & b[3] for a in fa for b in fb)
+
+    def emit():
+        eng = {"V": g.vector, "A": g.scalar, "P": g.tensor, "G": g, "S": g.sync}
+        known = {q: set() for q in eng}
+        for i, o in enumerate(ops):
+            o["waits"], o["used"] = [], False
+            if o["kind"] == "arrival":
+                o["known"] = set()
+                continue
+            need = []
+            banks = [f for f in o["rd"] if SCRATCH[f[0]][0] == "psum"]
+            for j in range(i - 1, -1, -1):
+                p = ops[j]
+                if j in known[o["q"]] or p["kind"] == "remote":
+                    continue
+                if (meet(o["rd"], p["wr"]) or meet(o["wr"], p["wr"]) or meet(o["wr"], p["rd"])
+                        or (p["q"] != o["q"] and meet(banks, p["rd"]))):
+                    need.append(j)
+                    known[o["q"]].add(j)
+                    known[o["q"]] |= p["known"]
+            o["waits"] = need[::-1]
+            for j in need:
+                ops[j]["used"] = True
+            o["known"] = set(known[o["q"]])
+        turn = {q: 0 for q in ROT}
+        nd = 0
+        for o in ops:
+            if o["kind"] == "dma":
+                o["sem"], o["count"] = "d%d" % nd, 16
+                nd += 1
+            elif o["kind"] == "c" and o["used"]:
+                n = turn[o["q"]]
+                turn[o["q"]] += 1
+                o["sem"], o["count"] = "%s%d" % (o["q"].lower(), n % ROT[o["q"]]), n // ROT[o["q"]] + 1
+        sent = 0
+        for o in ops:
+            if o["kind"] == "arrival":
+                continue
+            e = eng[o["q"]]
+            for j in o["waits"]:
+                e.wait_ge(T.sem[ops[j]["sem"]], ops[j]["count"])
+            ins = o["call"](e)
+            if o["kind"] == "dma":
+                ins.then_inc(T.sem[o["sem"]], 16)
+            elif o["kind"] == "remote":
+                sent += o["count"]
+            elif o["used"]:
+                ins.then_inc(T.sem[o["sem"]], 1)
+        for o in ops:
+            if o["kind"] == "dma" and not o["used"]:
+                eng[o["q"]].wait_ge(T.sem[o["sem"]], 16)
+        g.wait_ge(T.sem.sent, sent)
+
+    def dma(q, out, in_):
+        rec(q, lambda e: e.dma_start(real(out), real(in_)), [in_], [out], "dma")
+
+    def memset(ap, c):
+        rec("V", lambda e: e.memset(real(ap), c), [], [ap])
+
+    def copy(out, in_):
+        rec("V", lambda e: e.tensor_copy(real(out), real(in_)), [in_], [out])
+
+    def tt(out, a, b, op):
+        rec("V", lambda e: e.tensor_tensor(real(out), real(a), real(b), op), [a, b], [out])
+
+    def ts(out, a, s1, op0, s2=None, op1=None):
+        if op1 is None:
+            rec("V", lambda e: e.tensor_scalar(real(out), real(a), real(s1), None, op0), [a, s1], [out])
+        else:
+            rec("V", lambda e: e.tensor_scalar(real(out), real(a), real(s1), real(s2), op0, op1), [a, s1, s2], [out])
+
+    def red(out, a, op):
+        rec("V", lambda e: e.tensor_reduce(real(out), real(a), AxisListType.X, op), [a], [out])
+
+    def scan(out, d0, d1, init, op0, op1):
+        rec("V", lambda e: e.tensor_tensor_scan(real(out), real(d0), real(d1), real(init), op0, op1), [d0, d1, init], [out])
+
+    def transp(out, a):
+        rec("V", lambda e: e.transpose(real(out), real(a)), [a], [out])
+
+    def quant(q, z, a):
+        rec("V", lambda e: e.quantize_mx(real(q), real(z), real(a)), [a], [q, z])
+
+    def quant_run(q, z, tile, a, b):
+        quant(A(q, s_[:, a:b]), A(z, s_[:, a:b]), A(tile, s_[:, 4 * a:4 * b]))
+
+    def act(out, a, func, bias=None, scale=None, accum=None):
+        def call(e):
+            kw = {}
+            if bias is not None:
+                kw["bias"] = real(bias)
+            if scale is not None:
+                kw["scale"] = scale
+            if accum is not None:
+                kw["accum_out"] = real(accum)
+            return e.activation(real(out), real(a), func, **kw)
+        rec("A", call, [a, bias], [out] + ([accum] if accum is not None else []))
+
+    def acopy(out, a):
+        act(out, a, Act.Copy)
+
+    def lin(out, a, scale, bias):
+        act(out, a, Act.Identity, bias, scale)
+
+    def const(name, a, b, c, p0=0, p1=128):
+        for k in range(a, b, 256):
+            n = min(256, b - k)
+            lin(A(name, s_[p0:p1, k:k + n]), A("row", s_[p0:p1, 0:n]), 0.0, c)
+
+    def mm(bank, lq, lz, lo, rq, rz, a, b):
+        out = A("ps%d" % bank, s_[:, 0:b - a])
+        l, ls = A(lq, s_[:, lo:lo + 128]), A(lz, s_[:, lo:lo + 128])
+        m, ms = A(rq, s_[:, a:b]), A(rz, s_[:, a:b])
+        rec("P", lambda e: e.matmul_mx(real(out), real(l), real(ls), real(m), real(ms), True, True), [l, ls, m, ms], [out])
+
+    def iota(out, pattern, base, cm, small=True):
+        if small:
+            rec("G", lambda e: e.iota(real(out), pattern, base, cm, allow_small_or_imprecise_dtypes=True), [], [out])
+        else:
+            rec("G", lambda e: e.iota(real(out), pattern, base, cm), [], [out])
+
+    def dst(to):
+        rid, pid = topo.addr(to, core)
+        return DstId(rid=rid, pnc=pid)
+
+    def shared_engines(a, others):
+        return [e for e in topo.engines(T.cores[a], T.cores[others[0]])
+                if all(e in topo.engines(T.cores[a], T.cores[o]) for o in others)]
+
+    def share(a):
+        return len(shared_engines(a, neighbours(a))) // len(neighbours(a))
+
+    def send(sem, transfers):
+        rec("G", lambda e: e.remote_dma_fused(
+            [RemoteDMATransfer(dst_ids=[dst(c) for c, d in to], dma_engine_mask=as_mask(es), remote_sem=T.sem[sem],
+                               src=real(src), dsts=[real(d) for c, d in to]) for es, src, to in transfers],
+            local_sem=T.sem.sent), [src for es, src, to in transfers], [], "remote", None,
+            sum(len(es) for es, src, to in transfers))
+
+    def send_pair(sem, pieces):
+        es, n = shared_engines(r, neighbours(r)), share(r)
+        send(sem, [(es[n * k:n * k + n], pieces[o][0], [(T.cores[o], pieces[o][1])]) for k, o in enumerate(neighbours(r))])
+
+    def arrival(sem, count, writes):
+        rec("R", None, [], writes, "arrival", sem, count)
+
+    others = [o for o in range(N) if o != r]
+    wl = L * sent_strips(r - 1) if r > 0 else 0
+    wr = L * sent_strips(r + 1) if r + 1 < N else 0
+    ws_ = L * sent_strips(r)
+
+    def places_at(o):
+        return (32 if o > 0 else 15), (15 if o + 1 == N else 34 if o > 0 else 32)
+    h0 = halo_at(r)[0]
+    hend = max(PADC, h0 + 128)
+    pend = 32 + 2 * len(neighbours(r))
+    low = 2 * r < N
+    lo, hi = (min(0, r - 1), r + 1) if low else (r - 1, max(N - 1, r + 1))
+    first = 0 if low else 4
+    extra = [b for b in range(max(lo, 0), min(hi, N - 1) + 1) if not first <= b < first + 4]
+    nh = 1 + len(extra)
+    nblk = hi - lo + 1
+    win = S * (r - lo) - 16
+    cst = float(-C * r + (L - 1) * S * lo) if low else float(C * (N - r))
+
+    def slot(o, at):
+        return 0 if o == at else 4 + o - (1 if o > at else 0)
+
+    dma("A", A("us"), A("u"))
+    for a, b in PIECES:
+        dma("S", A("xs", s_[:, 4 * a:4 * b]), A("x", s_[:, 4 * a:4 * b]))
+    dma("S", A("wq", None, "u8"), A("wc"))
+    dma("S", A("wz"), A("ws"))
+    dma("S", A("vs"), A("v"))
+
+    iota(A("pi"), [[0, 1]], 0, 1, False)
+    iota(A("row"), [[1, 256]], 0, 0)
+    iota(A("cb"), [[1, 12], [0, 7]], -6, 0)
+    iota(A("dm"), [[0, 4], [1, 16]], 0, 0)
+    iota(A("jt"), [[0, 4], [32, 24]], 0, 0)
+    JJ, KK, AA, PP = range(4)
+    memset(A("idt"), 0.0)
+    ts(col("ints", JJ), A("pi"), 15, Op.bitwise_and)
+    ts(col("ints", KK), A("pi"), 31, Op.bitwise_and)
+    ts(col("ints", AA), A("pi"), 5, Op.arith_shift_right)
+    copy(col("ints", PP), A("pi"))
+    memset(A("mm"), BIG)
+    copy(A("fc"), A("ints"))
+    jj = col("fc", JJ)
+    ts(col("cc", 0), jj, -1.0, Op.mult, 15.0, Op.add)
+    quant(A("uq"), A("uz"), A("us"))
+    ts(col("cc", 1), col("cc", 0), jj, Op.min, 16.0, Op.mult)
+    for b in range(2):
+        ts(A("idt", s_[:, 512 * b + b:512 * b + 512:4]), col("row", 0, 128), col("fc", PP), Op.is_equal)
+    ts(A("ul"), col("row", 0, 8), 0.0, Op.mult, col("cc", 1), Op.add)
+    for b in range(2, 4):
+        ts(A("idt", s_[:, 512 * b + b:512 * b + 512:4]), col("row", 0, 128), col("fc", PP), Op.is_equal)
+    copy(A("uq2", None, "u32"), ind(A("uq", None, "u32"), A("ul")))
+    copy(A("uz2"), ind(A("uz"), A("ul")))
+
+    for t in range(R):
+        const("land%d" % t, 0, 4, 0.0)
+    lin(A("cb"), A("cb"), 1.0, 0.5)
+    const("acc", 0, 32, 0.0)
+    lin(A("cb", s_[:, :, 6]), A("cb", s_[:, :, 6]), 1.0, 6.0)
+    for b in range(4):
+        const("fw%d" % b, 0, OWN - wl, 0.0)
+        const("fw%d" % b, OWN + C + wr, HB, 0.0)
+    if hend > PADC:
+        const("zt", 0, 512, 0.0)
+    const("vt", 256, 512, 0.0)
+    for a in range(4):
+        const("st", 0, 2, float(slot(first + a, r)), 32 * a, 32 * a + 32)
+    for o in range(N):
+        const("st", 2 + 2 * o, 4 + 2 * o, float(slot(o, r)))
+    for k, c in enumerate((places_at(r)[0], 15, places_at(r)[1])):
+        lin(col("st", 18 + 2 * k, 2), col("row", 0, 2), 1.0, float(c))
+    lin(col("cc", 2), col("fc", AA), 2.0, 0.0)
+    lin(col("cc", 3), col("fc", PP), 1.0, float(S * first))
+    if extra:
+        lin(col("cc", 4), col("fc", KK), 1.0, float(S * extra[0]))
+    lin(col("cc", 12), jj, float(L), 6.0)
+    lin(col("cc", 13), jj, 2.0, 0.0)
+    lin(col("cc", 8), jj, 32.0, 1.0 - 2 * cst)
+    lin(col("cc", 10), jj, 32.0, 257.0 - 2 * cst)
+    lin(col("st", 24, 2), col("row", 0, 2), 1.0, col("cc", 2))
+    for h in range(nh):
+        lin(col("cc", 5 + h), col("cc", 3 + h), 2.0, -float(N * S))
+    lin(A("pd", s_[:, :, 16]), A("row", s_[:, 0:64:16]), float(L), col("cc", 12))
+    lin(A("jt"), A("jt"), 1.0, col("cc", 13))
+    const("c11", 0, 192, float(L - 1))
+    const("fb", 0, 192, 0.0)
+    for h in range(nh):
+        const("th%d" % h, 0, 32, col("cc", 5 + h))
+        act(A("sj%d" % h), A("row"), Act.Abs, col("cc", 3 + h), -1.0)
+    lin(A("ec"), col("row", 0, 64), 2.0, 2.0 * HB)
+    lin(A("bs", s_[:, 1, :]), col("row", 0, 32), 0.0, 0.0)
+    lin(A("c12"), col("row", 0, 32), float(L), 6.0)
+    lin(A("cbb"), col("row", 0, 64), 2.0 * L, -2 * cst)
+    for h in range(nh):
+        act(A("m%d" % h), A("sj%d" % h), Act.Sign, -0.5, 1.0)
+    lin(A("npp", s_[:, 65:68:2]), col("row", 0, 2), 0.0, 1.0e6)
+    lin(col("npp", 64), jj, 2.0e6, -15.0e6)
+    lin(col("npp", 66), jj, -2.0e6, 15.0e6)
+
+    def late_constants():
+        yield lambda: copy(A("cl"), A("st"))
+        yield lambda: ts(A("dm"), A("dm"), jj, Op.is_equal, -0.5, Op.mult)
+        yield lambda: ts(col("cc", 11), jj, 8.0, Op.is_ge, -768.0, Op.mult)
+        yield lambda: ts(col("cc", 9), col("cc", 8), col("cc", 11), Op.add, 512.0, Op.add)
+        if hend > PADC:
+            for t in range(R):
+                yield lambda t=t: quant(col("hq%d" % t, PADC, 128), col("hz%d" % t, PADC, 128), A("zt"))
+        yield lambda: quant(A("vq"), A("vz"), A("vs"))
+    late = list(late_constants())
+
+    def fill(n):
+        for _i in range(n):
+            if late:
+                late.pop(0)()
+
+    for a, b in PIECES:
+        quant_run("tq0", "tz0", "xs", a, b)
+    for t in range(R):
+        tq, tz, hq, hz, land, pw = ("%s%d" % (n, t) for n in ("tq", "tz", "hq", "hz", "land", "pw"))
+        mm(0, "uq2", "uz2", 0, tq, tz, 0, C)
+        if t == 0:
+            quant(A("idq"), A("idz"), A("idt"))
+        for b in range(4):
+            mm(4 + b, "idq", "idz", 128 * b, tq, tz, 0, C)
+        edge = {r - 1: s_[:, 0:ws_], r + 1: s_[:, C - ws_:C]}
+        send("halo%d" % t, [(chip_engines(T, topo, r)[o], A(tq, edge[o], "u8"),
+                             [(helper(T, topo, r, o), A("via%d" % t, s_[:, 0:ws_], "u8"))]) for o in neighbours(r)])
+        at = {o: halo_at(o)[1 if o < r else 0] for o in neighbours(r)}
+        send_pair("halo%d" % t, {o: (A(tz, edge[o]), col(hz, at[o], ws_)) for o in neighbours(r)})
+        for i in range(L):
+            transp(A("et", s_[:, i, :]), A("ps0", s_[:, i:C:L]))
+        act(A("mm", s_[:, 1:13, 0:9:8]), A("et", s_[:, :, 0:9:8]), Act.Abs)
+        act(A("ea", s_[:, :, 1:12]), A("et", s_[:, :, 1:12]), Act.Abs)
+        for b in range(4):
+            acopy(col("fw%d" % b, OWN, C), col("ps%d" % (4 + b), 0, C))
+
+        def step(name, a, b, s, both):
+            return A(name, s_[:, a:b, s:s + 9:8] if both else s_[:, a:b, s])
+
+        def back(k, c):
+            if k == 0:
+                tt(A("rr", s_[:, :, c]), A("mm", s_[:, 2:14, c]), A("tt", s_[:, 0:12, c]), Op.is_lt)
+            elif k == 1:
+                tt(A("ll", s_[:, :, c]), A("mm", s_[:, 1:13, c]), A("tt", s_[:, 2:14, c]), Op.is_le)
+            elif k == 2:
+                tt(A("rr", s_[:, :, c]), A("cb", s_[:, :, c]), A("rr", s_[:, :, c]), Op.subtract)
+            else:
+                tt(A("bi", s_[:, :, c]), A("ll", s_[:, :, c]), A("rr", s_[:, :, c]), Op.add)
+        for s in range(1, 8):
+            tt(step("tt", 0, 14, s - 1, s <= 4), step("mm", 0, 14, s - 1, s <= 4), step("mm", 1, 15, s - 1, s <= 4), Op.min)
+            if s == 5:
+                fill(1)
+            if s == 7:
+                back(1, s_[0:6])
+            tt(step("mn", 0, 12, s - 1, s <= 4), step("tt", 0, 12, s - 1, s <= 4), step("mm", 2, 14, s - 1, s <= 4), Op.min)
+            if s == 4:
+                tt(A("cmb"), A("mm", s_[:, 1:13, 3]), A("mn", s_[:, :, 11]), Op.max)
+            if s == 5:
+                fill(1)
+            if s == 6:
+                back(0, s_[0:6])
+            if s == 7:
+                back(0, 6)
+                back(1, 6)
+            tt(A("m7") if s == 7 else step("mm", 1, 13, s, s <= 3), step("ea", 0, 12, s, s <= 3),
+               step("mn", 0, 12, s - 1, s <= 3), Op.max)
+            if s == 4:
+                red(col(land, 0), A("cmb"), Op.min)
+                send("cost%d" % t, [(shared_engines(r, others), col(land, 0),
+                                     [(T.cores[o], col(land, slot(r, o))) for o in others])])
+            if s == 5:
+                fill(1)
+            if s == 6:
+                back(2, s_[0:6])
+        back(2, 6)
+        scan(A("pm"), A("m7"), A("m7"), BIG, Op.min, Op.min)
+        back(3, 6)
+        back(3, s_[0:6])
+        act(A("junk", s_[:, 7, :]), A("pm"), Act.Sign, col(land, 0), -1.0, col("acc", 8))
+        for gg in range(7, 0, -1):
+            act(A("junk", s_[:, gg - 1, :]), A("bi", s_[:, :, gg - 1]), Act.Sign, col("acc", 8 if gg == 7 else gg),
+                1.0 if gg == 7 else 2.0, col("acc", gg - 1))
+        fill(len(late))
+        ts(col("acc", 7), col("acc", 8), 2.0, Op.mult, float(L), Op.add)
+        copy(col(pw, 0, 32), ind(col("acc", 0, 8), col("cl", 24, 2)))
+        at = {o: places_at(o)[1 if o < r else 0] for o in neighbours(r)}
+        send_pair("place%d" % t, {o: (col(pw, 15, 2), col(pw, at[o], 2)) for o in neighbours(r)})
+        arrival("halo%d" % t, sum(share(o) + len(topo.engines(helper(T, topo, o, r), core)) for o in neighbours(r)),
+                [A(hq, s_[:, h0:PADC]), A(hz, s_[:, h0:PADC])])
+        for b in range(4):
+            mm(b, "idq", "idz", 128 * b, hq, hz, h0, hend)
+        for b in range(4):
+            move = copy if b < 2 else acopy
+            if wl:
+                move(col("fw%d" % b, OWN - wl, wl), col("ps%d" % b, 0, wl))
+            if wr:
+                move(col("fw%d" % b, OWN + C, wr), col("ps%d" % b, wl, wr))
+        if t == R - 1:
+            transp(A("pt", s_[0:32, :]), A("acc", s_[0:32, :]))
+            ts(A("pt", s_[0:32, :]), A("pt", s_[0:32, :]), -0.5, Op.mult)
+            tt(A("olb", s_[0:32, :]), A("pt", s_[0:32, :]), A("c12", s_[0:32, :]), Op.add)
+            dma("S", A("ol"), A("olb", s_[0:8, :]))
+        arrival("cost%d" % t, sum(len(shared_engines(o, [x for x in range(N) if x != o])) for o in others),
+                [col(land, 4, 7)])
+        copy(col("cg", 0, 160), ind(col(land, 0, 11), col("cl", 0, 10)))
+        acopy(col("cg", 160, 128), ind(col(land, 0, 11), col("cl", 10, 8)))
+        transp(A("ct"), col("cg", 32, 256))
+        sel = [col("cg", 0)] + [col("cg", 32 + S * b) for b in extra]
+        for h in range(nh):
+            ts(A("ne%d" % h), A("ct"), sel[h], Op.not_equal, -1.0, Op.mult)
+            act(A("sj%d" % h), A("ct"), Act.Sign, sel[h], -1.0, col("sg", h))
+        for h in range(nh):
+            scan(A("sc%d" % h), A("m%d" % h), A("ne%d" % h), col("sg", h), Op.mult, Op.add)
+        for b in sorted(range(max(lo, 0), min(hi, N - 1) + 1), key=lambda b: b in extra):
+            h, a = (1, 0) if b in extra else (0, b - first)
+            ts(A("fb", s_[0:32, S * (b - lo):S * (b - lo) + S]), A("th%d" % h, s_[32 * a:32 * a + 32, :]),
+               A("sc%d" % h, s_[32 * a:32 * a + 32, 255:256]), Op.is_ge, 2.0, Op.mult)
+        transp(A("fr", s_[0:32, 0:S * nblk]), A("fb", s_[0:32, 0:S * nblk]))
+        scan(A("sx", s_[0:32, 1:1 + S * nblk]), A("fr", s_[0:32, 0:S * nblk]), A("c11", s_[0:32, 0:S * nblk]), 0.0,
+             Op.add, Op.add)
+        prow, npp = col("prow", 16, 64), col("npp", 0, 64)
+        for a in range(4):
+            lin(A("dr", s_[32 * a:32 * a + 32, :]), A("fr", s_[0:32, win:win + 64]), 0.5, 0.0)
+        lin(A("pdd"), A("dr"), 2.0, 2 * cst + L)
+        for a in range(4):
+            o, i = A("npp", s_[32 * a:32 * a + 32, 0:64]), A("sx", s_[0:32, win:win + 64])
+            if low:
+                ts(o, i, -2.0, Op.mult)
+            else:
+                k = S * (N - lo)
+                ts(o, i, A("sx", s_[0:32, k:k + 1]), Op.subtract, -2.0, Op.mult)
+        for x, n in enumerate((64, 66, 68)):
+            act(A("cmp", s_[:, x, 0:n]), col("npp", 0, n), Act.Sign, col("cc", 8 + x), 1.0, col("cnt", x))
+        lin(A("sig"), A("dr"), -4.0, 2.0)
+        tt(A("kr"), A("ec"), A("dr"), Op.mult)
+        tt(A("pc"), A("pdd"), npp, Op.subtract)
+        tt(A("br"), npp, A("cbb"), Op.add)
+        arrival("place%d" % t, sum(share(o) for o in neighbours(r)), [A(pw, s_[:, 32:pend])])
+        copy(A("pb"), ind(col(pw, 0, pend), col("cl", 18, 6)))
+        ts(col("kl", 0, 3), col("cnt", 0, 3), 0.5, Op.mult, 31.0, Op.add)
+        ts(col("kl", 3, 2), col("cnt", 0, 2), 0.5, Op.mult, 33.0, Op.add)
+        transp(A("prow"), A("pb"))
+        tt(A("bs", s_[:, 0, :]), ind(A("br"), col("kl", 0, 2)), col("jt", 0, 32), Op.add)
+        tt(A("pd", s_[:, :, 0:16]), prow, A("dm"), Op.mult)
+        tt(A("the"), A("pc"), prow, Op.subtract)
+        for x in range(4):
+            if x < 2:
+                red(col("vf", x), A("pd", s_[:, x, 0:17]), Op.add)
+            else:
+                act(A("cmp", s_[:, x - 2, 0:17]), A("pd", s_[:, x, 0:17]), Act.Identity, None, None, col("vf", x))
+        kl, j80 = col("kl", 0, 5), col("jt", 0, 80)
+        copy(col("vo", 0, 4), A("vf"))
+        for b in range(4):
+            acopy(A("vt", s_[:, b:256:4]), ind(col("fw%d" % b, 0, HB), col("vo", 0, 4)))
+        tt(A("ge"), ind(A("the"), kl), j80, Op.is_le)
+        tt(A("eq"), ind(A("the"), kl), j80, Op.is_equal)
+        tt(A("xy", s_[:, 0, :]), ind(A("sig"), kl), A("ge"), Op.mult)
+        tt(A("xy", s_[:, 1, :]), ind(A("kr"), kl), A("eq"), Op.mult)
+        quant(A("vtq"), A("vtz"), A("vt"))
+        for b in range(4):
+            mm(4 + b, "wq", "wz", 128 * b, "vtq", "vtz", 0, 128)
+        for b in range(4):
+            act(col("fw%d" % b, HB, 64), col("ps%d" % (4 + b), 0, 64), Act.Relu, None, 0.03125)
+        tt(A("w2", s_[:, :, 0:24]), A("xy", s_[:, :, 0:24]), A("xy", s_[:, :, 24:48]), Op.add)
+        tt(A("w2", s_[:, :, 24:48]), A("xy", s_[:, :, 48:72]), A("bs", s_[:, :, 0:24]), Op.add)
+        tt(A("w3"), A("w2", s_[:, :, 0:24]), A("w2", s_[:, :, 24:48]), Op.add)
+        tt(col("w4", 0, 24), A("w3", s_[:, 0, :]), A("w3", s_[:, 1, :]), Op.max)
+        ts(col("eo", 0, 24), col("w4", 0, 24), 0.5, Op.mult)
+        for k, (a, b) in enumerate(PIECES):
+            for e in range(4):
+                (acopy if e % 2 else copy)(A("ee", s_[:, 4 * a + e:4 * b:4]),
+                                           ind(A("fw%d" % e), A("eo", s_[:, a // 16:b // 16])))
+            quant_run("eq8", "ez", "ee", a, b)
+        nq, nz = "tq%d" % (t + 1), "tz%d" % (t + 1)
+        for k, (a, b) in enumerate(PIECES):
+            for e in range(4):
+                mm(e, "wq", "wz", 128 * e, "eq8", "ez", a, b)
+                mm(4 + e, "idq", "idz", 128 * e, "eq8", "ez", a, b)
+            for e in range(4):
+                rl = col("rl", C * e + a, b - a)
+                act(rl, col("ps%d" % e, 0, b - a), Act.Relu, None, 0.015625)
+                tt(A("xn", s_[:, 4 * a + e:4 * b:4]), col("ps%d" % (4 + e), 0, b - a), rl, Op.add)
+            quant_run(nq, nz, "xn", a, b)
+            if t == R - 1:
+                dma("S", A("oc", s_[:, 4 * a:4 * b]), A(nq, s_[:, a:b], "u8"))
+
+    tq, tz = "tq%d" % R, "tz%d" % R
+    for k, (a, b) in enumerate(PIECES):
+        mm(k, "vq", "vz", 0, tq, tz, a, b)
+        acopy(col("ys", a, b - a), col("ps%d" % k, 0, b - a))
+        dma("A", A("y", s_[:, a:b]), col("ys", a, b - a))
+    for k in range(4):
+        dma("S", A("osc", s_[4 * k:4 * k + 4, :]), A(tz, s_[32 * k:32 * k + 4, :]))
+    emit()

@@ -36,7 +36,7 @@ _sb(I32, [4], "ints")
 _sb(U16, [8], "ul kl vo")
 _sb(U16, [26], "cl eo")
 _sb(F32, [4], "fc vf cnt sg")
-_sb(F32, [12], "m7 cmb pm land0 land1")
+_sb(F32, [12], "pm land0 land1")
 _sb(F32, [16], "cc")
 _sb(F32, [26], "st w4")
 _sb(F32, [32], "th0 th1 c12 acc pt olb")
@@ -50,11 +50,11 @@ _sb(F32, [256], "row ct")
 _sb(F32, [288], "cg")
 _sb(F32, [C], "ys")
 _sb(F32, [4 * C], "rl")
-_sb(F32, [12, 7], "cb rr ll bi")
+_sb(F32, [7, 12], "cb rr ll bi")
 _sb(F32, [12, 32], "et")
-_sb(F32, [12, 16], "ea mn")
-_sb(F32, [15, 16], "mm")
-_sb(F32, [14, 16], "tt")
+_sb(F32, [8, 64], "mm")
+_sb(F32, [7, 64], "tt")
+_sb(F32, [27, 8], "ea")
 _sb(F32, [8, 12], "junk")
 _sb(F32, [4, 20], "pd")
 _sb(F32, [3, 72], "cmp")
@@ -369,7 +369,7 @@ def rank_program(g, core, T, topo):
 
     iota(A("pi"), [[0, 1]], 0, 1, False)
     iota(A("row"), [[1, 256]], 0, 0)
-    iota(A("cb"), [[1, 12], [0, 7]], -6, 0)
+    iota(A("cb"), [[0, 7], [1, 12]], -6, 0)
     iota(A("dm"), [[0, 4], [1, 16]], 0, 0)
     iota(A("jt"), [[0, 4], [32, 24]], 0, 0)
     JJ, KK, AA, PP = range(4)
@@ -378,8 +378,10 @@ def rank_program(g, core, T, topo):
     ts(col("ints", KK), A("pi"), 31, Op.bitwise_and)
     ts(col("ints", AA), A("pi"), 5, Op.arith_shift_right)
     copy(col("ints", PP), A("pi"))
-    memset(A("mm"), BIG)
+    memset(A("mm", s_[:, :, 1:64:2]), BIG)
     copy(A("fc"), A("ints"))
+    memset(A("mm", s_[:, 0, 0:64:2]), BIG)
+    memset(A("ea", s_[:, 12:15, :]), BIG)
     jj = col("fc", JJ)
     ts(col("cc", 0), jj, -1.0, Op.mult, 15.0, Op.add)
     quant(A("uq"), A("uz"), A("us"))
@@ -394,9 +396,10 @@ def rank_program(g, core, T, topo):
 
     for t in range(R):
         const("land%d" % t, 0, 4, 0.0)
+    lin(A("tt", s_[:, :, 0:64:2]), col("row", 0, 224), 0.0, 0.0)
     lin(A("cb"), A("cb"), 1.0, 0.5)
     const("acc", 0, 32, 0.0)
-    lin(A("cb", s_[:, :, 6]), A("cb", s_[:, :, 6]), 1.0, 6.0)
+    lin(A("cb", s_[:, 6, :]), A("cb", s_[:, 6, :]), 1.0, 6.0)
     for b in range(4):
         const("fw%d" % b, 0, OWN - wl, 0.0)
         const("fw%d" % b, OWN + C + wr, HB, 0.0)
@@ -424,34 +427,30 @@ def rank_program(g, core, T, topo):
     lin(A("jt"), A("jt"), 1.0, col("cc", 13))
     const("c11", 0, 192, float(L - 1))
     const("fb", 0, 192, 0.0)
-    for h in range(nh):
-        const("th%d" % h, 0, 32, col("cc", 5 + h))
-        act(A("sj%d" % h), A("row"), Act.Abs, col("cc", 3 + h), -1.0)
     lin(A("ec"), col("row", 0, 64), 2.0, 2.0 * HB)
     lin(A("bs", s_[:, 1, :]), col("row", 0, 32), 0.0, 0.0)
     lin(A("c12"), col("row", 0, 32), float(L), 6.0)
     lin(A("cbb"), col("row", 0, 64), 2.0 * L, -2 * cst)
-    for h in range(nh):
-        act(A("m%d" % h), A("sj%d" % h), Act.Sign, -0.5, 1.0)
     lin(A("npp", s_[:, 65:68:2]), col("row", 0, 2), 0.0, 1.0e6)
     lin(col("npp", 64), jj, 2.0e6, -15.0e6)
     lin(col("npp", 66), jj, -2.0e6, 15.0e6)
 
+    def rank_constants():
+        for h in range(nh):
+            const("th%d" % h, 0, 32, col("cc", 5 + h))
+            act(A("sj%d" % h), A("row"), Act.Abs, col("cc", 3 + h), -1.0)
+        for h in range(nh):
+            act(A("m%d" % h), A("sj%d" % h), Act.Sign, -0.5, 1.0)
+
     def late_constants():
-        yield lambda: copy(A("cl"), A("st"))
-        yield lambda: ts(A("dm"), A("dm"), jj, Op.is_equal, -0.5, Op.mult)
-        yield lambda: ts(col("cc", 11), jj, 8.0, Op.is_ge, -768.0, Op.mult)
-        yield lambda: ts(col("cc", 9), col("cc", 8), col("cc", 11), Op.add, 512.0, Op.add)
+        copy(A("cl"), A("st"))
+        ts(col("cc", 11), jj, 8.0, Op.is_ge, -768.0, Op.mult)
+        ts(A("dm"), A("dm"), jj, Op.is_equal, -0.5, Op.mult)
+        ts(col("cc", 9), col("cc", 8), col("cc", 11), Op.add, 512.0, Op.add)
         if hend > PADC:
             for t in range(R):
-                yield lambda t=t: quant(col("hq%d" % t, PADC, 128), col("hz%d" % t, PADC, 128), A("zt"))
-        yield lambda: quant(A("vq"), A("vz"), A("vs"))
-    late = list(late_constants())
-
-    def fill(n):
-        for _i in range(n):
-            if late:
-                late.pop(0)()
+                quant(col("hq%d" % t, PADC, 128), col("hz%d" % t, PADC, 128), A("zt"))
+        quant(A("vq"), A("vz"), A("vs"))
 
     for a, b in PIECES:
         quant_run("tq0", "tz0", "xs", a, b)
@@ -469,72 +468,62 @@ def rank_program(g, core, T, topo):
         send_pair("halo%d" % t, {o: (A(tz, edge[o]), col(hz, at[o], ws_)) for o in neighbours(r)})
         for i in range(L):
             transp(A("et", s_[:, i, :]), A("ps0", s_[:, i:C:L]))
-        act(A("mm", s_[:, 1:13, 0:9:8]), A("et", s_[:, :, 0:9:8]), Act.Abs)
-        act(A("ea", s_[:, :, 1:12]), A("et", s_[:, :, 1:12]), Act.Abs)
-        for b in range(4):
-            acopy(col("fw%d" % b, OWN, C), col("ps%d" % (4 + b), 0, C))
-
-        def step(name, a, b, s, both):
-            return A(name, s_[:, a:b, s:s + 9:8] if both else s_[:, a:b, s])
+        act(A("mm", s_[:, 0, 3:27:2]), A("et", s_[:, :, 0]), Act.Abs)
+        act(A("mm", s_[:, 0, 33:57:2]), A("et", s_[:, :, 8]), Act.Abs)
+        act(A("mm", s_[:, 0, 6:30:2]), A("et", s_[:, :, 1]), Act.Abs)
+        act(A("mm", s_[:, 0, 36:60:2]), A("et", s_[:, :, 9]), Act.Abs)
+        act(A("ea", s_[:, 0:12, 1:7]), A("et", s_[:, :, 2:8]), Act.Abs)
+        act(A("ea", s_[:, 15:27, 1:3]), A("et", s_[:, :, 10:12]), Act.Abs)
 
         def back(k, c):
             if k == 0:
-                tt(A("rr", s_[:, :, c]), A("mm", s_[:, 2:14, c]), A("tt", s_[:, 0:12, c]), Op.is_lt)
+                tt(A("rr", s_[:, c, :]), A("mm", s_[:, c, 5:29:2]), A("tt", s_[:, c, 1:25:2]), Op.is_lt)
             elif k == 1:
-                tt(A("ll", s_[:, :, c]), A("mm", s_[:, 1:13, c]), A("tt", s_[:, 2:14, c]), Op.is_le)
+                tt(A("ll", s_[:, c, :]), A("mm", s_[:, c, 3:27:2]), A("tt", s_[:, c, 5:29:2]), Op.is_le)
             elif k == 2:
-                tt(A("rr", s_[:, :, c]), A("cb", s_[:, :, c]), A("rr", s_[:, :, c]), Op.subtract)
+                tt(A("rr", s_[:, c, :]), A("cb", s_[:, c, :]), A("rr", s_[:, c, :]), Op.subtract)
             else:
-                tt(A("bi", s_[:, :, c]), A("ll", s_[:, :, c]), A("rr", s_[:, :, c]), Op.add)
-        for s in range(1, 8):
-            tt(step("tt", 0, 14, s - 1, s <= 4), step("mm", 0, 14, s - 1, s <= 4), step("mm", 1, 15, s - 1, s <= 4), Op.min)
-            if s == 5:
-                fill(1)
-            if s == 7:
-                back(1, s_[0:6])
-            tt(step("mn", 0, 12, s - 1, s <= 4), step("tt", 0, 12, s - 1, s <= 4), step("mm", 2, 14, s - 1, s <= 4), Op.min)
-            if s == 4:
-                tt(A("cmb"), A("mm", s_[:, 1:13, 3]), A("mn", s_[:, :, 11]), Op.max)
-            if s == 5:
-                fill(1)
-            if s == 6:
-                back(0, s_[0:6])
-            if s == 7:
-                back(0, 6)
-                back(1, 6)
-            tt(A("m7") if s == 7 else step("mm", 1, 13, s, s <= 3), step("ea", 0, 12, s, s <= 3),
-               step("mn", 0, 12, s - 1, s <= 3), Op.max)
-            if s == 4:
-                red(col(land, 0), A("cmb"), Op.min)
+                tt(A("bi", s_[:, c, :]), A("ll", s_[:, c, :]), A("rr", s_[:, c, :]), Op.add)
+        for s in range(7):
+            n = 27 if s < 4 else 12
+            tt(A("tt", s_[:, s, 1:2 * n + 4:2]), A("mm", s_[:, s, 1:2 * n + 4:2]), A("mm", s_[:, s, 3:2 * n + 6:2]), Op.min)
+            if s > 0:
+                k = 15 if s == 3 else n
+                (acopy if s < 4 else copy)(A("mm", s_[:, s, 6:2 * k + 6:2]), A("ea", s_[:, 0:k, s]))
+            if s == 3:
+                copy(A("mm", s_[:, 3, 36:60:2]), A("mm", s_[:, 3, 3:27:2]))
+                for b in range(4):
+                    acopy(col("fw%d" % b, OWN, C), col("ps%d" % (4 + b), 0, C))
+            scan(A("mm", s_[:, s + 1, 2:2 * n + 2]), A("tt", s_[:, s, 0:2 * n]), A("mm", s_[:, s, 5:2 * n + 5]), 0.0,
+                 Op.min, Op.max)
+            if s == 3:
+                red(col(land, 0), A("mm", s_[:, 4, 33:57:2]), Op.min)
                 send("cost%d" % t, [(shared_engines(r, others), col(land, 0),
                                      [(T.cores[o], col(land, slot(r, o))) for o in others])])
+            if s == 4:
+                back(0, s_[0:5])
             if s == 5:
-                fill(1)
+                back(1, s_[0:5])
             if s == 6:
-                back(2, s_[0:6])
-        back(2, 6)
-        scan(A("pm"), A("m7"), A("m7"), BIG, Op.min, Op.min)
-        back(3, 6)
-        back(3, s_[0:6])
+                back(0, s_[5:7])
+                back(1, s_[5:7])
+        m7 = A("mm", s_[:, 7, 3:27:2])
+        scan(A("pm"), m7, m7, BIG, Op.min, Op.min)
+        back(2, s_[5:7])
+        back(2, s_[0:5])
+        back(3, s_[5:7])
+        back(3, s_[0:5])
         act(A("junk", s_[:, 7, :]), A("pm"), Act.Sign, col(land, 0), -1.0, col("acc", 8))
         for gg in range(7, 0, -1):
-            act(A("junk", s_[:, gg - 1, :]), A("bi", s_[:, :, gg - 1]), Act.Sign, col("acc", 8 if gg == 7 else gg),
+            act(A("junk", s_[:, gg - 1, :]), A("bi", s_[:, gg - 1, :]), Act.Sign, col("acc", 8 if gg == 7 else gg),
                 1.0 if gg == 7 else 2.0, col("acc", gg - 1))
-        fill(len(late))
+        if t == 0:
+            rank_constants()
+            late_constants()
         ts(col("acc", 7), col("acc", 8), 2.0, Op.mult, float(L), Op.add)
         copy(col(pw, 0, 32), ind(col("acc", 0, 8), col("cl", 24, 2)))
         at = {o: places_at(o)[1 if o < r else 0] for o in neighbours(r)}
         send_pair("place%d" % t, {o: (col(pw, 15, 2), col(pw, at[o], 2)) for o in neighbours(r)})
-        arrival("halo%d" % t, sum(share(o) + len(topo.engines(helper(T, topo, o, r), core)) for o in neighbours(r)),
-                [A(hq, s_[:, h0:PADC]), A(hz, s_[:, h0:PADC])])
-        for b in range(4):
-            mm(b, "idq", "idz", 128 * b, hq, hz, h0, hend)
-        for b in range(4):
-            move = copy if b < 2 else acopy
-            if wl:
-                move(col("fw%d" % b, OWN - wl, wl), col("ps%d" % b, 0, wl))
-            if wr:
-                move(col("fw%d" % b, OWN + C, wr), col("ps%d" % b, wl, wr))
         if t == R - 1:
             transp(A("pt", s_[0:32, :]), A("acc", s_[0:32, :]))
             ts(A("pt", s_[0:32, :]), A("pt", s_[0:32, :]), -0.5, Op.mult)
@@ -549,6 +538,18 @@ def rank_program(g, core, T, topo):
         for h in range(nh):
             ts(A("ne%d" % h), A("ct"), sel[h], Op.not_equal, -1.0, Op.mult)
             act(A("sj%d" % h), A("ct"), Act.Sign, sel[h], -1.0, col("sg", h))
+        arrival("halo%d" % t, sum(share(o) + len(topo.engines(helper(T, topo, o, r), core)) for o in neighbours(r)),
+                [A(hq, s_[:, h0:PADC]), A(hz, s_[:, h0:PADC])])
+        for b in range(4):
+            mm(b, "idq", "idz", 128 * b, hq, hz, h0, hend)
+
+        def unpack(b):
+            if wl:
+                acopy(col("fw%d" % b, OWN - wl, wl), col("ps%d" % b, 0, wl))
+            if wr:
+                acopy(col("fw%d" % b, OWN + C, wr), col("ps%d" % b, wl, wr))
+        for b in range(3):
+            unpack(b)
         for h in range(nh):
             scan(A("sc%d" % h), A("m%d" % h), A("ne%d" % h), col("sg", h), Op.mult, Op.add)
         for b in sorted(range(max(lo, 0), min(hi, N - 1) + 1), key=lambda b: b in extra):
@@ -559,9 +560,12 @@ def rank_program(g, core, T, topo):
         scan(A("sx", s_[0:32, 1:1 + S * nblk]), A("fr", s_[0:32, 0:S * nblk]), A("c11", s_[0:32, 0:S * nblk]), 0.0,
              Op.add, Op.add)
         prow, npp = col("prow", 16, 64), col("npp", 0, 64)
+        arrival("place%d" % t, sum(share(o) for o in neighbours(r)), [A(pw, s_[:, 32:pend])])
+        copy(A("pb"), ind(col(pw, 0, pend), col("cl", 18, 6)))
         for a in range(4):
             lin(A("dr", s_[32 * a:32 * a + 32, :]), A("fr", s_[0:32, win:win + 64]), 0.5, 0.0)
         lin(A("pdd"), A("dr"), 2.0, 2 * cst + L)
+        unpack(3)
         for a in range(4):
             o, i = A("npp", s_[32 * a:32 * a + 32, 0:64]), A("sx", s_[0:32, win:win + 64])
             if low:
@@ -569,18 +573,10 @@ def rank_program(g, core, T, topo):
             else:
                 k = S * (N - lo)
                 ts(o, i, A("sx", s_[0:32, k:k + 1]), Op.subtract, -2.0, Op.mult)
+        transp(A("prow"), A("pb"))
         for x, n in enumerate((64, 66, 68)):
             act(A("cmp", s_[:, x, 0:n]), col("npp", 0, n), Act.Sign, col("cc", 8 + x), 1.0, col("cnt", x))
-        lin(A("sig"), A("dr"), -4.0, 2.0)
-        tt(A("kr"), A("ec"), A("dr"), Op.mult)
         tt(A("pc"), A("pdd"), npp, Op.subtract)
-        tt(A("br"), npp, A("cbb"), Op.add)
-        arrival("place%d" % t, sum(share(o) for o in neighbours(r)), [A(pw, s_[:, 32:pend])])
-        copy(A("pb"), ind(col(pw, 0, pend), col("cl", 18, 6)))
-        ts(col("kl", 0, 3), col("cnt", 0, 3), 0.5, Op.mult, 31.0, Op.add)
-        ts(col("kl", 3, 2), col("cnt", 0, 2), 0.5, Op.mult, 33.0, Op.add)
-        transp(A("prow"), A("pb"))
-        tt(A("bs", s_[:, 0, :]), ind(A("br"), col("kl", 0, 2)), col("jt", 0, 32), Op.add)
         tt(A("pd", s_[:, :, 0:16]), prow, A("dm"), Op.mult)
         tt(A("the"), A("pc"), prow, Op.subtract)
         for x in range(4):
@@ -588,14 +584,20 @@ def rank_program(g, core, T, topo):
                 red(col("vf", x), A("pd", s_[:, x, 0:17]), Op.add)
             else:
                 act(A("cmp", s_[:, x - 2, 0:17]), A("pd", s_[:, x, 0:17]), Act.Identity, None, None, col("vf", x))
+        lin(A("sig"), A("dr"), -4.0, 2.0)
+        ts(col("kl", 0, 3), col("cnt", 0, 3), 0.5, Op.mult, 31.0, Op.add)
+        ts(col("kl", 3, 2), col("cnt", 0, 2), 0.5, Op.mult, 33.0, Op.add)
         kl, j80 = col("kl", 0, 5), col("jt", 0, 80)
         copy(col("vo", 0, 4), A("vf"))
         for b in range(4):
             acopy(A("vt", s_[:, b:256:4]), ind(col("fw%d" % b, 0, HB), col("vo", 0, 4)))
+        tt(A("kr"), A("ec"), A("dr"), Op.mult)
         tt(A("ge"), ind(A("the"), kl), j80, Op.is_le)
         tt(A("eq"), ind(A("the"), kl), j80, Op.is_equal)
+        tt(A("br"), npp, A("cbb"), Op.add)
         tt(A("xy", s_[:, 0, :]), ind(A("sig"), kl), A("ge"), Op.mult)
         tt(A("xy", s_[:, 1, :]), ind(A("kr"), kl), A("eq"), Op.mult)
+        tt(A("bs", s_[:, 0, :]), ind(A("br"), col("kl", 0, 2)), col("jt", 0, 32), Op.add)
         quant(A("vtq"), A("vtz"), A("vt"))
         for b in range(4):
             mm(4 + b, "wq", "wz", 128 * b, "vtq", "vtz", 0, 128)
@@ -627,8 +629,11 @@ def rank_program(g, core, T, topo):
     tq, tz = "tq%d" % R, "tz%d" % R
     for k, (a, b) in enumerate(PIECES):
         mm(k, "vq", "vz", 0, tq, tz, a, b)
-        acopy(col("ys", a, b - a), col("ps%d" % k, 0, b - a))
+        if b == C:
+            for j in range(4):
+                dma("S" if j < 2 else "A", A("osc", s_[4 * j:4 * j + 4, :]), A(tz, s_[32 * j:32 * j + 4, :]))
+            copy(col("ys", a, b - a), col("ps%d" % k, 0, b - a))
+        else:
+            acopy(col("ys", a, b - a), col("ps%d" % k, 0, b - a))
         dma("A", A("y", s_[:, a:b]), col("ys", a, b - a))
-    for k in range(4):
-        dma("S", A("osc", s_[4 * k:4 * k + 4, :]), A(tz, s_[32 * k:32 * k + 4, :]))
     emit()

@@ -4,11 +4,10 @@ from concourse.mybir import dt, AluOpType, AxisListType, ActivationFunctionType
 
 N, C, S, L, R = 8, 384, 32, 12, 2
 BIG = 1.0e29
-OWN = 16 * L
-HB = 64 * L
-FW = HB + 64
 PADC = 256
+LOADS = ((0, 128), (256, 384), (128, 256))
 PIECES = ((0, 192), (192, 384))
+ON_VECTOR = ((0, 2), (0, 2))
 F32, BF, I32, U16, MX, U8 = "float32", "bfloat16", "int32", "uint16", "float8_e4m3fn_x4", "uint8"
 
 SCRATCH = {}
@@ -21,54 +20,52 @@ def _sb(d, shape, names):
 
 _sb(BF, [4 * C], "xs ee xn")
 _sb(BF, [512], "us vs zt vt")
-_sb(BF, [2048], "idt")
-_sb(BF, [256], "m0 m1 ne0 ne1 sc0 sc1 sj0 sj1")
-_sb(BF, [192], "c11 fb fr")
-_sb(BF, [FW], "fw0 fw1 fw2 fw3")
+_sb(BF, [516], "idt")
+_sb(BF, [256], "one m0 m1 ne0 ne1 sc0 sc1 sj0 sj1")
+_sb(BF, [160], "c12 fb fr")
+_sb(BF, [704], "fw0 fw1 fw2 fw3")
 _sb(MX, [128], "uq uq2 vq vtq via0 via1")
-_sb(U8, [128], "uz uz2 vz vtz")
+_sb(U8, [128], "uz uz2 vz vtz viz0 viz1")
 _sb(MX, [512], "wq idq")
 _sb(U8, [512], "wz idz")
 _sb(MX, [C], "eq8 tq0 tq1 tq2 hq0 hq1")
 _sb(U8, [C], "ez tz0 tz1 tz2 hz0 hz1")
-_sb(I32, [1], "pi")
-_sb(I32, [4], "ints")
-_sb(U16, [8], "ul kl vo")
+_sb(I32, [8], "p16 p7 ints")
+_sb(U16, [8], "ul l1 l3 vo")
 _sb(U16, [26], "cl eo")
-_sb(F32, [4], "fc vf cnt sg")
-_sb(F32, [12], "pm land0 land1")
-_sb(F32, [16], "cc")
-_sb(F32, [26], "st w4")
-_sb(F32, [32], "th0 th1 c12 acc pt olb")
-_sb(F32, [36], "pw0 pw1")
-_sb(F32, [64], "dm ec cbb dr sig pc pdd kr the br")
-_sb(F32, [68], "npp")
-_sb(F32, [80], "ge eq")
-_sb(F32, [96], "jt pb prow")
-_sb(F32, [200], "sx")
-_sb(F32, [256], "row ct")
-_sb(F32, [288], "cg")
+_sb(F32, [8], "fc cc cnt thr sg")
+_sb(F32, [12], "land0 land1")
+_sb(F32, [16], "acc pm")
+_sb(F32, [26], "st")
+_sb(F32, [32], "th0 th1 olb")
+_sb(F32, [36], "pw0 pw1 meet iw7")
+_sb(F32, [64], "dm cb hk fh zz prel dg")
+_sb(F32, [72], "tp")
+_sb(F32, [75], "iw")
+_sb(F32, [96], "row c16 cn cge ck pcr pc pb prow")
+_sb(F32, [128], "jp")
+_sb(F32, [168], "sx")
+_sb(F32, [192], "mw kw d1 hs")
+_sb(F32, [194], "d0")
+_sb(F32, [256], "ct")
+_sb(F32, [272], "cg")
 _sb(F32, [C], "ys")
 _sb(F32, [4 * C], "rl")
-_sb(F32, [7, 12], "cb rr ll bi")
 _sb(F32, [12, 32], "et")
-_sb(F32, [8, 64], "mm")
-_sb(F32, [7, 64], "tt")
-_sb(F32, [27, 8], "ea")
-_sb(F32, [8, 12], "junk")
-_sb(F32, [4, 20], "pd")
-_sb(F32, [3, 72], "cmp")
-_sb(F32, [2, 80], "xy")
-_sb(F32, [2, 32], "bs")
-_sb(F32, [2, 48], "w2")
-_sb(F32, [2, 24], "w3")
+_sb(F32, [8, 60], "mm")
+_sb(F32, [7, 56], "tt")
+_sb(F32, [4, 75], "zl")
+_sb(F32, [2, 75], "wn")
+_sb(F32, [4, 153], "tb")
+_sb(F32, [8, 25], "junk")
+_sb(F32, [6, 64], "cmp")
 for _b in range(8):
     SCRATCH["ps%d" % _b] = ("psum", [128, 512], F32)
 
-ROT = {"V": 48, "A": 32, "P": 16, "G": 8}
+ROT = {"V": 48, "A": 32, "P": 16, "G": 12}
 NDMA = 20
 SEMAPHORES = (["%s%d" % (q.lower(), i) for q in "VAPG" for i in range(ROT[q])] + ["d%d" % i for i in range(NDMA)]
-              + ["sent"] + ["%s%d" % (n, t) for n in ("halo", "cost", "place") for t in range(R)])
+              + ["sent"] + ["%s%d" % (n, t) for n in ("plane", "halo", "cost", "place") for t in range(R)])
 
 
 def from_left(b):
@@ -98,35 +95,33 @@ def as_mask(engines):
     return m
 
 
-def helper(T, topo, a, o):
+def relays(T, topo, a):
     c = T.cores[a]
-    free = [h for h in topo.cores_of(c) if T.rank_of(h) is None and topo.die(h) == topo.die(c)
+    free = [h for h in topo.cores_of(c) if T.rank_of(h) is None and topo.die(h) != topo.die(c)
             and all(topo.may_write(h, T.cores[x]) for x in neighbours(a))]
-    return free[0 if o < a else 1]
-
-
-def chip_engines(T, topo, a):
-    nb = neighbours(a)
-    far = [e for x in range(N) if x != a for e in topo.engines(T.cores[a], T.cores[x])]
-    es = [e for e in topo.engines(T.cores[a], helper(T, topo, a, nb[0])) if e not in far]
-    n = len(es) // len(nb)
-    return {x: es[n * k:n * k + n] for k, x in enumerate(nb)}
+    jobs = [(o, k) for o in neighbours(a) for k in range(2)]
+    es = topo.engines(c, free[0])
+    n = len(es) // len(jobs)
+    return [(free[i], o, k, es[n * i:n * i + n]) for i, (o, k) in enumerate(jobs)]
 
 
 def hand_on(g, core, T, topo):
     for a in range(N):
-        for o in neighbours(a):
-            if helper(T, topo, a, o) == core:
-                w = L * sent_strips(a)
-                at = halo_at(o)[1 if o < a else 0]
+        for h, o, k, es in relays(T, topo, a):
+            if h == core:
+                w = L * sent_strips(a) // 2
+                at = halo_at(o)[1 if o < a else 0] + k * w
                 rid, pid = topo.addr(T.cores[o], core)
                 for t in range(R):
-                    g.wait_ge(T.sem["halo%d" % t], len(chip_engines(T, topo, a)[o]))
-                    g.remote_dma_fused([RemoteDMATransfer(
-                        dst_ids=[DstId(rid=rid, pnc=pid)], dma_engine_mask=topo.mask(core, T.cores[o]),
-                        remote_sem=T.sem["halo%d" % t], src=T["via%d" % t][:, 0:w].bitcast(dt.uint8),
-                        dst=T["hq%d" % t][:, at:at + w].bitcast(dt.uint8))], local_sem=T.sem.sent)
-                g.wait_ge(T.sem.sent, R * len(topo.engines(core, T.cores[o])))
+                    for sem, src, to in (
+                            ("plane%d" % t, T["viz%d" % t][:, 0:w], T["hz%d" % t][:, at:at + w]),
+                            ("halo%d" % t, T["via%d" % t][:, 0:w].bitcast(dt.uint8),
+                             T["hq%d" % t][:, at:at + w].bitcast(dt.uint8))):
+                        g.wait_ge(T.sem[sem], len(es))
+                        g.remote_dma_fused([RemoteDMATransfer(
+                            dst_ids=[DstId(rid=rid, pnc=pid)], dma_engine_mask=topo.mask(core, T.cores[o]),
+                            remote_sem=T.sem["halo%d" % t], src=src, dst=to)], local_sem=T.sem.sent)
+                g.wait_ge(T.sem.sent, 2 * R * len(topo.engines(core, T.cores[o])))
 
 
 def rank_program(g, core, T, topo):
@@ -245,8 +240,8 @@ def rank_program(g, core, T, topo):
                 eng[o["q"]].wait_ge(T.sem[o["sem"]], 16)
         g.wait_ge(T.sem.sent, sent)
 
-    def dma(q, out, in_):
-        rec(q, lambda e: e.dma_start(real(out), real(in_)), [in_], [out], "dma")
+    def dma(q, out, in_, after=None):
+        rec(q, lambda e: e.dma_start(real(out), real(in_)), [in_, after], [out], "dma")
 
     def memset(ap, c):
         rec("V", lambda e: e.memset(real(ap), c), [], [ap])
@@ -296,10 +291,11 @@ def rank_program(g, core, T, topo):
     def lin(out, a, scale, bias):
         act(out, a, Act.Identity, bias, scale)
 
+    def fill(out, n, c, p0=0, p1=128):
+        lin(out, A("one", s_[p0:p1, 0:n]), 0.0, c)
+
     def const(name, a, b, c, p0=0, p1=128):
-        for k in range(a, b, 256):
-            n = min(256, b - k)
-            lin(A(name, s_[p0:p1, k:k + n]), A("row", s_[p0:p1, 0:n]), 0.0, c)
+        fill(A(name, s_[p0:p1, a:b]), b - a, c, p0, p1)
 
     def mm(bank, lq, lz, lo, rq, rz, a, b):
         out = A("ps%d" % bank, s_[:, 0:b - a])
@@ -312,6 +308,9 @@ def rank_program(g, core, T, topo):
             rec("G", lambda e: e.iota(real(out), pattern, base, cm, allow_small_or_imprecise_dtypes=True), [], [out])
         else:
             rec("G", lambda e: e.iota(real(out), pattern, base, cm), [], [out])
+
+    def select(out, a, pattern, op, c, base, cm):
+        rec("G", lambda e: e.affine_select(real(out), real(a), pattern, op, c, base, cm), [a], [out])
 
     def dst(to):
         rid, pid = topo.addr(to, core)
@@ -338,10 +337,12 @@ def rank_program(g, core, T, topo):
     def arrival(sem, count, writes):
         rec("R", None, [], writes, "arrival", sem, count)
 
-    others = [o for o in range(N) if o != r]
+    others = sorted((o for o in range(N) if o != r), key=lambda o: abs(2 * o - N + 1))
     wl = L * sent_strips(r - 1) if r > 0 else 0
     wr = L * sent_strips(r + 1) if r + 1 < N else 0
     ws_ = L * sent_strips(r)
+    cap = wl + C + wr
+    hb = cap + L
 
     def places_at(o):
         return (32 if o > 0 else 15), (15 if o + 1 == N else 34 if o > 0 else 32)
@@ -351,270 +352,288 @@ def rank_program(g, core, T, topo):
     low = 2 * r < N
     lo, hi = (min(0, r - 1), r + 1) if low else (r - 1, max(N - 1, r + 1))
     first = 0 if low else 4
-    extra = [b for b in range(max(lo, 0), min(hi, N - 1) + 1) if not first <= b < first + 4]
+    blocks = list(range(max(lo, 0), min(hi, N - 1) + 1))
+    extra = [b for b in blocks if not first <= b < first + 4]
     nh = 1 + len(extra)
-    nblk = hi - lo + 1
+    nrow = S * (hi - lo + 1)
     win = S * (r - lo) - 16
-    cst = float(-C * r + (L - 1) * S * lo) if low else float(C * (N - r))
 
     def slot(o, at):
         return 0 if o == at else 4 + o - (1 if o > at else 0)
 
     dma("A", A("us"), A("u"))
-    for a, b in PIECES:
+    for a, b in LOADS:
         dma("S", A("xs", s_[:, 4 * a:4 * b]), A("x", s_[:, 4 * a:4 * b]))
     dma("S", A("wq", None, "u8"), A("wc"))
     dma("S", A("wz"), A("ws"))
-    dma("S", A("vs"), A("v"))
 
-    iota(A("pi"), [[0, 1]], 0, 1, False)
-    iota(A("row"), [[1, 256]], 0, 0)
-    iota(A("cb"), [[0, 7], [1, 12]], -6, 0)
+    iota(A("p16"), [[0, 8]], 0, 16, False)
+    iota(A("jp"), [[1, 128]], 0, -1)
+    iota(A("c16"), [[16, 24], [0, 4]], 0, 0)
+    iota(A("row"), [[1, 96]], 0, 0)
+    iota(col("iw", 0, 36), [[1, 12], [-1, 3]], 2, 0)
     iota(A("dm"), [[0, 4], [1, 16]], 0, 0)
-    iota(A("jt"), [[0, 4], [32, 24]], 0, 0)
-    JJ, KK, AA, PP = range(4)
+    JJ, S4, U2, AA, Q4 = range(5)
+    memset(A("one"), 1.0)
     memset(A("idt"), 0.0)
-    ts(col("ints", JJ), A("pi"), 15, Op.bitwise_and)
-    ts(col("ints", KK), A("pi"), 31, Op.bitwise_and)
-    ts(col("ints", AA), A("pi"), 5, Op.arith_shift_right)
-    copy(col("ints", PP), A("pi"))
-    memset(A("mm", s_[:, :, 1:64:2]), BIG)
-    copy(A("fc"), A("ints"))
-    memset(A("mm", s_[:, 0, 0:64:2]), BIG)
-    memset(A("ea", s_[:, 12:15, :]), BIG)
-    jj = col("fc", JJ)
-    ts(col("cc", 0), jj, -1.0, Op.mult, 15.0, Op.add)
+    memset(A("mm", s_[:, :, 1:5:2]), BIG)
+    memset(A("mm", s_[:, :, 53:60:2]), BIG)
+    ts(A("p7"), A("p16"), 127, Op.bitwise_and)
+    for c, (sh, mask) in enumerate(((4, 15), (4, 3), (5, 1), (9, 3), (6, 3))):
+        ts(col("ints", c), col("p16", 0), sh, Op.arith_shift_right, mask, Op.bitwise_and)
+    copy(A("ul"), A("p7"))
+    ts(A("idt", s_[:, 3:515:4]), A("jp"), 0.0, Op.is_equal)
+    copy(col("fc", 0, 5), col("ints", 0, 5))
+    for b in range(4):
+        quant(col("idq", 128 * b, 128), col("idz", 128 * b, 128), col("idt", 3 - b, 512))
     quant(A("uq"), A("uz"), A("us"))
-    ts(col("cc", 1), col("cc", 0), jj, Op.min, 16.0, Op.mult)
-    for b in range(2):
-        ts(A("idt", s_[:, 512 * b + b:512 * b + 512:4]), col("row", 0, 128), col("fc", PP), Op.is_equal)
-    ts(A("ul"), col("row", 0, 8), 0.0, Op.mult, col("cc", 1), Op.add)
-    for b in range(2, 4):
-        ts(A("idt", s_[:, 512 * b + b:512 * b + 512:4]), col("row", 0, 128), col("fc", PP), Op.is_equal)
+    jj = col("fc", JJ)
+    A1, A2, B1, B3, JH, TQ, AD = range(7)
+    ts(col("cc", A1), col("fc", S4), 3.0, Op.is_lt, 0.5, Op.mult)
+    ts(col("cc", A2), col("fc", S4), 3.0, Op.is_lt)
     copy(A("uq2", None, "u32"), ind(A("uq", None, "u32"), A("ul")))
     copy(A("uz2"), ind(A("uz"), A("ul")))
 
+    fill(A("tt", s_[:, :, 0:48:2]), 168, 0.0)
+    fill(A("zl", s_[:, :, 0:75:3]), 100, 0.0)
+    fill(A("zl", s_[:, 0:3, 37:39]), 6, 0.0)
+    fill(A("tb", s_[:, :, 2:39:3]), 52, 0.0)
+    fill(A("tb", s_[:, 0:3, 116:153:3]), 39, 0.0)
+    fill(A("wn", s_[:, :, 38]), 2, 0.0)
+    const("iw", 36, 39, 0.0)
+    const("pm", 12, 13, BIG)
     for t in range(R):
-        const("land%d" % t, 0, 4, 0.0)
-    lin(A("tt", s_[:, :, 0:64:2]), col("row", 0, 224), 0.0, 0.0)
-    lin(A("cb"), A("cb"), 1.0, 0.5)
-    const("acc", 0, 32, 0.0)
-    lin(A("cb", s_[:, 6, :]), A("cb", s_[:, 6, :]), 1.0, 6.0)
+        const("land%d" % t, 1, 4, 0.0)
+    if hi - lo + 1 > len(blocks):
+        const("fb", 0, nrow, 1.0)
+    const("c12", 0, nrow, float(L if low else -L))
+    const("ck", 0, 96, 0.0)
+    const("tp", 0, 8, 0.0)
+    const("d0", 0, 1, 0.0)
     for b in range(4):
-        const("fw%d" % b, 0, OWN - wl, 0.0)
-        const("fw%d" % b, OWN + C + wr, HB, 0.0)
-    if hend > PADC:
-        const("zt", 0, 512, 0.0)
-    const("vt", 256, 512, 0.0)
+        const("fw%d" % b, cap, hb, 0.0)
+    const("st", 2 * r, 2 * r + 2, 0.0)
     for a in range(4):
-        const("st", 0, 2, float(slot(first + a, r)), 32 * a, 32 * a + 32)
-    for o in range(N):
-        const("st", 2 + 2 * o, 4 + 2 * o, float(slot(o, r)))
+        const("st", 16, 18, float(slot(first + a, r)), 32 * a, 32 * a + 32)
+    lin(col("cc", AD), col("fc", AA), 2.0, 0.0)
+    lin(col("cc", JH), jj, 1.0, 0.5)
+    lin(col("cc", TQ), col("fc", Q4), 16.0, 0.5)
+    lin(col("cc", B3), col("fc", S4), 64.0, 31.0)
+    if r > 0:
+        lin(col("st", 0, 2 * r), A("c16", s_[:, 0:4 * r:2]), 0.0625, 4.0)
+    if r + 1 < N:
+        lin(col("st", 2 * r + 2, 14 - 2 * r), A("c16", s_[:, 4 * r + 4:32:2]), 0.0625, 3.0)
+    lin(A("cn"), A("c16"), 1.0, jj)
+    lin(A("cge"), A("c16"), 1.0, col("cc", JH))
+    lin(col("cc", B3), col("fc", U2), -63.0, col("cc", B3))
     for k, c in enumerate((places_at(r)[0], 15, places_at(r)[1])):
         lin(col("st", 18 + 2 * k, 2), col("row", 0, 2), 1.0, float(c))
-    lin(col("cc", 2), col("fc", AA), 2.0, 0.0)
-    lin(col("cc", 3), col("fc", PP), 1.0, float(S * first))
-    if extra:
-        lin(col("cc", 4), col("fc", KK), 1.0, float(S * extra[0]))
-    lin(col("cc", 12), jj, float(L), 6.0)
-    lin(col("cc", 13), jj, 2.0, 0.0)
-    lin(col("cc", 8), jj, 32.0, 1.0 - 2 * cst)
-    lin(col("cc", 10), jj, 32.0, 257.0 - 2 * cst)
-    lin(col("st", 24, 2), col("row", 0, 2), 1.0, col("cc", 2))
-    for h in range(nh):
-        lin(col("cc", 5 + h), col("cc", 3 + h), 2.0, -float(N * S))
-    lin(A("pd", s_[:, :, 16]), A("row", s_[:, 0:64:16]), float(L), col("cc", 12))
-    lin(A("jt"), A("jt"), 1.0, col("cc", 13))
-    const("c11", 0, 192, float(L - 1))
-    const("fb", 0, 192, 0.0)
-    lin(A("ec"), col("row", 0, 64), 2.0, 2.0 * HB)
-    lin(A("bs", s_[:, 1, :]), col("row", 0, 32), 0.0, 0.0)
-    lin(A("c12"), col("row", 0, 32), float(L), 6.0)
-    lin(A("cbb"), col("row", 0, 64), 2.0 * L, -2 * cst)
-    lin(A("npp", s_[:, 65:68:2]), col("row", 0, 2), 0.0, 1.0e6)
-    lin(col("npp", 64), jj, 2.0e6, -15.0e6)
-    lin(col("npp", 66), jj, -2.0e6, 15.0e6)
+    lin(col("st", 24, 2), col("row", 0, 2), 1.0, col("cc", AD))
+    lin(A("pcr"), col("row", 0, 96), float(L), float(wl - C))
+    lin(A("cb"), col("row", 0, 64), float(L - 1), float(wl - 16 * L - hb))
+    lin(A("hk"), col("row", 0, 64), 1.0, float(hb))
+    lin(col("thr", 0, 6), col("row", 0, 6), 64.0, col("cc", TQ))
+    lin(col("iw", 39, 36), col("iw", 0, 36), 1.0, 0.0)
+    lin(A("iw7"), col("iw", 0, 36), 1.0, 0.5)
+    fill(A("cn", s_[:, 3:96:4]), 24, 0.0)
+    fill(A("cge", s_[:, 3:96:4]), 24, -1.0e9)
+    lin(A("ck", s_[:, 0:96:4]), A("c16", s_[:, 0:96:4]), 1.0, jj)
 
-    def rank_constants():
-        for h in range(nh):
-            const("th%d" % h, 0, 32, col("cc", 5 + h))
-            act(A("sj%d" % h), A("row"), Act.Abs, col("cc", 3 + h), -1.0)
-        for h in range(nh):
-            act(A("m%d" % h), A("sj%d" % h), Act.Sign, -0.5, 1.0)
+    def rank_constants(h, b):
+        iota(A("th%d" % h), [[0, 32]], 2 * S * b - N * S + 1, 2)
+        select(A("m%d" % h), A("one"), [[1, 256]], Op.not_equal, -1.0, -S * b, -1)
+    rank_constants(0, first)
 
     def late_constants():
-        copy(A("cl"), A("st"))
-        ts(col("cc", 11), jj, 8.0, Op.is_ge, -768.0, Op.mult)
-        ts(A("dm"), A("dm"), jj, Op.is_equal, -0.5, Op.mult)
-        ts(col("cc", 9), col("cc", 8), col("cc", 11), Op.add, 512.0, Op.add)
+        ts(A("pcr"), A("pcr"), 0.0, Op.max, float(cap), Op.min)
+        ts(col("cc", B1), col("fc", S4), 39.0, Op.add, col("cc", A2), Op.mult)
+        ts(A("dm"), A("dm"), jj, Op.is_equal, BIG, Op.mult)
+        memset(col("vt", 256, 256), 0.0)
+        transp(A("pc"), A("pcr"))
         if hend > PADC:
+            memset(A("zt"), 0.0)
             for t in range(R):
                 quant(col("hq%d" % t, PADC, 128), col("hz%d" % t, PADC, 128), A("zt"))
-        quant(A("vq"), A("vz"), A("vs"))
 
-    for a, b in PIECES:
+    for a, b in LOADS:
         quant_run("tq0", "tz0", "xs", a, b)
     for t in range(R):
         tq, tz, hq, hz, land, pw = ("%s%d" % (n, t) for n in ("tq", "tz", "hq", "hz", "land", "pw"))
         mm(0, "uq2", "uz2", 0, tq, tz, 0, C)
-        if t == 0:
-            quant(A("idq"), A("idz"), A("idt"))
         for b in range(4):
             mm(4 + b, "idq", "idz", 128 * b, tq, tz, 0, C)
-        edge = {r - 1: s_[:, 0:ws_], r + 1: s_[:, C - ws_:C]}
-        send("halo%d" % t, [(chip_engines(T, topo, r)[o], A(tq, edge[o], "u8"),
-                             [(helper(T, topo, r, o), A("via%d" % t, s_[:, 0:ws_], "u8"))]) for o in neighbours(r)])
-        at = {o: halo_at(o)[1 if o < r else 0] for o in neighbours(r)}
-        send_pair("halo%d" % t, {o: (A(tz, edge[o]), col(hz, at[o], ws_)) for o in neighbours(r)})
+        edge = {r - 1: 0, r + 1: C - ws_}
+        half = ws_ // 2
+        send("plane%d" % t, [(es, col(tz, edge[o] + k * half, half), [(h, col("viz%d" % t, 0, half))])
+                             for h, o, k, es in relays(T, topo, r)])
+        send("halo%d" % t, [(es, A(tq, s_[:, edge[o] + k * half:edge[o] + k * half + half], "u8"),
+                             [(h, A("via%d" % t, s_[:, 0:half], "u8"))]) for h, o, k, es in relays(T, topo, r)])
+        if t == 0 and extra:
+            rank_constants(1, extra[0])
         for i in range(L):
             transp(A("et", s_[:, i, :]), A("ps0", s_[:, i:C:L]))
-        act(A("mm", s_[:, 0, 3:27:2]), A("et", s_[:, :, 0]), Act.Abs)
-        act(A("mm", s_[:, 0, 33:57:2]), A("et", s_[:, :, 8]), Act.Abs)
-        act(A("mm", s_[:, 0, 6:30:2]), A("et", s_[:, :, 1]), Act.Abs)
-        act(A("mm", s_[:, 0, 36:60:2]), A("et", s_[:, :, 9]), Act.Abs)
-        act(A("ea", s_[:, 0:12, 1:7]), A("et", s_[:, :, 2:8]), Act.Abs)
-        act(A("ea", s_[:, 15:27, 1:3]), A("et", s_[:, :, 10:12]), Act.Abs)
+        def own(k):
+            b, a = k // 2, k % 2 * (C // 2)
+            acopy(col("fw%d" % b, wl + a, C // 2), col("ps%d" % (4 + b), a, C // 2))
+        for k in range(3):
+            own(k)
+        act(A("mm", s_[:, 0, 5:53:2]), A("et", s_[:, :, 0:8:7]), Act.Abs)
 
-        def back(k, c):
-            if k == 0:
-                tt(A("rr", s_[:, c, :]), A("mm", s_[:, c, 5:29:2]), A("tt", s_[:, c, 1:25:2]), Op.is_lt)
-            elif k == 1:
-                tt(A("ll", s_[:, c, :]), A("mm", s_[:, c, 3:27:2]), A("tt", s_[:, c, 5:29:2]), Op.is_le)
-            elif k == 2:
-                tt(A("rr", s_[:, c, :]), A("cb", s_[:, c, :]), A("rr", s_[:, c, :]), Op.subtract)
-            else:
-                tt(A("bi", s_[:, c, :]), A("ll", s_[:, c, :]), A("rr", s_[:, c, :]), Op.add)
+        def sides(q, at, s):
+            tt(A("zl", s_[:, q, at + 1:at + 36:3]), A("mm", s_[:, s, 5:50:4]), A("tt", s_[:, s, 9:54:4]), Op.is_le)
+            tt(A("zl", s_[:, q, at + 2:at + 36:3]), A("mm", s_[:, s, 9:54:4]), A("tt", s_[:, s, 1:46:4]), Op.is_ge)
+
+        def table(q, w, n):
+            scan(A("tb", s_[:, q, 39:39 + n]), A("zl", s_[:, q, 0:n]), w, 0.0, Op.mult, Op.max)
+
+        def windows(q):
+            acopy(A("wn", s_[:, q, 0:75:3]), A("tb", s_[:, q + 1, 44:117:3]))
+            copy(A("wn", s_[:, q, 1:75:3]), A("tb", s_[:, q + 1, 41:114:3]))
+            acopy(A("wn", s_[:, q, 2:36:3]), A("tb", s_[:, q + 1, 38:72:3]))
+            copy(A("wn", s_[:, q, 41:75:3]), A("tb", s_[:, q + 1, 77:111:3]))
         for s in range(7):
-            n = 27 if s < 4 else 12
-            tt(A("tt", s_[:, s, 1:2 * n + 4:2]), A("mm", s_[:, s, 1:2 * n + 4:2]), A("mm", s_[:, s, 3:2 * n + 6:2]), Op.min)
-            if s > 0:
-                k = 15 if s == 3 else n
-                (acopy if s < 4 else copy)(A("mm", s_[:, s, 6:2 * k + 6:2]), A("ea", s_[:, 0:k, s]))
             if s == 3:
-                copy(A("mm", s_[:, 3, 36:60:2]), A("mm", s_[:, 3, 3:27:2]))
-                for b in range(4):
-                    acopy(col("fw%d" % b, OWN, C), col("ps%d" % (4 + b), 0, C))
-            scan(A("mm", s_[:, s + 1, 2:2 * n + 2]), A("tt", s_[:, s, 0:2 * n]), A("mm", s_[:, s, 5:2 * n + 5]), 0.0,
-                 Op.min, Op.max)
+                tt(col("meet", 0, 24), A("mm", s_[:, 3, 5:53:2]), A("mm", s_[:, 3, 7:55:2]), Op.max)
+                tt(col("meet", 24, 12), A("mm", s_[:, 3, 5:53:4]), A("mm", s_[:, 3, 11:59:4]), Op.max)
+            tt(A("tt", s_[:, s, 1:56:2]), A("mm", s_[:, s, 1:56:2]), A("mm", s_[:, s, 5:60:2]), Op.min)
+            far = 6 - s if s < 3 else s + 9
+            act(A("mm", s_[:, s, 10:58:2]), A("et", s_[:, :, s + 1:far + 1:far - s - 1]), Act.Abs)
+            if s < 5:
+                own(3 + s)
             if s == 3:
-                red(col(land, 0), A("mm", s_[:, 4, 33:57:2]), Op.min)
+                red(col(land, 0), A("meet"), Op.min)
                 send("cost%d" % t, [(shared_engines(r, others), col(land, 0),
                                      [(T.cores[o], col(land, slot(r, o))) for o in others])])
-            if s == 4:
-                back(0, s_[0:5])
-            if s == 5:
-                back(1, s_[0:5])
             if s == 6:
-                back(0, s_[5:7])
-                back(1, s_[5:7])
-        m7 = A("mm", s_[:, 7, 3:27:2])
-        scan(A("pm"), m7, m7, BIG, Op.min, Op.min)
-        back(2, s_[5:7])
-        back(2, s_[0:5])
-        back(3, s_[5:7])
-        back(3, s_[0:5])
-        act(A("junk", s_[:, 7, :]), A("pm"), Act.Sign, col(land, 0), -1.0, col("acc", 8))
-        for gg in range(7, 0, -1):
-            act(A("junk", s_[:, gg - 1, :]), A("bi", s_[:, gg - 1, :]), Act.Sign, col("acc", 8 if gg == 7 else gg),
-                1.0 if gg == 7 else 2.0, col("acc", gg - 1))
-        if t == 0:
-            rank_constants()
-            late_constants()
-        ts(col("acc", 7), col("acc", 8), 2.0, Op.mult, float(L), Op.add)
-        copy(col(pw, 0, 32), ind(col("acc", 0, 8), col("cl", 24, 2)))
+                table(2, A("iw"), 75)
+            scan(A("mm", s_[:, s + 1, 4:52]), A("tt", s_[:, s, 0:48]), A("mm", s_[:, s, 9:57]), 0.0, Op.min, Op.max)
+            if s == 1 and t == 0:
+                copy(A("cl"), A("st"))
+            if s == 3:
+                sides(s_[0:3], 39, s_[0:3])
+            if s == 4:
+                sides(s_[0:2], 0, s_[3:5])
+            if s == 5:
+                sides(2, 0, 5)
+        sides(3, 0, 6)
+        m7 = A("mm", s_[:, 7, 5:53:4])
+        scan(col("pm", 0, 12), m7, m7, BIG, Op.min, Op.min)
+        windows(1)
+        table(3, A("iw7"), 36)
+        table(1, A("wn", s_[:, 1, :]), 75)
+        act(A("junk", s_[:, 7, 0:13]), col("pm", 0, 13), Act.Sign, col(land, 0), -1.0, col("acc", 8))
+        windows(0)
+        act(A("junk", s_[:, 6, :]), A("tb", s_[:, 3, 2:75:3]), Act.Sign, col("acc", 8), 1.0, col("acc", 6))
+        table(0, A("wn", s_[:, 0, :]), 75)
+        lin(col("acc", 7), col("acc", 8), 2.0, 1.0)
+        for q in range(3):
+            act(A("junk", s_[:, 3 + q, :]), A("tb", s_[:, q, 2:75:3]), Act.Sign, col("acc", 6), 2.0, col("acc", 3 + q))
+        for q in (2, 1, 0):
+            act(A("junk", s_[:, q, :]), A("tb", s_[:, q, 80:153:3]), Act.Sign, col("acc", 3), 2.0, col("acc", q))
+        lin(col(pw, 0, 32), ind(col("acc", 0, 8), col("cl", 24, 2)), -0.5, -0.5)
         at = {o: places_at(o)[1 if o < r else 0] for o in neighbours(r)}
         send_pair("place%d" % t, {o: (col(pw, 15, 2), col(pw, at[o], 2)) for o in neighbours(r)})
-        if t == R - 1:
-            transp(A("pt", s_[0:32, :]), A("acc", s_[0:32, :]))
-            ts(A("pt", s_[0:32, :]), A("pt", s_[0:32, :]), -0.5, Op.mult)
-            tt(A("olb", s_[0:32, :]), A("pt", s_[0:32, :]), A("c12", s_[0:32, :]), Op.add)
-            dma("S", A("ol"), A("olb", s_[0:8, :]))
+        if t == 0:
+            late_constants()
+        else:
+            quant(A("vq"), A("vz"), A("vs"))
         arrival("cost%d" % t, sum(len(shared_engines(o, [x for x in range(N) if x != o])) for o in others),
                 [col(land, 4, 7)])
-        copy(col("cg", 0, 160), ind(col(land, 0, 11), col("cl", 0, 10)))
-        acopy(col("cg", 160, 128), ind(col(land, 0, 11), col("cl", 10, 8)))
-        transp(A("ct"), col("cg", 32, 256))
-        sel = [col("cg", 0)] + [col("cg", 32 + S * b) for b in extra]
-        for h in range(nh):
-            ts(A("ne%d" % h), A("ct"), sel[h], Op.not_equal, -1.0, Op.mult)
-            act(A("sj%d" % h), A("ct"), Act.Sign, sel[h], -1.0, col("sg", h))
-        arrival("halo%d" % t, sum(share(o) + len(topo.engines(helper(T, topo, o, r), core)) for o in neighbours(r)),
-                [A(hq, s_[:, h0:PADC]), A(hz, s_[:, h0:PADC])])
+        copy(col("cg", 0, 128), ind(col(land, 0, 11), col("cl", 0, 8)))
+        acopy(col("cg", 128, 144), ind(col(land, 0, 11), col("cl", 8, 9)))
+        for k in range(2):
+            transp(col("ct", 128 * k, 128), col("cg", 128 * k, 128))
+        arrival("halo%d" % t, sum(2 * len(topo.engines(h, core)) for o in neighbours(r)
+                                  for h, x, k, es in relays(T, topo, o) if x == r), [A(hq, s_[:, h0:PADC]), A(hz, s_[:, h0:PADC])])
         for b in range(4):
             mm(b, "idq", "idz", 128 * b, hq, hz, h0, hend)
 
         def unpack(b):
             if wl:
-                acopy(col("fw%d" % b, OWN - wl, wl), col("ps%d" % b, 0, wl))
+                acopy(col("fw%d" % b, 0, wl), col("ps%d" % b, 0, wl))
             if wr:
-                acopy(col("fw%d" % b, OWN + C, wr), col("ps%d" % b, wl, wr))
-        for b in range(3):
-            unpack(b)
+                acopy(col("fw%d" % b, wl + C, wr), col("ps%d" % b, wl, wr))
+        if t > 0:
+            unpack(0)
+            unpack(1)
+        sel = [col("cg", 256)] + [col("cg", S * b) for b in extra]
+        for h in range(nh):
+            ts(A("ne%d" % h), A("ct"), sel[h], Op.not_equal, -1.0, Op.mult)
+            act(A("sj%d" % h), A("ct"), Act.Sign, sel[h], -1.0, col("sg", h))
         for h in range(nh):
             scan(A("sc%d" % h), A("m%d" % h), A("ne%d" % h), col("sg", h), Op.mult, Op.add)
-        for b in sorted(range(max(lo, 0), min(hi, N - 1) + 1), key=lambda b: b in extra):
+        if t > 0:
+            unpack(2)
+        for b in sorted(blocks, key=lambda b: b in extra):
             h, a = (1, 0) if b in extra else (0, b - first)
-            ts(A("fb", s_[0:32, S * (b - lo):S * (b - lo) + S]), A("th%d" % h, s_[32 * a:32 * a + 32, :]),
-               A("sc%d" % h, s_[32 * a:32 * a + 32, 255:256]), Op.is_ge, 2.0, Op.mult)
-        transp(A("fr", s_[0:32, 0:S * nblk]), A("fb", s_[0:32, 0:S * nblk]))
-        scan(A("sx", s_[0:32, 1:1 + S * nblk]), A("fr", s_[0:32, 0:S * nblk]), A("c11", s_[0:32, 0:S * nblk]), 0.0,
-             Op.add, Op.add)
-        prow, npp = col("prow", 16, 64), col("npp", 0, 64)
+            act(A("fb", s_[0:32, S * (b - lo):S * (b - lo) + S]), A("th%d" % h, s_[32 * a:32 * a + 32, :]), Act.Sign,
+                A("sc%d" % h, s_[32 * a:32 * a + 32, 255:256]), -1.0)
+        for b in range(3, 4) if t > 0 else range(2):
+            unpack(b)
+        for a in range(4):
+            transp(A("fr", s_[32 * a:32 * a + 32, 0:nrow]), A("fb", s_[0:32, 0:nrow]))
+        if low:
+            scan(col("sx", 1, win + 63), col("c12", 0, win + 63), col("fr", 0, win + 63), float(-C * r + (L - 1) * S * lo),
+                 Op.add, Op.subtract)
+        else:
+            back = s_[:, nrow - 1:win - 1:-1]
+            scan(A("sx", back), A("c12", back), A("fr", back), float(C * (N - r) + (L - 1) * S * (hi - N + 1)),
+                 Op.add, Op.add)
+        start, sig = col("sx", win, 64), col("fr", win, 64)
+        lin(A("fh"), sig, -0.25, 0.75)
+        acopy(col("mw", 0, 64), sig)
+        lin(col("kw", 64, 63), col("fr", win, 63), -1.0, 0.0)
+        acopy(col("mw", 127, 64), sig)
+        vo = col("vo", 0, 4)
+        for n in range(6):
+            act(A("cmp", s_[:, n, :]), start, Act.Sign, col("thr", n), -1.0, col("cnt", n))
+        tt(col("mw", 64, 63), col("fr", win, 63), col("fr", win + 1, 63), Op.mult)
         arrival("place%d" % t, sum(share(o) for o in neighbours(r)), [A(pw, s_[:, 32:pend])])
-        copy(A("pb"), ind(col(pw, 0, pend), col("cl", 18, 6)))
-        for a in range(4):
-            lin(A("dr", s_[32 * a:32 * a + 32, :]), A("fr", s_[0:32, win:win + 64]), 0.5, 0.0)
-        lin(A("pdd"), A("dr"), 2.0, 2 * cst + L)
-        unpack(3)
-        for a in range(4):
-            o, i = A("npp", s_[32 * a:32 * a + 32, 0:64]), A("sx", s_[0:32, win:win + 64])
-            if low:
-                ts(o, i, -2.0, Op.mult)
-            else:
-                k = S * (N - lo)
-                ts(o, i, A("sx", s_[0:32, k:k + 1]), Op.subtract, -2.0, Op.mult)
+        tt(A("pb"), ind(col(pw, 0, pend), col("cl", 18, 6)), A("pc"), Op.add)
+        tt(A("zz"), start, A("fh"), Op.add)
         transp(A("prow"), A("pb"))
-        for x, n in enumerate((64, 66, 68)):
-            act(A("cmp", s_[:, x, 0:n]), col("npp", 0, n), Act.Sign, col("cc", 8 + x), 1.0, col("cnt", x))
-        tt(A("pc"), A("pdd"), npp, Op.subtract)
-        tt(A("pd", s_[:, :, 0:16]), prow, A("dm"), Op.mult)
-        tt(A("the"), A("pc"), prow, Op.subtract)
-        for x in range(4):
-            if x < 2:
-                red(col("vf", x), A("pd", s_[:, x, 0:17]), Op.add)
-            else:
-                act(A("cmp", s_[:, x - 2, 0:17]), A("pd", s_[:, x, 0:17]), Act.Identity, None, None, col("vf", x))
-        lin(A("sig"), A("dr"), -4.0, 2.0)
-        ts(col("kl", 0, 3), col("cnt", 0, 3), 0.5, Op.mult, 31.0, Op.add)
-        ts(col("kl", 3, 2), col("cnt", 0, 2), 0.5, Op.mult, 33.0, Op.add)
-        kl, j80 = col("kl", 0, 5), col("jt", 0, 80)
-        copy(col("vo", 0, 4), A("vf"))
-        for b in range(4):
-            acopy(A("vt", s_[:, b:256:4]), ind(col("fw%d" % b, 0, HB), col("vo", 0, 4)))
-        tt(A("kr"), A("ec"), A("dr"), Op.mult)
-        tt(A("ge"), ind(A("the"), kl), j80, Op.is_le)
-        tt(A("eq"), ind(A("the"), kl), j80, Op.is_equal)
-        tt(A("br"), npp, A("cbb"), Op.add)
-        tt(A("xy", s_[:, 0, :]), ind(A("sig"), kl), A("ge"), Op.mult)
-        tt(A("xy", s_[:, 1, :]), ind(A("kr"), kl), A("eq"), Op.mult)
-        tt(A("bs", s_[:, 0, :]), ind(A("br"), col("kl", 0, 2)), col("jt", 0, 32), Op.add)
+        tt(col("kw", 0, 64), A("cb"), start, Op.subtract)
+        scan(A("dg"), A("dm"), col("prow", 16, 64), BIG, Op.add, Op.min)
+        tt(A("prel"), col("prow", 16, 64), col("pcr", 16, 64), Op.subtract)
+        copy(vo, A("dg", s_[:, 15:64:16]))
+        ts(col("l3", 0, 6), col("cnt", 0, 6), 0.5, Op.mult, col("cc", B3), Op.add)
+        tt(col("tp", 8, 64), A("zz"), A("prel"), Op.add)
+        ts(col("l1", 0, 6), col("cnt", 0, 6), col("cc", A1), Op.mult, col("cc", B1), Op.add)
+        copy(A("vt", s_[:, 0:256:4]), ind(col("fw0", 0, hb), vo))
+        if t == 0:
+            unpack(2)
+            unpack(3)
+        for b in range(1, 4):
+            acopy(A("vt", s_[:, b:256:4]), ind(col("fw%d" % b, 0, hb), vo))
+        tt(col("kw", 127, 64), sig, A("hk"), Op.mult)
+        l1, l3 = col("l1", 0, 6), col("l3", 0, 6)
+        tt(A("d1", s_[:, 1:192:2]), ind(A("tp"), l1), A("cge"), Op.is_le)
+        acopy(A("d0", s_[:, 1:192:2]), ind(col("mw", 0, 191), l3))
         quant(A("vtq"), A("vtz"), A("vt"))
         for b in range(4):
             mm(4 + b, "wq", "wz", 128 * b, "vtq", "vtz", 0, 128)
+        tt(A("d0", s_[:, 2:194:2]), ind(A("tp"), l1), A("cn"), Op.not_equal)
+        tt(A("d1", s_[:, 0:192:2]), ind(col("kw", 0, 191), l3), A("ck"), Op.add)
         for b in range(4):
-            act(col("fw%d" % b, HB, 64), col("ps%d" % (4 + b), 0, 64), Act.Relu, None, 0.03125)
-        tt(A("w2", s_[:, :, 0:24]), A("xy", s_[:, :, 0:24]), A("xy", s_[:, :, 24:48]), Op.add)
-        tt(A("w2", s_[:, :, 24:48]), A("xy", s_[:, :, 48:72]), A("bs", s_[:, :, 0:24]), Op.add)
-        tt(A("w3"), A("w2", s_[:, :, 0:24]), A("w2", s_[:, :, 24:48]), Op.add)
-        tt(col("w4", 0, 24), A("w3", s_[:, 0, :]), A("w3", s_[:, 1, :]), Op.max)
-        ts(col("eo", 0, 24), col("w4", 0, 24), 0.5, Op.mult)
-        for k, (a, b) in enumerate(PIECES):
-            for e in range(4):
-                (acopy if e % 2 else copy)(A("ee", s_[:, 4 * a + e:4 * b:4]),
-                                           ind(A("fw%d" % e), A("eo", s_[:, a // 16:b // 16])))
-            quant_run("eq8", "ez", "ee", a, b)
+            act(col("fw%d" % b, hb, 64), col("ps%d" % (4 + b), 0, 64), Act.Relu, None, 0.03125)
+        scan(A("hs"), col("d0", 0, 192), A("d1"), 0.0, Op.mult, Op.add)
+        copy(col("eo", 0, 24), A("hs", s_[:, 7:192:8]))
+        if t == 0:
+            dma("S", A("vs"), A("v"), A("eo"))
+        if t == R - 1:
+            ts(A("olb"), col("prow", 32, 32), float(-wl), Op.add)
+            dma("S", A("ol"), A("olb", s_[0:128:16, :]))
         nq, nz = "tq%d" % (t + 1), "tz%d" % (t + 1)
-        for k, (a, b) in enumerate(PIECES):
+
+        def gather(k):
+            a, b = PIECES[k]
+            for e in range(4):
+                (copy if e in ON_VECTOR[k] else acopy)(A("ee", s_[:, 4 * a + e:4 * b:4]),
+                                                       ind(col("fw%d" % e, 0, hb + 64), A("eo", s_[:, a // 16:b // 16])))
+            quant_run("eq8", "ez", "ee", a, b)
+
+        def layer(k):
+            a, b = PIECES[k]
             for e in range(4):
                 mm(e, "wq", "wz", 128 * e, "eq8", "ez", a, b)
                 mm(4 + e, "idq", "idz", 128 * e, "eq8", "ez", a, b)
@@ -625,11 +644,16 @@ def rank_program(g, core, T, topo):
             quant_run(nq, nz, "xn", a, b)
             if t == R - 1:
                 dma("S", A("oc", s_[:, 4 * a:4 * b]), A(nq, s_[:, a:b], "u8"))
+        gather(0)
+        for k in range(len(PIECES)):
+            if k + 1 < len(PIECES):
+                gather(k + 1)
+            layer(k)
 
     tq, tz = "tq%d" % R, "tz%d" % R
     for k, (a, b) in enumerate(PIECES):
         mm(k, "vq", "vz", 0, tq, tz, a, b)
-        if b == C:
+        if k == len(PIECES) - 1:
             for j in range(4):
                 dma("S" if j < 2 else "A", A("osc", s_[4 * j:4 * j + 4, :]), A(tz, s_[32 * j:32 * j + 4, :]))
             copy(col("ys", a, b - a), col("ps%d" % k, 0, b - a))

@@ -7,7 +7,12 @@ BIG = 1.0e29
 PADC = 256
 LOADS = ((0, 128), (256, 384), (128, 256))
 PIECES = ((0, 192), (192, 384))
-ON_VECTOR = ((0, 2), (0, 2))
+ON_VECTOR = ((0, 1), (0,))
+V_ON_SCALAR = (2, 3)
+STEPS = [([("cost", 0)] if s == 3 else []) + ([("carry", s - 1)] if s else []) + [("scan", s), ("sides", s)]
+         + ([("across", s)] if s else []) for s in range(7)]
+LEFT = 6
+UNPACK = ({"sigma": (0, 1, 2), "counts": (3,)}, {"costs": (0, 1), "signs": (2,), "sigma": (3,)})
 F32, BF, I32, U16, MX, U8 = "float32", "bfloat16", "int32", "uint16", "float8_e4m3fn_x4", "uint8"
 
 SCRATCH = {}
@@ -19,11 +24,11 @@ def _sb(d, shape, names):
 
 
 _sb(BF, [4 * C], "xs ee xn")
-_sb(BF, [512], "us vs zt vt")
+_sb(BF, [512], "us vs vt")
 _sb(BF, [516], "idt")
 _sb(BF, [256], "one m0 m1 ne0 ne1 sc0 sc1 sj0 sj1")
 _sb(BF, [160], "c12 fb fr")
-_sb(BF, [704], "fw0 fw1 fw2 fw3")
+_sb(BF, [720], "fw0 fw1 fw2 fw3")
 _sb(MX, [128], "uq uq2 vq vtq via0 via1")
 _sb(U8, [128], "uz uz2 vz vtz viz0 viz1")
 _sb(MX, [512], "wq idq")
@@ -34,15 +39,14 @@ _sb(I32, [8], "p16 p7 ints")
 _sb(U16, [8], "ul l1 l3 vo")
 _sb(U16, [26], "cl eo")
 _sb(F32, [8], "fc cc cnt thr sg")
-_sb(F32, [12], "land0 land1")
-_sb(F32, [16], "acc pm")
+_sb(F32, [12], "land0 land1 pm")
 _sb(F32, [26], "st")
 _sb(F32, [32], "th0 th1 olb")
-_sb(F32, [36], "pw0 pw1 meet iw7")
-_sb(F32, [64], "dm cb hk fh zz prel dg")
+_sb(F32, [36], "pw0 pw1 meet")
+_sb(F32, [64], "dm hk fh fp zz dg")
 _sb(F32, [72], "tp")
-_sb(F32, [75], "iw")
-_sb(F32, [96], "row c16 cn cge ck pcr pc pb prow")
+_sb(F32, [96], "row c16 cn cge pcr pc pb prow")
+_sb(F32, [160], "ck")
 _sb(F32, [128], "jp")
 _sb(F32, [168], "sx")
 _sb(F32, [192], "mw kw d1 hs")
@@ -54,10 +58,8 @@ _sb(F32, [4 * C], "rl")
 _sb(F32, [12, 32], "et")
 _sb(F32, [8, 60], "mm")
 _sb(F32, [7, 56], "tt")
-_sb(F32, [4, 75], "zl")
-_sb(F32, [2, 75], "wn")
-_sb(F32, [4, 153], "tb")
-_sb(F32, [8, 25], "junk")
+_sb(F32, [7, 36], "zl")
+_sb(F32, [8, 81], "lb")
 _sb(F32, [6, 64], "cmp")
 for _b in range(8):
     SCRATCH["ps%d" % _b] = ("psum", [128, 512], F32)
@@ -101,8 +103,8 @@ def relays(T, topo, a):
             and all(topo.may_write(h, T.cores[x]) for x in neighbours(a))]
     jobs = [(o, k) for o in neighbours(a) for k in range(2)]
     es = topo.engines(c, free[0])
-    n = len(es) // len(jobs)
-    return [(free[i], o, k, es[n * i:n * i + n]) for i, (o, k) in enumerate(jobs)]
+    n = len(es) // 2
+    return [(free[i], o, k, es[n * k:n * k + n]) for i, (o, k) in enumerate(jobs)]
 
 
 def hand_on(g, core, T, topo):
@@ -342,10 +344,10 @@ def rank_program(g, core, T, topo):
     wr = L * sent_strips(r + 1) if r + 1 < N else 0
     ws_ = L * sent_strips(r)
     cap = wl + C + wr
-    hb = cap + L
+    hb = cap + 2 * L
 
     def places_at(o):
-        return (32 if o > 0 else 15), (15 if o + 1 == N else 34 if o > 0 else 32)
+        return (32 if o > 0 else 19), (19 if o + 1 == N else 34 if o > 0 else 32)
     h0 = halo_at(r)[0]
     hend = max(PADC, h0 + 128)
     pend = 32 + 2 * len(neighbours(r))
@@ -371,43 +373,39 @@ def rank_program(g, core, T, topo):
     iota(A("jp"), [[1, 128]], 0, -1)
     iota(A("c16"), [[16, 24], [0, 4]], 0, 0)
     iota(A("row"), [[1, 96]], 0, 0)
-    iota(col("iw", 0, 36), [[1, 12], [-1, 3]], 2, 0)
     iota(A("dm"), [[0, 4], [1, 16]], 0, 0)
-    JJ, S4, U2, AA, Q4 = range(5)
+    iota(A("lb", s_[:, :, 2:80:3]), [[0, 16], [1, 13]], -1, 0)
+    JJ, S4, U2, Q4 = range(4)
     memset(A("one"), 1.0)
     memset(A("idt"), 0.0)
     memset(A("mm", s_[:, :, 1:5:2]), BIG)
     memset(A("mm", s_[:, :, 53:60:2]), BIG)
     ts(A("p7"), A("p16"), 127, Op.bitwise_and)
-    for c, (sh, mask) in enumerate(((4, 15), (4, 3), (5, 1), (9, 3), (6, 3))):
+    for c, (sh, mask) in enumerate(((4, 15), (4, 3), (5, 1), (6, 3))):
         ts(col("ints", c), col("p16", 0), sh, Op.arith_shift_right, mask, Op.bitwise_and)
     copy(A("ul"), A("p7"))
     ts(A("idt", s_[:, 3:515:4]), A("jp"), 0.0, Op.is_equal)
-    copy(col("fc", 0, 5), col("ints", 0, 5))
+    copy(col("fc", 0, 4), col("ints", 0, 4))
     for b in range(4):
         quant(col("idq", 128 * b, 128), col("idz", 128 * b, 128), col("idt", 3 - b, 512))
     quant(A("uq"), A("uz"), A("us"))
     jj = col("fc", JJ)
-    A1, A2, B1, B3, JH, TQ, AD = range(7)
+    A1, A2, B1, B3, JH, TQ, JK = range(7)
     ts(col("cc", A1), col("fc", S4), 3.0, Op.is_lt, 0.5, Op.mult)
     ts(col("cc", A2), col("fc", S4), 3.0, Op.is_lt)
     copy(A("uq2", None, "u32"), ind(A("uq", None, "u32"), A("ul")))
     copy(A("uz2"), ind(A("uz"), A("ul")))
 
     fill(A("tt", s_[:, :, 0:48:2]), 168, 0.0)
-    fill(A("zl", s_[:, :, 0:75:3]), 100, 0.0)
-    fill(A("zl", s_[:, 0:3, 37:39]), 6, 0.0)
-    fill(A("tb", s_[:, :, 2:39:3]), 52, 0.0)
-    fill(A("tb", s_[:, 0:3, 116:153:3]), 39, 0.0)
-    fill(A("wn", s_[:, :, 38]), 2, 0.0)
-    const("iw", 36, 39, 0.0)
-    const("pm", 12, 13, BIG)
+    fill(A("zl", s_[:, :, 0:36:3]), 84, 0.0)
+    fill(A("lb", s_[:, :, 80]), 8, 0.0)
+    const("vt", 256, 512, 0.0)
     for t in range(R):
         const("land%d" % t, 1, 4, 0.0)
     if hi - lo + 1 > len(blocks):
         const("fb", 0, nrow, 1.0)
     const("c12", 0, nrow, float(L if low else -L))
-    const("ck", 0, 96, 0.0)
+    const("ck", 0, 160, 0.0)
     const("tp", 0, 8, 0.0)
     const("d0", 0, 1, 0.0)
     for b in range(4):
@@ -415,7 +413,6 @@ def rank_program(g, core, T, topo):
     const("st", 2 * r, 2 * r + 2, 0.0)
     for a in range(4):
         const("st", 16, 18, float(slot(first + a, r)), 32 * a, 32 * a + 32)
-    lin(col("cc", AD), col("fc", AA), 2.0, 0.0)
     lin(col("cc", JH), jj, 1.0, 0.5)
     lin(col("cc", TQ), col("fc", Q4), 16.0, 0.5)
     lin(col("cc", B3), col("fc", S4), 64.0, 31.0)
@@ -426,18 +423,15 @@ def rank_program(g, core, T, topo):
     lin(A("cn"), A("c16"), 1.0, jj)
     lin(A("cge"), A("c16"), 1.0, col("cc", JH))
     lin(col("cc", B3), col("fc", U2), -63.0, col("cc", B3))
-    for k, c in enumerate((places_at(r)[0], 15, places_at(r)[1])):
-        lin(col("st", 18 + 2 * k, 2), col("row", 0, 2), 1.0, float(c))
-    lin(col("st", 24, 2), col("row", 0, 2), 1.0, col("cc", AD))
+    for k, c in enumerate((places_at(r)[0], 19, places_at(r)[1])):
+        lin(col("st", 18 + 2 * k, 2), col("row", 0, 2), 1.0, float(c - 8))
     lin(A("pcr"), col("row", 0, 96), float(L), float(wl - C))
-    lin(A("cb"), col("row", 0, 64), float(L - 1), float(wl - 16 * L - hb))
+    lin(col("cc", JK), jj, -1.0, float(L - 1 + 16 * L - wl + hb))
     lin(A("hk"), col("row", 0, 64), 1.0, float(hb))
     lin(col("thr", 0, 6), col("row", 0, 6), 64.0, col("cc", TQ))
-    lin(col("iw", 39, 36), col("iw", 0, 36), 1.0, 0.0)
-    lin(A("iw7"), col("iw", 0, 36), 1.0, 0.5)
     fill(A("cn", s_[:, 3:96:4]), 24, 0.0)
     fill(A("cge", s_[:, 3:96:4]), 24, -1.0e9)
-    lin(A("ck", s_[:, 0:96:4]), A("c16", s_[:, 0:96:4]), 1.0, jj)
+    lin(A("ck", s_[:, 0:96:4]), A("c16", s_[:, 0:96:4]), -1.0, col("cc", JK))
 
     def rank_constants(h, b):
         iota(A("th%d" % h), [[0, 32]], 2 * S * b - N * S + 1, 2)
@@ -445,15 +439,19 @@ def rank_program(g, core, T, topo):
     rank_constants(0, first)
 
     def late_constants():
-        ts(A("pcr"), A("pcr"), 0.0, Op.max, float(cap), Op.min)
+        ts(A("pcr"), A("pcr"), 0.0, Op.max, float(cap + L), Op.min)
         ts(col("cc", B1), col("fc", S4), 39.0, Op.add, col("cc", A2), Op.mult)
         ts(A("dm"), A("dm"), jj, Op.is_equal, BIG, Op.mult)
-        memset(col("vt", 256, 256), 0.0)
+        copy(col("cl", 0, 24), col("st", 0, 24))
         transp(A("pc"), A("pcr"))
-        if hend > PADC:
-            memset(A("zt"), 0.0)
-            for t in range(R):
-                quant(col("hq%d" % t, PADC, 128), col("hz%d" % t, PADC, 128), A("zt"))
+
+    def beside(s):
+        acopy(A("lb", s_[:, s, 4:79:3]), A("lb", s_[:, s, 8:81:3]))
+
+    def across(s):
+        copy(A("lb", s_[:, s, 6:79:3]), A("lb", s_[:, s, 2:77:3]))
+    beside(0)
+    acopy(A("lb", s_[:, 0, 6:79:3]), A("lb", s_[:, 0, 2:77:3]))
 
     for a, b in LOADS:
         quant_run("tq0", "tz0", "xs", a, b)
@@ -464,14 +462,18 @@ def rank_program(g, core, T, topo):
             mm(4 + b, "idq", "idz", 128 * b, tq, tz, 0, C)
         edge = {r - 1: 0, r + 1: C - ws_}
         half = ws_ // 2
-        send("plane%d" % t, [(es, col(tz, edge[o] + k * half, half), [(h, col("viz%d" % t, 0, half))])
-                             for h, o, k, es in relays(T, topo, r)])
-        send("halo%d" % t, [(es, A(tq, s_[:, edge[o] + k * half:edge[o] + k * half + half], "u8"),
-                             [(h, A("via%d" % t, s_[:, 0:half], "u8"))]) for h, o, k, es in relays(T, topo, r)])
-        if t == 0 and extra:
-            rank_constants(1, extra[0])
+        for x in neighbours(r):
+            mine = [(h, edge[o] + k * half, es) for h, o, k, es in relays(T, topo, r) if o == x]
+            send("plane%d" % t, [(es, col(tz, a, half), [(h, col("viz%d" % t, 0, half))]) for h, a, es in mine])
+            send("halo%d" % t, [(es, A(tq, s_[:, a:a + half], "u8"), [(h, A("via%d" % t, s_[:, 0:half], "u8"))])
+                                for h, a, es in mine])
+        if t == 0:
+            late_constants()
+            if extra:
+                rank_constants(1, extra[0])
         for i in range(L):
             transp(A("et", s_[:, i, :]), A("ps0", s_[:, i:C:L]))
+
         def own(k):
             b, a = k // 2, k % 2 * (C // 2)
             acopy(col("fw%d" % b, wl + a, C // 2), col("ps%d" % (4 + b), a, C // 2))
@@ -479,18 +481,17 @@ def rank_program(g, core, T, topo):
             own(k)
         act(A("mm", s_[:, 0, 5:53:2]), A("et", s_[:, :, 0:8:7]), Act.Abs)
 
-        def sides(q, at, s):
-            tt(A("zl", s_[:, q, at + 1:at + 36:3]), A("mm", s_[:, s, 5:50:4]), A("tt", s_[:, s, 9:54:4]), Op.is_le)
-            tt(A("zl", s_[:, q, at + 2:at + 36:3]), A("mm", s_[:, s, 9:54:4]), A("tt", s_[:, s, 1:46:4]), Op.is_ge)
+        def sides(s):
+            tt(A("zl", s_[:, s, 1:36:3]), A("mm", s_[:, s, 9:54:4]), A("tt", s_[:, s, 1:46:4]), Op.is_lt)
+            tt(A("zl", s_[:, s, 2:36:3]), A("tt", s_[:, s, 5:50:4]), A("mm", s_[:, s, 1:46:4]), Op.is_lt)
 
-        def table(q, w, n):
-            scan(A("tb", s_[:, q, 39:39 + n]), A("zl", s_[:, q, 0:n]), w, 0.0, Op.mult, Op.max)
-
-        def windows(q):
-            acopy(A("wn", s_[:, q, 0:75:3]), A("tb", s_[:, q + 1, 44:117:3]))
-            copy(A("wn", s_[:, q, 1:75:3]), A("tb", s_[:, q + 1, 41:114:3]))
-            acopy(A("wn", s_[:, q, 2:36:3]), A("tb", s_[:, q + 1, 38:72:3]))
-            copy(A("wn", s_[:, q, 41:75:3]), A("tb", s_[:, q + 1, 77:111:3]))
+        def carry(s):
+            for w in range(min(s + 1, 2)):
+                p = 32 * ((s - w) // 2 + 1)
+                scan(A("lb", s_[0:p, s + 1, 3 + 39 * w:39 + 39 * w]), A("zl", s_[0:p, s, :]),
+                     A("lb", s_[0:p, s, 4 + 39 * w:40 + 39 * w]), 0.0, Op.mult, Op.max)
+            if s < 6:
+                beside(s + 1)
         for s in range(7):
             if s == 3:
                 tt(col("meet", 0, 24), A("mm", s_[:, 3, 5:53:2]), A("mm", s_[:, 3, 7:55:2]), Op.max)
@@ -500,120 +501,107 @@ def rank_program(g, core, T, topo):
             act(A("mm", s_[:, s, 10:58:2]), A("et", s_[:, :, s + 1:far + 1:far - s - 1]), Act.Abs)
             if s < 5:
                 own(3 + s)
-            if s == 3:
-                red(col(land, 0), A("meet"), Op.min)
-                send("cost%d" % t, [(shared_engines(r, others), col(land, 0),
-                                     [(T.cores[o], col(land, slot(r, o))) for o in others])])
-            if s == 6:
-                table(2, A("iw"), 75)
-            scan(A("mm", s_[:, s + 1, 4:52]), A("tt", s_[:, s, 0:48]), A("mm", s_[:, s, 9:57]), 0.0, Op.min, Op.max)
-            if s == 1 and t == 0:
-                copy(A("cl"), A("st"))
-            if s == 3:
-                sides(s_[0:3], 39, s_[0:3])
-            if s == 4:
-                sides(s_[0:2], 0, s_[3:5])
-            if s == 5:
-                sides(2, 0, 5)
-        sides(3, 0, 6)
-        m7 = A("mm", s_[:, 7, 5:53:4])
-        scan(col("pm", 0, 12), m7, m7, BIG, Op.min, Op.min)
-        windows(1)
-        table(3, A("iw7"), 36)
-        table(1, A("wn", s_[:, 1, :]), 75)
-        act(A("junk", s_[:, 7, 0:13]), col("pm", 0, 13), Act.Sign, col(land, 0), -1.0, col("acc", 8))
-        windows(0)
-        act(A("junk", s_[:, 6, :]), A("tb", s_[:, 3, 2:75:3]), Act.Sign, col("acc", 8), 1.0, col("acc", 6))
-        table(0, A("wn", s_[:, 0, :]), 75)
-        lin(col("acc", 7), col("acc", 8), 2.0, 1.0)
-        for q in range(3):
-            act(A("junk", s_[:, 3 + q, :]), A("tb", s_[:, q, 2:75:3]), Act.Sign, col("acc", 6), 2.0, col("acc", 3 + q))
-        for q in (2, 1, 0):
-            act(A("junk", s_[:, q, :]), A("tb", s_[:, q, 80:153:3]), Act.Sign, col("acc", 3), 2.0, col("acc", q))
-        lin(col(pw, 0, 32), ind(col("acc", 0, 8), col("cl", 24, 2)), -0.5, -0.5)
+            for what, k in STEPS[s]:
+                if what == "scan":
+                    scan(A("mm", s_[:, s + 1, 4:52]), A("tt", s_[:, s, 0:48]), A("mm", s_[:, s, 9:57]), 0.0, Op.min, Op.max)
+                elif what == "cost":
+                    red(col(land, 0), A("meet"), Op.min)
+                    send("cost%d" % t, [(shared_engines(r, others), col(land, 0),
+                                         [(T.cores[o], col(land, slot(r, o))) for o in others])])
+                else:
+                    {"sides": sides, "carry": carry, "across": across}[what](k)
+        ts(col("pm", 0, 12), A("mm", s_[:, 7, 5:53:4]), col(land, 0), Op.is_gt)
+        for k in range(LEFT, 7):
+            carry(k)
+            if k < 6:
+                across(k + 1)
+        back = A("pm", s_[:, 11::-1])
+        scan(col(pw, 8, 12), back, A("lb", s_[:, 7, 38:4:-3]), 0.0, Op.mult, Op.max)
+        scan(A(pw, s_[:, 31:19:-1]), back, A("lb", s_[:, 7, 77:43:-3]), 0.0, Op.mult, Op.max)
         at = {o: places_at(o)[1 if o < r else 0] for o in neighbours(r)}
-        send_pair("place%d" % t, {o: (col(pw, 15, 2), col(pw, at[o], 2)) for o in neighbours(r)})
-        if t == 0:
-            late_constants()
-        else:
+        send_pair("place%d" % t, {o: (col(pw, 19, 2), col(pw, at[o], 2)) for o in neighbours(r)})
+        if t == 0 and hend > PADC:
+            for k in range(R):
+                quant(col("hq%d" % k, PADC, 128), col("hz%d" % k, PADC, 128), col("xs", 0, 512))
+        if t == R - 1:
             quant(A("vq"), A("vz"), A("vs"))
-        arrival("cost%d" % t, sum(len(shared_engines(o, [x for x in range(N) if x != o])) for o in others),
-                [col(land, 4, 7)])
-        copy(col("cg", 0, 128), ind(col(land, 0, 11), col("cl", 0, 8)))
-        acopy(col("cg", 128, 144), ind(col(land, 0, 11), col("cl", 8, 9)))
-        for k in range(2):
-            transp(col("ct", 128 * k, 128), col("cg", 128 * k, 128))
         arrival("halo%d" % t, sum(2 * len(topo.engines(h, core)) for o in neighbours(r)
                                   for h, x, k, es in relays(T, topo, o) if x == r), [A(hq, s_[:, h0:PADC]), A(hz, s_[:, h0:PADC])])
         for b in range(4):
             mm(b, "idq", "idz", 128 * b, hq, hz, h0, hend)
 
-        def unpack(b):
-            if wl:
-                acopy(col("fw%d" % b, 0, wl), col("ps%d" % b, 0, wl))
-            if wr:
-                acopy(col("fw%d" % b, wl + C, wr), col("ps%d" % b, wl, wr))
-        if t > 0:
-            unpack(0)
-            unpack(1)
+        def unpack(when):
+            for b in UNPACK[t].get(when, ()):
+                if wl:
+                    acopy(col("fw%d" % b, 0, wl), col("ps%d" % b, 0, wl))
+                if wr:
+                    acopy(col("fw%d" % b, wl + C, wr), col("ps%d" % b, wl, wr))
+        unpack("costs")
+        arrival("cost%d" % t, sum(len(shared_engines(o, [x for x in range(N) if x != o])) for o in others),
+                [col(land, 4, 7)])
+        (acopy if extra else copy)(col("cg", 0, 128), ind(col(land, 0, 11), col("cl", 0, 8)))
+        acopy(col("cg", 128, 128), ind(col(land, 0, 11), col("cl", 8, 8)))
+        copy(col("cg", 256, 16), ind(col(land, 0, 11), col("cl", 16, 1)))
+        transp(col("ct", 0, 128), col("cg", 0, 128))
+        transp(col("ct", 128, 128), col("cg", 128, 128))
         sel = [col("cg", 256)] + [col("cg", S * b) for b in extra]
         for h in range(nh):
             ts(A("ne%d" % h), A("ct"), sel[h], Op.not_equal, -1.0, Op.mult)
             act(A("sj%d" % h), A("ct"), Act.Sign, sel[h], -1.0, col("sg", h))
         for h in range(nh):
             scan(A("sc%d" % h), A("m%d" % h), A("ne%d" % h), col("sg", h), Op.mult, Op.add)
-        if t > 0:
-            unpack(2)
+        unpack("signs")
         for b in sorted(blocks, key=lambda b: b in extra):
             h, a = (1, 0) if b in extra else (0, b - first)
             act(A("fb", s_[0:32, S * (b - lo):S * (b - lo) + S]), A("th%d" % h, s_[32 * a:32 * a + 32, :]), Act.Sign,
                 A("sc%d" % h, s_[32 * a:32 * a + 32, 255:256]), -1.0)
-        for b in range(3, 4) if t > 0 else range(2):
-            unpack(b)
+        unpack("sigma")
+        arrival("place%d" % t, sum(share(o) for o in neighbours(r)), [A(pw, s_[:, 32:pend])])
+        tt(A("pb"), ind(col(pw, 8, pend - 8), col("cl", 18, 6)), A("pc"), Op.add)
         for a in range(4):
             transp(A("fr", s_[32 * a:32 * a + 32, 0:nrow]), A("fb", s_[0:32, 0:nrow]))
+        transp(A("prow"), A("pb"))
         if low:
             scan(col("sx", 1, win + 63), col("c12", 0, win + 63), col("fr", 0, win + 63), float(-C * r + (L - 1) * S * lo),
                  Op.add, Op.subtract)
         else:
-            back = s_[:, nrow - 1:win - 1:-1]
-            scan(A("sx", back), A("c12", back), A("fr", back), float(C * (N - r) + (L - 1) * S * (hi - N + 1)),
+            down = s_[:, nrow - 1:win - 2:-1]
+            scan(A("sx", down), A("c12", down), A("fr", down), float(C * (N - r) + (L - 1) * S * (hi - N + 1)),
                  Op.add, Op.add)
         start, sig = col("sx", win, 64), col("fr", win, 64)
-        lin(A("fh"), sig, -0.25, 0.75)
-        acopy(col("mw", 0, 64), sig)
+        lin(A("fh"), sig, -0.25, 0.75 + 16 * L - wl + L)
+        lin(col("mw", 0, 64), sig, -1.0, 0.0)
         lin(col("kw", 64, 63), col("fr", win, 63), -1.0, 0.0)
         acopy(col("mw", 127, 64), sig)
         vo = col("vo", 0, 4)
         for n in range(6):
             act(A("cmp", s_[:, n, :]), start, Act.Sign, col("thr", n), -1.0, col("cnt", n))
-        tt(col("mw", 64, 63), col("fr", win, 63), col("fr", win + 1, 63), Op.mult)
-        arrival("place%d" % t, sum(share(o) for o in neighbours(r)), [A(pw, s_[:, 32:pend])])
-        tt(A("pb"), ind(col(pw, 0, pend), col("cl", 18, 6)), A("pc"), Op.add)
-        tt(A("zz"), start, A("fh"), Op.add)
-        transp(A("prow"), A("pb"))
-        tt(col("kw", 0, 64), A("cb"), start, Op.subtract)
         scan(A("dg"), A("dm"), col("prow", 16, 64), BIG, Op.add, Op.min)
-        tt(A("prel"), col("prow", 16, 64), col("pcr", 16, 64), Op.subtract)
+        tt(col("mw", 64, 63), col("fr", win, 63), col("fr", win + 1, 63), Op.mult)
+        before, sigb = col("sx", win - 1), col("fr", win - 1, 64)
+        scan(A("fp"), col("ck", 96, 64), sigb, before, Op.add, Op.subtract)
         copy(vo, A("dg", s_[:, 15:64:16]))
-        ts(col("l3", 0, 6), col("cnt", 0, 6), 0.5, Op.mult, col("cc", B3), Op.add)
-        tt(col("tp", 8, 64), A("zz"), A("prel"), Op.add)
-        ts(col("l1", 0, 6), col("cnt", 0, 6), col("cc", A1), Op.mult, col("cc", B1), Op.add)
-        copy(A("vt", s_[:, 0:256:4]), ind(col("fw0", 0, hb), vo))
-        if t == 0:
-            unpack(2)
-            unpack(3)
-        for b in range(1, 4):
-            acopy(A("vt", s_[:, b:256:4]), ind(col("fw%d" % b, 0, hb), vo))
         tt(col("kw", 127, 64), sig, A("hk"), Op.mult)
+        tt(A("zz"), A("fp"), A("fh"), Op.add)
+        scan(col("kw", 0, 64), col("one", 0, 64), sigb, before, Op.add, Op.subtract)
+        unpack("counts")
+
+        def seam_parts(b):
+            (acopy if b in V_ON_SCALAR else copy)(A("vt", s_[:, b:256:4]), ind(col("fw%d" % b, 0, hb), vo))
+        seam_parts(0)
+        tt(col("tp", 8, 64), A("zz"), col("prow", 16, 64), Op.add)
         l1, l3 = col("l1", 0, 6), col("l3", 0, 6)
-        tt(A("d1", s_[:, 1:192:2]), ind(A("tp"), l1), A("cge"), Op.is_le)
+        ts(l3, col("cnt", 0, 6), 0.5, Op.mult, col("cc", B3), Op.add)
+        ts(l1, col("cnt", 0, 6), col("cc", A1), Op.mult, col("cc", B1), Op.add)
+        for b in range(1, 4):
+            seam_parts(b)
         acopy(A("d0", s_[:, 1:192:2]), ind(col("mw", 0, 191), l3))
+        tt(A("d1", s_[:, 0:192:2]), ind(col("kw", 0, 191), l3), A("ck", s_[:, 0:96]), Op.add)
+        tt(A("d1", s_[:, 1:192:2]), ind(A("tp"), l1), A("cge"), Op.is_le)
         quant(A("vtq"), A("vtz"), A("vt"))
+        tt(A("d0", s_[:, 2:194:2]), ind(A("tp"), l1), A("cn"), Op.not_equal)
         for b in range(4):
             mm(4 + b, "wq", "wz", 128 * b, "vtq", "vtz", 0, 128)
-        tt(A("d0", s_[:, 2:194:2]), ind(A("tp"), l1), A("cn"), Op.not_equal)
-        tt(A("d1", s_[:, 0:192:2]), ind(col("kw", 0, 191), l3), A("ck"), Op.add)
         for b in range(4):
             act(col("fw%d" % b, hb, 64), col("ps%d" % (4 + b), 0, 64), Act.Relu, None, 0.03125)
         scan(A("hs"), col("d0", 0, 192), A("d1"), 0.0, Op.mult, Op.add)
@@ -634,13 +622,20 @@ def rank_program(g, core, T, topo):
 
         def layer(k):
             a, b = PIECES[k]
-            for e in range(4):
-                mm(e, "wq", "wz", 128 * e, "eq8", "ez", a, b)
-                mm(4 + e, "idq", "idz", 128 * e, "eq8", "ez", a, b)
+            for e in range(5):
+                if e < 4:
+                    mm(e, "wq", "wz", 128 * e, "eq8", "ez", a, b)
+                if e > 0:
+                    mm(3 + e, "idq", "idz", 128 * (e - 1), "eq8", "ez", a, b)
             for e in range(4):
                 rl = col("rl", C * e + a, b - a)
                 act(rl, col("ps%d" % e, 0, b - a), Act.Relu, None, 0.015625)
                 tt(A("xn", s_[:, 4 * a + e:4 * b:4]), col("ps%d" % (4 + e), 0, b - a), rl, Op.add)
+                if e == 0 and k > 0:
+                    pack(k - 1)
+
+        def pack(k):
+            a, b = PIECES[k]
             quant_run(nq, nz, "xn", a, b)
             if t == R - 1:
                 dma("S", A("oc", s_[:, 4 * a:4 * b]), A(nq, s_[:, a:b], "u8"))
@@ -649,6 +644,7 @@ def rank_program(g, core, T, topo):
             if k + 1 < len(PIECES):
                 gather(k + 1)
             layer(k)
+        pack(len(PIECES) - 1)
 
     tq, tz = "tq%d" % R, "tz%d" % R
     for k, (a, b) in enumerate(PIECES):

@@ -7,12 +7,12 @@ BIG = 1.0e29
 PADC = 256
 LOADS = ((0, 128), (256, 384), (128, 256))
 PIECES = ((0, 192), (192, 384))
-ON_VECTOR = ((0, 1), (0,))
-V_ON_SCALAR = (2, 3)
-STEPS = [([("cost", 0)] if s == 3 else []) + ([("carry", s - 1)] if s else []) + [("scan", s), ("sides", s)]
+STEPS = [([("carry", s - 1)] if s else []) + ([("cost", 0)] if s == 3 else []) + [("scan", s), ("sides", s)]
          + ([("across", s)] if s else []) for s in range(7)]
-LEFT = 6
-UNPACK = ({"sigma": (0, 1, 2), "counts": (3,)}, {"costs": (0, 1), "signs": (2,), "sigma": (3,)})
+UNPACK = ({"sigma": (0, 1, 2), "counts": (3,)}, {"costs": (0, 1), "sigma": (2, 3)})
+ORDER = """tau0 rows0 vo0 hk0 zz0 fp0 kw0 counts0 unpack0 lists0 tp0 vv1 va2 va0 va3 counts1
+           terms0 other0 signs0 passed0 qv0 lists1 sum0 signs1 h0 terms1 passed1 list0 other1
+           ea0 sum1 ev2 list1 ev3 ea1 ea5 ea6 ea7 out0 qe0 ev4 qe1"""
 F32, BF, I32, U16, MX, U8 = "float32", "bfloat16", "int32", "uint16", "float8_e4m3fn_x4", "uint8"
 
 SCRATCH = {}
@@ -26,7 +26,7 @@ def _sb(d, shape, names):
 _sb(BF, [4 * C], "xs ee xn")
 _sb(BF, [512], "us vs vt")
 _sb(BF, [516], "idt")
-_sb(BF, [256], "one m0 m1 ne0 ne1 sc0 sc1 sj0 sj1")
+_sb(BF, [258], "one m0 m1 ne0 ne1 sc0 sc1 sj0 sj1")
 _sb(BF, [160], "c12 fb fr")
 _sb(BF, [720], "fw0 fw1 fw2 fw3")
 _sb(MX, [128], "uq uq2 vq vtq via0 via1")
@@ -37,17 +37,19 @@ _sb(MX, [C], "eq8 tq0 tq1 tq2 hq0 hq1")
 _sb(U8, [C], "ez tz0 tz1 tz2 hz0 hz1")
 _sb(I32, [8], "p16 p7 ints")
 _sb(U16, [8], "ul l1 l3 vo")
-_sb(U16, [26], "cl eo")
+_sb(U16, [24], "cl eo")
 _sb(F32, [8], "fc cc cnt thr sg")
 _sb(F32, [12], "land0 land1 pm")
-_sb(F32, [26], "st")
+_sb(F32, [24], "st")
 _sb(F32, [32], "th0 th1 olb")
 _sb(F32, [36], "pw0 pw1 meet")
 _sb(F32, [64], "dm hk fh fp zz dg")
 _sb(F32, [72], "tp")
+_sb(F32, [78], "z1")
+_sb(F32, [90], "z0 zo")
 _sb(F32, [96], "row c16 cn cge pcr pc pb prow")
-_sb(F32, [160], "ck")
 _sb(F32, [128], "jp")
+_sb(F32, [160], "ck")
 _sb(F32, [168], "sx")
 _sb(F32, [192], "mw kw d1 hs")
 _sb(F32, [194], "d0")
@@ -366,20 +368,17 @@ def rank_program(g, core, T, topo):
     dma("A", A("us"), A("u"))
     for a, b in LOADS:
         dma("S", A("xs", s_[:, 4 * a:4 * b]), A("x", s_[:, 4 * a:4 * b]))
-    dma("S", A("wq", None, "u8"), A("wc"))
-    dma("S", A("wz"), A("ws"))
 
     iota(A("p16"), [[0, 8]], 0, 16, False)
     iota(A("jp"), [[1, 128]], 0, -1)
     iota(A("c16"), [[16, 24], [0, 4]], 0, 0)
     iota(A("row"), [[1, 96]], 0, 0)
-    iota(A("dm"), [[0, 4], [1, 16]], 0, 0)
     iota(A("lb", s_[:, :, 2:80:3]), [[0, 16], [1, 13]], -1, 0)
+    iota(A("dm"), [[0, 4], [1, 16]], 0, 0)
     JJ, S4, U2, Q4 = range(4)
     memset(A("one"), 1.0)
     memset(A("idt"), 0.0)
-    memset(A("mm", s_[:, :, 1:5:2]), BIG)
-    memset(A("mm", s_[:, :, 53:60:2]), BIG)
+    memset(col("vt", 256, 256), 0.0)
     ts(A("p7"), A("p16"), 127, Op.bitwise_and)
     for c, (sh, mask) in enumerate(((4, 15), (4, 3), (5, 1), (6, 3))):
         ts(col("ints", c), col("p16", 0), sh, Op.arith_shift_right, mask, Op.bitwise_and)
@@ -394,64 +393,79 @@ def rank_program(g, core, T, topo):
     ts(col("cc", A1), col("fc", S4), 3.0, Op.is_lt, 0.5, Op.mult)
     ts(col("cc", A2), col("fc", S4), 3.0, Op.is_lt)
     copy(A("uq2", None, "u32"), ind(A("uq", None, "u32"), A("ul")))
-    copy(A("uz2"), ind(A("uz"), A("ul")))
+
+    def beside(s, w):
+        acopy(A("lb", s_[:, s, 4 + 39 * w:40 + 39 * w:3]), A("lb", s_[:, s, 8 + 39 * w:42 + 39 * w:3]))
+
+    def behind(s, w, by):
+        by(A("lb", s_[:, s, 6 + 39 * w:42 + 39 * w:3]), A("lb", s_[:, s, 2 + 39 * w:38 + 39 * w:3]))
+
+    def across(s):
+        for w in range(min(s, 2)):
+            behind(s, w, copy)
 
     fill(A("tt", s_[:, :, 0:48:2]), 168, 0.0)
+    fill(A("mm", s_[:, :, 1:5:2]), 16, BIG)
+    fill(A("mm", s_[:, :, 53:60:2]), 32, BIG)
     fill(A("zl", s_[:, :, 0:36:3]), 84, 0.0)
+    const("z0", 0, 90, BIG)
+    const("z1", 0, 78, BIG)
+    const("zo", 78, 90, BIG)
     fill(A("lb", s_[:, :, 80]), 8, 0.0)
-    const("vt", 256, 512, 0.0)
-    for t in range(R):
-        const("land%d" % t, 1, 4, 0.0)
-    if hi - lo + 1 > len(blocks):
-        const("fb", 0, nrow, 1.0)
-    const("c12", 0, nrow, float(L if low else -L))
-    const("ck", 0, 160, 0.0)
-    const("tp", 0, 8, 0.0)
-    const("d0", 0, 1, 0.0)
-    for b in range(4):
-        const("fw%d" % b, cap, hb, 0.0)
     const("st", 2 * r, 2 * r + 2, 0.0)
     for a in range(4):
         const("st", 16, 18, float(slot(first + a, r)), 32 * a, 32 * a + 32)
-    lin(col("cc", JH), jj, 1.0, 0.5)
-    lin(col("cc", TQ), col("fc", Q4), 16.0, 0.5)
-    lin(col("cc", B3), col("fc", S4), 64.0, 31.0)
+    fill(A("z0", s_[:, 0:78:3]), 26, 0.0)
+    fill(A("z1", s_[:, 1:78:3]), 26, 0.0)
     if r > 0:
         lin(col("st", 0, 2 * r), A("c16", s_[:, 0:4 * r:2]), 0.0625, 4.0)
     if r + 1 < N:
         lin(col("st", 2 * r + 2, 14 - 2 * r), A("c16", s_[:, 4 * r + 4:32:2]), 0.0625, 3.0)
-    lin(A("cn"), A("c16"), 1.0, jj)
-    lin(A("cge"), A("c16"), 1.0, col("cc", JH))
-    lin(col("cc", B3), col("fc", U2), -63.0, col("cc", B3))
     for k, c in enumerate((places_at(r)[0], 19, places_at(r)[1])):
         lin(col("st", 18 + 2 * k, 2), col("row", 0, 2), 1.0, float(c - 8))
     lin(A("pcr"), col("row", 0, 96), float(L), float(wl - C))
+    for t in range(R):
+        const("land%d" % t, 1, 4, 0.0)
+    lin(col("cc", JH), jj, 1.0, 0.5)
+    lin(col("cc", TQ), col("fc", Q4), 16.0, 0.5)
+    lin(col("cc", B3), col("fc", S4), 64.0, 31.0)
     lin(col("cc", JK), jj, -1.0, float(L - 1 + 16 * L - wl + hb))
     lin(A("hk"), col("row", 0, 64), 1.0, float(hb))
+    acopy(A("uz2"), ind(A("uz"), A("ul")))
+    for w in range(2):
+        beside(w, w)
+        behind(w, w, acopy)
+    lin(col("cc", B3), col("fc", U2), -63.0, col("cc", B3))
     lin(col("thr", 0, 6), col("row", 0, 6), 64.0, col("cc", TQ))
-    fill(A("cn", s_[:, 3:96:4]), 24, 0.0)
-    fill(A("cge", s_[:, 3:96:4]), 24, -1.0e9)
-    lin(A("ck", s_[:, 0:96:4]), A("c16", s_[:, 0:96:4]), -1.0, col("cc", JK))
+    const("c12", 0, nrow, float(L if low else -L))
+    if hi - lo + 1 > len(blocks):
+        const("fb", 0, nrow, 1.0)
+
+    def tile_constants(s):
+        if s == 5:
+            for b in range(4):
+                const("fw%d" % b, cap, hb, 0.0)
+            const("tp", 0, 8, 0.0)
+            const("d0", 0, 1, 0.0)
+        if s == 6:
+            lin(A("cn"), A("c16"), 1.0, jj)
+            lin(A("cge"), A("c16"), 1.0, col("cc", JH))
+            const("ck", 0, 160, 0.0)
+        if s == 7:
+            fill(A("cn", s_[:, 3:96:4]), 24, 0.0)
+            fill(A("cge", s_[:, 3:96:4]), 24, -1.0e9)
+            lin(A("ck", s_[:, 0:96:4]), A("c16", s_[:, 0:96:4]), -1.0, col("cc", JK))
 
     def rank_constants(h, b):
-        iota(A("th%d" % h), [[0, 32]], 2 * S * b - N * S + 1, 2)
-        select(A("m%d" % h), A("one"), [[1, 256]], Op.not_equal, -1.0, -S * b, -1)
-    rank_constants(0, first)
+        iota(col("ne%d" % h, 256), [[0, 1]], N * S - 1 - 2 * S * b, -2)
+        select(A("m%d" % h), A("one"), [[1, 258]], Op.not_equal, -1.0, -S * b, -1)
 
     def late_constants():
         ts(A("pcr"), A("pcr"), 0.0, Op.max, float(cap + L), Op.min)
         ts(col("cc", B1), col("fc", S4), 39.0, Op.add, col("cc", A2), Op.mult)
         ts(A("dm"), A("dm"), jj, Op.is_equal, BIG, Op.mult)
-        copy(col("cl", 0, 24), col("st", 0, 24))
+        copy(A("cl"), A("st"))
         transp(A("pc"), A("pcr"))
-
-    def beside(s):
-        acopy(A("lb", s_[:, s, 4:79:3]), A("lb", s_[:, s, 8:81:3]))
-
-    def across(s):
-        copy(A("lb", s_[:, s, 6:79:3]), A("lb", s_[:, s, 2:77:3]))
-    beside(0)
-    acopy(A("lb", s_[:, 0, 6:79:3]), A("lb", s_[:, 0, 2:77:3]))
 
     for a, b in LOADS:
         quant_run("tq0", "tz0", "xs", a, b)
@@ -469,62 +483,81 @@ def rank_program(g, core, T, topo):
                                 for h, a, es in mine])
         if t == 0:
             late_constants()
-            if extra:
-                rank_constants(1, extra[0])
+            for h, b in enumerate([first] + extra):
+                rank_constants(h, b)
         for i in range(L):
             transp(A("et", s_[:, i, :]), A("ps0", s_[:, i:C:L]))
 
         def own(k):
             b, a = k // 2, k % 2 * (C // 2)
             acopy(col("fw%d" % b, wl + a, C // 2), col("ps%d" % (4 + b), a, C // 2))
-        for k in range(3):
+        for k in range(2):
             own(k)
-        act(A("mm", s_[:, 0, 5:53:2]), A("et", s_[:, :, 0:8:7]), Act.Abs)
+        act(A("z0", s_[:, 7:78:3]), A("et", s_[:, :, 0:8:7]), Act.Abs)
+        act(A("z0", s_[:, 14:78:3]), A("et", s_[:, 0:11, 0:8:7]), Act.Abs)
+        act(A("z1", s_[:, 0:70:3]), A("et", s_[:, :, 0:8:7]), Act.Abs)
+        act(A("z1", s_[:, 8:78:3]), A("et", s_[:, :, 1:7:5]), Act.Abs)
+
+        def m_at(s, j, n, lanes):
+            if s < 2:
+                a = 6 * j + 7 + s
+                return A("zo" if s else "z0", s_[:, a:a + 6 * n - (2 if lanes == 2 else 5):6 // lanes])
+            return A("mm", s_[:, s, 4 * j + 5:4 * j + 4 * n + (4 if lanes == 2 else 2):4 // lanes])
 
         def sides(s):
-            tt(A("zl", s_[:, s, 1:36:3]), A("mm", s_[:, s, 9:54:4]), A("tt", s_[:, s, 1:46:4]), Op.is_lt)
-            tt(A("zl", s_[:, s, 2:36:3]), A("tt", s_[:, s, 5:50:4]), A("mm", s_[:, s, 1:46:4]), Op.is_lt)
+            tt(A("zl", s_[:, s, 1:36:3]), m_at(s, 1, 12, 1), A("tt", s_[:, s, 1:46:4]), Op.is_lt)
+            tt(A("zl", s_[:, s, 2:36:3]), A("tt", s_[:, s, 5:50:4]), m_at(s, -1, 12, 1), Op.is_lt)
 
         def carry(s):
             for w in range(min(s + 1, 2)):
                 p = 32 * ((s - w) // 2 + 1)
                 scan(A("lb", s_[0:p, s + 1, 3 + 39 * w:39 + 39 * w]), A("zl", s_[0:p, s, :]),
                      A("lb", s_[0:p, s, 4 + 39 * w:40 + 39 * w]), 0.0, Op.mult, Op.max)
-            if s < 6:
-                beside(s + 1)
+                if s < 6:
+                    beside(s + 1, w)
+
+        def step_scan(s):
+            if s == 0:
+                scan(col("zo", 0, 78), col("z0", 0, 78), A("z1"), 0.0, Op.min, Op.max)
+            else:
+                scan(A("mm", s_[:, s + 1, 4:52]), A("tt", s_[:, s, 0:48]), A("mm", s_[:, s, 9:57]), 0.0, Op.min, Op.max)
+
+        def cost(s):
+            red(col(land, 0), A("meet"), Op.min)
+            send("cost%d" % t, [(shared_engines(r, others), col(land, 0),
+                                 [(T.cores[o], col(land, slot(r, o))) for o in others])])
         for s in range(7):
             if s == 3:
                 tt(col("meet", 0, 24), A("mm", s_[:, 3, 5:53:2]), A("mm", s_[:, 3, 7:55:2]), Op.max)
                 tt(col("meet", 24, 12), A("mm", s_[:, 3, 5:53:4]), A("mm", s_[:, 3, 11:59:4]), Op.max)
-            tt(A("tt", s_[:, s, 1:56:2]), A("mm", s_[:, s, 1:56:2]), A("mm", s_[:, s, 5:60:2]), Op.min)
-            far = 6 - s if s < 3 else s + 9
-            act(A("mm", s_[:, s, 10:58:2]), A("et", s_[:, :, s + 1:far + 1:far - s - 1]), Act.Abs)
+            tt(A("tt", s_[:, s, 1:56:2]), m_at(s, -1, 14, 2), m_at(s, 0, 14, 2), Op.min)
+            if s == 1:
+                acopy(A("mm", s_[:, 1, 5:53:2]), m_at(1, 0, 12, 2))
+            else:
+                k = max(s, 1)
+                far = 6 - k if k < 3 else k + 9
+                act(A("mm", s_[:, k, 10:58:2]), A("et", s_[:, :, k + 1:far + 1:far - k - 1]), Act.Abs)
             if s < 5:
-                own(3 + s)
+                own(2 + s)
+            elif t == 0:
+                tile_constants(s)
             for what, k in STEPS[s]:
-                if what == "scan":
-                    scan(A("mm", s_[:, s + 1, 4:52]), A("tt", s_[:, s, 0:48]), A("mm", s_[:, s, 9:57]), 0.0, Op.min, Op.max)
-                elif what == "cost":
-                    red(col(land, 0), A("meet"), Op.min)
-                    send("cost%d" % t, [(shared_engines(r, others), col(land, 0),
-                                         [(T.cores[o], col(land, slot(r, o))) for o in others])])
-                else:
-                    {"sides": sides, "carry": carry, "across": across}[what](k)
+                {"scan": step_scan, "cost": cost, "sides": sides, "carry": carry, "across": across}[what](k)
         ts(col("pm", 0, 12), A("mm", s_[:, 7, 5:53:4]), col(land, 0), Op.is_gt)
-        for k in range(LEFT, 7):
-            carry(k)
-            if k < 6:
-                across(k + 1)
+        carry(6)
+        own(7)
         back = A("pm", s_[:, 11::-1])
         scan(col(pw, 8, 12), back, A("lb", s_[:, 7, 38:4:-3]), 0.0, Op.mult, Op.max)
         scan(A(pw, s_[:, 31:19:-1]), back, A("lb", s_[:, 7, 77:43:-3]), 0.0, Op.mult, Op.max)
         at = {o: places_at(o)[1 if o < r else 0] for o in neighbours(r)}
         send_pair("place%d" % t, {o: (col(pw, 19, 2), col(pw, at[o], 2)) for o in neighbours(r)})
-        if t == 0 and hend > PADC:
-            for k in range(R):
-                quant(col("hq%d" % k, PADC, 128), col("hz%d" % k, PADC, 128), col("xs", 0, 512))
-        if t == R - 1:
-            quant(A("vq"), A("vz"), A("vs"))
+        if t == 0:
+            tile_constants(7)
+            if hend > PADC:
+                for k in range(R):
+                    quant(col("hq%d" % k, PADC, 128), col("hz%d" % k, PADC, 128), col("xs", 0, 512))
+            dma("S", A("wq", None, "u8"), A("wc"), col(pw, 19, 2))
+            dma("S", A("wz"), A("ws"))
         arrival("halo%d" % t, sum(2 * len(topo.engines(h, core)) for o in neighbours(r)
                                   for h, x, k, es in relays(T, topo, o) if x == r), [A(hq, s_[:, h0:PADC]), A(hz, s_[:, h0:PADC])])
         for b in range(4):
@@ -539,28 +572,33 @@ def rank_program(g, core, T, topo):
         unpack("costs")
         arrival("cost%d" % t, sum(len(shared_engines(o, [x for x in range(N) if x != o])) for o in others),
                 [col(land, 4, 7)])
-        (acopy if extra else copy)(col("cg", 0, 128), ind(col(land, 0, 11), col("cl", 0, 8)))
-        acopy(col("cg", 128, 128), ind(col(land, 0, 11), col("cl", 8, 8)))
+        for k in range(4):
+            (acopy if k % 2 else copy)(col("cg", 64 * k, 64), ind(col(land, 0, 11), col("cl", 4 * k, 4)))
         copy(col("cg", 256, 16), ind(col(land, 0, 11), col("cl", 16, 1)))
-        transp(col("ct", 0, 128), col("cg", 0, 128))
-        transp(col("ct", 128, 128), col("cg", 128, 128))
+        for k in range(4):
+            transp(col("ct", 64 * k, 64), col("cg", 64 * k, 64))
         sel = [col("cg", 256)] + [col("cg", S * b) for b in extra]
         for h in range(nh):
-            ts(A("ne%d" % h), A("ct"), sel[h], Op.not_equal, -1.0, Op.mult)
-            act(A("sj%d" % h), A("ct"), Act.Sign, sel[h], -1.0, col("sg", h))
+            for k in range(2):
+                ts(col("ne%d" % h, 128 * k, 128), col("ct", 128 * k, 128), sel[h], Op.not_equal, -1.0, Op.mult)
+                act(col("sj%d" % h, 128 * k, 128), col("ct", 128 * k, 128), Act.Sign, sel[h], -1.0, col("sg", 2 * h + k))
         for h in range(nh):
-            scan(A("sc%d" % h), A("m%d" % h), A("ne%d" % h), col("sg", h), Op.mult, Op.add)
-        unpack("signs")
+            const("th%d" % h, 0, 32, col("sg", 2 * h + 1))
+        for h in range(nh):
+            scan(col("sc%d" % h, 0, 257), col("m%d" % h, 0, 257), col("ne%d" % h, 0, 257), col("sg", 2 * h), Op.mult, Op.add)
         for b in sorted(blocks, key=lambda b: b in extra):
             h, a = (1, 0) if b in extra else (0, b - first)
             act(A("fb", s_[0:32, S * (b - lo):S * (b - lo) + S]), A("th%d" % h, s_[32 * a:32 * a + 32, :]), Act.Sign,
-                A("sc%d" % h, s_[32 * a:32 * a + 32, 255:256]), -1.0)
+                A("sc%d" % h, s_[32 * a:32 * a + 32, 256:257]), -1.0)
         unpack("sigma")
         arrival("place%d" % t, sum(share(o) for o in neighbours(r)), [A(pw, s_[:, 32:pend])])
         tt(A("pb"), ind(col(pw, 8, pend - 8), col("cl", 18, 6)), A("pc"), Op.add)
+        if t == R - 1:
+            quant(A("vq"), A("vz"), A("vs"))
+        transp(A("prow"), A("pb"))
         for a in range(4):
             transp(A("fr", s_[32 * a:32 * a + 32, 0:nrow]), A("fb", s_[0:32, 0:nrow]))
-        transp(A("prow"), A("pb"))
+        scan(A("dg"), A("dm"), col("prow", 16, 64), BIG, Op.add, Op.min)
         if low:
             scan(col("sx", 1, win + 63), col("c12", 0, win + 63), col("fr", 0, win + 63), float(-C * r + (L - 1) * S * lo),
                  Op.add, Op.subtract)
@@ -569,59 +607,78 @@ def rank_program(g, core, T, topo):
             scan(A("sx", down), A("c12", down), A("fr", down), float(C * (N - r) + (L - 1) * S * (hi - N + 1)),
                  Op.add, Op.add)
         start, sig = col("sx", win, 64), col("fr", win, 64)
-        lin(A("fh"), sig, -0.25, 0.75 + 16 * L - wl + L)
-        lin(col("mw", 0, 64), sig, -1.0, 0.0)
-        lin(col("kw", 64, 63), col("fr", win, 63), -1.0, 0.0)
-        acopy(col("mw", 127, 64), sig)
-        vo = col("vo", 0, 4)
-        for n in range(6):
-            act(A("cmp", s_[:, n, :]), start, Act.Sign, col("thr", n), -1.0, col("cnt", n))
-        scan(A("dg"), A("dm"), col("prow", 16, 64), BIG, Op.add, Op.min)
-        tt(col("mw", 64, 63), col("fr", win, 63), col("fr", win + 1, 63), Op.mult)
         before, sigb = col("sx", win - 1), col("fr", win - 1, 64)
-        scan(A("fp"), col("ck", 96, 64), sigb, before, Op.add, Op.subtract)
-        copy(vo, A("dg", s_[:, 15:64:16]))
-        tt(col("kw", 127, 64), sig, A("hk"), Op.mult)
-        tt(A("zz"), A("fp"), A("fh"), Op.add)
-        scan(col("kw", 0, 64), col("one", 0, 64), sigb, before, Op.add, Op.subtract)
-        unpack("counts")
-
-        def seam_parts(b):
-            (acopy if b in V_ON_SCALAR else copy)(A("vt", s_[:, b:256:4]), ind(col("fw%d" % b, 0, hb), vo))
-        seam_parts(0)
-        tt(col("tp", 8, 64), A("zz"), col("prow", 16, 64), Op.add)
-        l1, l3 = col("l1", 0, 6), col("l3", 0, 6)
-        ts(l3, col("cnt", 0, 6), 0.5, Op.mult, col("cc", B3), Op.add)
-        ts(l1, col("cnt", 0, 6), col("cc", A1), Op.mult, col("cc", B1), Op.add)
-        for b in range(1, 4):
-            seam_parts(b)
-        acopy(A("d0", s_[:, 1:192:2]), ind(col("mw", 0, 191), l3))
-        tt(A("d1", s_[:, 0:192:2]), ind(col("kw", 0, 191), l3), A("ck", s_[:, 0:96]), Op.add)
-        tt(A("d1", s_[:, 1:192:2]), ind(A("tp"), l1), A("cge"), Op.is_le)
-        quant(A("vtq"), A("vtz"), A("vt"))
-        tt(A("d0", s_[:, 2:194:2]), ind(A("tp"), l1), A("cn"), Op.not_equal)
-        for b in range(4):
-            mm(4 + b, "wq", "wz", 128 * b, "vtq", "vtz", 0, 128)
-        for b in range(4):
-            act(col("fw%d" % b, hb, 64), col("ps%d" % (4 + b), 0, 64), Act.Relu, None, 0.03125)
-        scan(A("hs"), col("d0", 0, 192), A("d1"), 0.0, Op.mult, Op.add)
-        copy(col("eo", 0, 24), A("hs", s_[:, 7:192:8]))
-        if t == 0:
-            dma("S", A("vs"), A("v"), A("eo"))
-        if t == R - 1:
-            ts(A("olb"), col("prow", 32, 32), float(-wl), Op.add)
-            dma("S", A("ol"), A("olb", s_[0:128:16, :]))
+        vo = col("vo", 0, 4)
         nq, nz = "tq%d" % (t + 1), "tz%d" % (t + 1)
 
-        def gather(k):
-            a, b = PIECES[k]
-            for e in range(4):
-                (copy if e in ON_VECTOR[k] else acopy)(A("ee", s_[:, 4 * a + e:4 * b:4]),
-                                                       ind(col("fw%d" % e, 0, hb + 64), A("eo", s_[:, a // 16:b // 16])))
-            quant_run("eq8", "ez", "ee", a, b)
+        def rows(k):
+            lin(A("fh"), sig, -0.25, 0.75 + 16 * L - wl + L)
+            lin(col("mw", 0, 64), sig, -1.0, 0.0)
+            lin(col("kw", 64, 63), col("fr", win, 63), -1.0, 0.0)
+            acopy(col("mw", 127, 64), sig)
 
-        def layer(k):
+        def counts(k):
+            for n in range(3 * k, 3 * k + 3):
+                act(A("cmp", s_[:, n, :]), start, Act.Sign, col("thr", n), -1.0, col("cnt", n))
+
+        def lists(k):
+            ts(col("l3", 4 * k, 3), col("cnt", 3 * k, 3), 0.5, Op.mult, col("cc", B3), Op.add)
+            ts(col("l1", 4 * k, 3), col("cnt", 3 * k, 3), col("cc", A1), Op.mult, col("cc", B1), Op.add)
+
+        def seam_parts(b, by):
+            by(A("vt", s_[:, b:256:4]), ind(col("fw%d" % b, 0, hb), vo))
+
+        def layer_of_seams(k):
+            quant(A("vtq"), A("vtz"), A("vt"))
+            for b in range(4):
+                mm(4 + b, "wq", "wz", 128 * b, "vtq", "vtz", 0, 128)
+
+        def seams_made(k):
+            for b in range(4):
+                act(col("fw%d" % b, hb, 64), col("ps%d" % (4 + b), 0, 64), Act.Relu, None, 0.03125)
+
+        def beside_the_tile(k):
+            if t == 0:
+                dma("S", A("vs"), A("v"), col("eo", 0, 12))
+            if t == R - 1:
+                ts(A("olb"), col("prow", 32, 32), float(-wl), Op.add)
+                dma("S", A("ol"), A("olb", s_[0:128:16, :]))
+
+        def part(k, e, by):
             a, b = PIECES[k]
+            by(A("ee", s_[:, 4 * a + e:4 * b:4]), ind(col("fw%d" % e, 0, hb + 64), A("eo", s_[:, a // 16:b // 16])))
+
+        def second(name, k, at):
+            return A(name, s_[:, 96 * k + at:96 * k + at + 95:2])
+        step = {
+            "rows": rows, "counts": counts, "lists": lists, "qv": layer_of_seams, "h": seams_made, "out": beside_the_tile,
+            "unpack": lambda k: unpack("counts"),
+            "vo": lambda k: copy(vo, A("dg", s_[:, 15:64:16])),
+            "tau": lambda k: tt(col("mw", 64, 63), col("fr", win, 63), col("fr", win + 1, 63), Op.mult),
+            "zz": lambda k: tt(A("zz"), col("prow", 16, 64), A("fh"), Op.add),
+            "fp": lambda k: scan(A("fp"), col("ck", 96, 64), sigb, before, Op.add, Op.subtract),
+            "kw": lambda k: scan(col("kw", 0, 64), col("one", 0, 64), sigb, before, Op.add, Op.subtract),
+            "hk": lambda k: tt(col("kw", 127, 64), sig, A("hk"), Op.mult),
+            "tp": lambda k: tt(col("tp", 8, 64), A("zz"), A("fp"), Op.add),
+            "vv": lambda k: seam_parts(k, copy), "va": lambda k: seam_parts(k, acopy),
+            "signs": lambda k: acopy(second("d0", k, 1), ind(col("mw", 0, 191), col("l3", 4 * k, 3))),
+            "terms": lambda k: tt(second("d1", k, 0), ind(col("kw", 0, 191), col("l3", 4 * k, 3)), col("ck", 48 * k, 48), Op.add),
+            "passed": lambda k: tt(second("d1", k, 1), ind(A("tp"), col("l1", 4 * k, 3)), col("cge", 48 * k, 48), Op.is_le),
+            "other": lambda k: tt(second("d0", k, 2), ind(A("tp"), col("l1", 4 * k, 3)), col("cn", 48 * k, 48), Op.not_equal),
+            "sum": lambda k: scan(col("hs", 96 * k, 96), col("d0", 96 * k, 96), col("d1", 96 * k, 96), 0.0, Op.mult, Op.add),
+            "list": lambda k: copy(col("eo", 12 * k, 12), A("hs", s_[:, 96 * k + 7:96 * k + 96:8])),
+            "ev": lambda k: part(k // 4, k % 4, copy), "ea": lambda k: part(k // 4, k % 4, acopy),
+            "qe": lambda k: quant_run("eq8", "ez", "ee", *PIECES[k]),
+        }
+        for name in ORDER.split():
+            step[name[:-1]](int(name[-1]))
+
+        def pack(k):
+            a, b = PIECES[k]
+            quant_run(nq, nz, "xn", a, b)
+            if t == R - 1:
+                dma("S", A("oc", s_[:, 4 * a:4 * b]), A(nq, s_[:, a:b], "u8"))
+        for k, (a, b) in enumerate(PIECES):
             for e in range(5):
                 if e < 4:
                     mm(e, "wq", "wz", 128 * e, "eq8", "ez", a, b)
@@ -631,19 +688,8 @@ def rank_program(g, core, T, topo):
                 rl = col("rl", C * e + a, b - a)
                 act(rl, col("ps%d" % e, 0, b - a), Act.Relu, None, 0.015625)
                 tt(A("xn", s_[:, 4 * a + e:4 * b:4]), col("ps%d" % (4 + e), 0, b - a), rl, Op.add)
-                if e == 0 and k > 0:
+                if k > 0 and e == (0 if t == R - 1 else 3):
                     pack(k - 1)
-
-        def pack(k):
-            a, b = PIECES[k]
-            quant_run(nq, nz, "xn", a, b)
-            if t == R - 1:
-                dma("S", A("oc", s_[:, 4 * a:4 * b]), A(nq, s_[:, a:b], "u8"))
-        gather(0)
-        for k in range(len(PIECES)):
-            if k + 1 < len(PIECES):
-                gather(k + 1)
-            layer(k)
         pack(len(PIECES) - 1)
 
     tq, tz = "tq%d" % R, "tz%d" % R

import numpy as np
from concourse.bass import DstId, RemoteDMATransfer
from concourse.mybir import dt, AluOpType, AxisListType, ActivationFunctionType

N, C, S, L, R = 8, 384, 32, 12, 2
BIG = 1.0e29
PADC = 256
LOADS = ((0, 128), (256, 384), (128, 256))
PIECES = ((0, 192), (192, 384))
STEPS = [([("carry", s - 1)] if s else []) + ([("cost", 0)] if s == 3 else []) + [("scan", s), ("sides", s)]
         + ([("across", s)] if s else []) for s in range(7)]
UNPACK = ({"sigma": (0, 1, 2), "counts": (3,)}, {"costs": (0, 1), "sigma": (2, 3)})
ORDER = """tau0 rows0 vo0 hk0 zz0 fp0 kw0 counts0 unpack0 lists0 tp0 vv1 va2 va0 va3 counts1
           terms0 other0 signs0 passed0 qv0 lists1 sum0 signs1 h0 terms1 passed1 list0 other1
           ea0 sum1 ev2 list1 ev3 ea1 ea5 ea6 ea7 out0 qe0 ev4 qe1"""
F32, BF, I32, U16, MX, U8 = "float32", "bfloat16", "int32", "uint16", "float8_e4m3fn_x4", "uint8"

SCRATCH = {}


def _sb(d, shape, names):
    for n in names.split():
        SCRATCH[n] = ("sbuf", [128] + shape, d)


_sb(BF, [4 * C], "xs ee xn")
_sb(BF, [512], "us vs vt")
_sb(BF, [516], "idt")
_sb(BF, [258], "one m0 m1 ne0 ne1 sc0 sc1 sj0 sj1")
_sb(BF, [160], "c12 fb fr")
_sb(BF, [720], "fw0 fw1 fw2 fw3")
_sb(MX, [128], "uq uq2 vq vtq via0 via1")
_sb(U8, [128], "uz uz2 vz vtz viz0 viz1")
_sb(MX, [512], "wq idq")
_sb(U8, [512], "wz idz")
_sb(MX, [C], "eq8 tq0 tq1 tq2 hq0 hq1")
_sb(U8, [C], "ez tz0 tz1 tz2 hz0 hz1")
_sb(I32, [8], "p16 p7 ints")
_sb(U16, [8], "ul l1 l3 vo")
_sb(U16, [24], "cl eo")
_sb(F32, [8], "fc cc cnt thr sg")
_sb(F32, [12], "land0 land1 pm")
_sb(F32, [24], "st")
_sb(F32, [32], "th0 th1 olb")
_sb(F32, [36], "pw0 pw1 meet")
_sb(F32, [64], "dm hk fh fp zz dg")
_sb(F32, [72], "tp")
_sb(F32, [78], "z1")
_sb(F32, [90], "z0 zo")
_sb(F32, [96], "row c16 cn cge pcr pc pb prow")
_sb(F32, [128], "jp")
_sb(F32, [160], "ck")
_sb(F32, [168], "sx")
_sb(F32, [192], "mw kw d1 hs")
_sb(F32, [194], "d0")
_sb(F32, [256], "ct")
_sb(F32, [272], "cg")
_sb(F32, [C], "ys")
_sb(F32, [4 * C], "rl")
_sb(F32, [12, 32], "et")
_sb(F32, [8, 60], "mm")
_sb(F32, [7, 56], "tt")
_sb(F32, [7, 36], "zl")
_sb(F32, [8, 81], "lb")
_sb(F32, [6, 64], "cmp")
for _b in range(8):
    SCRATCH["ps%d" % _b] = ("psum", [128, 512], F32)

ROT = {"V": 48, "A": 32, "P": 16, "G": 12}
NDMA = 20
SEMAPHORES = (["%s%d" % (q.lower(), i) for q in "VAPG" for i in range(ROT[q])] + ["d%d" % i for i in range(NDMA)]
              + ["sent"] + ["%s%d" % (n, t) for n in ("plane", "halo", "cost", "place") for t in range(R)])


def from_left(b):
    if 2 * b <= N:
        return -(-S * b // (L + 1))
    return -(-S * (N - b) // (L - 1))


def sent_strips(r):
    return max(([from_left(r + 1)] if r + 1 < N else []) + ([from_left(N - r)] if r > 0 else []))


def halo_at(o):
    a = L * sent_strips(o - 1) if o > 0 else 0
    b = L * sent_strips(o + 1) if o + 1 < N else 0
    return PADC - a - b, PADC - b


def neighbours(a):
    return [o for o in (a - 1, a + 1) if 0 <= o < N]


def as_mask(engines):
    m = 0
    for e in engines:
        m |= 1 << e
    return m


def relays(T, topo, a):
    c = T.cores[a]
    free = [h for h in topo.cores_of(c) if T.rank_of(h) is None and topo.die(h) != topo.die(c)
            and all(topo.may_write(h, T.cores[x]) for x in neighbours(a))]
    jobs = [(o, k) for o in neighbours(a) for k in range(2)]
    es = topo.engines(c, free[0])
    n = len(es) // 2
    return [(free[i], o, k, es[n * k:n * k + n]) for i, (o, k) in enumerate(jobs)]


def hand_on(g, core, T, topo):
    for a in range(N):
        for h, o, k, es in relays(T, topo, a):
            if h == core:
                w = L * sent_strips(a) // 2
                at = halo_at(o)[1 if o < a else 0] + k * w
                rid, pid = topo.addr(T.cores[o], core)
                for t in range(R):
                    for sem, src, to in (
                            ("plane%d" % t, T["viz%d" % t][:, 0:w], T["hz%d" % t][:, at:at + w]),
                            ("halo%d" % t, T["via%d" % t][:, 0:w].bitcast(dt.uint8),
                             T["hq%d" % t][:, at:at + w].bitcast(dt.uint8))):
                        g.wait_ge(T.sem[sem], len(es))
                        g.remote_dma_fused([RemoteDMATransfer(
                            dst_ids=[DstId(rid=rid, pnc=pid)], dma_engine_mask=topo.mask(core, T.cores[o]),
                            remote_sem=T.sem["halo%d" % t], src=src, dst=to)], local_sem=T.sem.sent)
                g.wait_ge(T.sem.sent, 2 * R * len(topo.engines(core, T.cores[o])))


def rank_program(g, core, T, topo):
    r = T.rank_of(core)
    if r is None:
        return hand_on(g, core, T, topo)
    Op, Act = AluOpType, ActivationFunctionType
    ops = []
    s_ = np.s_

    def A(name, idx=None, mod=None):
        return (name, s_[:] if idx is None else idx, mod)

    def col(name, c, n=1):
        return A(name, s_[:, c:c + n])

    def ind(ap, off):
        return (ap[0], ap[1], ("ind", off, ap[2]))

    def real(ap):
        if not isinstance(ap, tuple):
            return ap
        v = T[ap[0]][ap[1]]
        mod = ap[2]
        if mod == "u8":
            return v.bitcast(dt.uint8)
        if mod == "u32":
            return v.bitcast(dt.uint32)
        if mod is not None:
            if mod[2] == "u32":
                v = v.bitcast(dt.uint32)
            return v.indirect(real(mod[1]))
        return v

    cache = {}

    def foot(ap):
        name, idx = ap[0], ap[1]
        if name not in SCRATCH:
            return []
        key = (name, str(idx))
        if key not in cache:
            where, shape, _d = SCRATCH[name]
            ix = idx if isinstance(idx, tuple) else (idx,)
            parts = range(128)[ix[0]]
            if where == "psum":
                cache[key] = (name, 0, 128, 1)
            else:
                free = np.arange(int(np.prod(shape[1:]))).reshape(shape[1:])[ix[1:]].reshape(-1)
                bits = 0
                for e in free.tolist():
                    bits |= 1 << e
                cache[key] = (name, parts[0], parts[-1] + 1, bits)
        out = [cache[key]]
        if ap[2] is not None and ap[2][0] == "ind":
            out += foot(ap[2][1])
        return out

    def rec(q, call, reads, writes, kind="c", sem=None, count=0):
        rd = [f for a in reads if isinstance(a, tuple) for f in foot(a)]
        wr = [f for a in writes for f in foot(a)]
        ops.append({"q": q, "call": call, "rd": rd, "wr": wr, "kind": kind, "sem": sem, "count": count})

    def meet(fa, fb):
        return any(a[0] == b[0] and a[1] < b[2] and b[1] < a[2] and a[3] & b[3] for a in fa for b in fb)

    def emit():
        eng = {"V": g.vector, "A": g.scalar, "P": g.tensor, "G": g, "S": g.sync}
        known = {q: set() for q in eng}
        for i, o in enumerate(ops):
            o["waits"], o["used"] = [], False
            if o["kind"] == "arrival":
                o["known"] = set()
                continue
            need = []
            banks = [f for f in o["rd"] if SCRATCH[f[0]][0] == "psum"]
            for j in range(i - 1, -1, -1):
                p = ops[j]
                if j in known[o["q"]] or p["kind"] == "remote":
                    continue
                if (meet(o["rd"], p["wr"]) or meet(o["wr"], p["wr"]) or meet(o["wr"], p["rd"])
                        or (p["q"] != o["q"] and meet(banks, p["rd"]))):
                    need.append(j)
                    known[o["q"]].add(j)
                    known[o["q"]] |= p["known"]
            o["waits"] = need[::-1]
            for j in need:
                ops[j]["used"] = True
            o["known"] = set(known[o["q"]])
        turn = {q: 0 for q in ROT}
        nd = 0
        for o in ops:
            if o["kind"] == "dma":
                o["sem"], o["count"] = "d%d" % nd, 16
                nd += 1
            elif o["kind"] == "c" and o["used"]:
                n = turn[o["q"]]
                turn[o["q"]] += 1
                o["sem"], o["count"] = "%s%d" % (o["q"].lower(), n % ROT[o["q"]]), n // ROT[o["q"]] + 1
        sent = 0
        for o in ops:
            if o["kind"] == "arrival":
                continue
            e = eng[o["q"]]
            for j in o["waits"]:
                e.wait_ge(T.sem[ops[j]["sem"]], ops[j]["count"])
            ins = o["call"](e)
            if o["kind"] == "dma":
                ins.then_inc(T.sem[o["sem"]], 16)
            elif o["kind"] == "remote":
                sent += o["count"]
            elif o["used"]:
                ins.then_inc(T.sem[o["sem"]], 1)
        for o in ops:
            if o["kind"] == "dma" and not o["used"]:
                eng[o["q"]].wait_ge(T.sem[o["sem"]], 16)
        g.wait_ge(T.sem.sent, sent)

    def dma(q, out, in_, after=None):
        rec(q, lambda e: e.dma_start(real(out), real(in_)), [in_, after], [out], "dma")

    def memset(ap, c):
        rec("V", lambda e: e.memset(real(ap), c), [], [ap])

    def copy(out, in_):
        rec("V", lambda e: e.tensor_copy(real(out), real(in_)), [in_], [out])

    def tt(out, a, b, op):
        rec("V", lambda e: e.tensor_tensor(real(out), real(a), real(b), op), [a, b], [out])

    def ts(out, a, s1, op0, s2=None, op1=None):
        if op1 is None:
            rec("V", lambda e: e.tensor_scalar(real(out), real(a), real(s1), None, op0), [a, s1], [out])
        else:
            rec("V", lambda e: e.tensor_scalar(real(out), real(a), real(s1), real(s2), op0, op1), [a, s1, s2], [out])

    def red(out, a, op):
        rec("V", lambda e: e.tensor_reduce(real(out), real(a), AxisListType.X, op), [a], [out])

    def scan(out, d0, d1, init, op0, op1):
        rec("V", lambda e: e.tensor_tensor_scan(real(out), real(d0), real(d1), real(init), op0, op1), [d0, d1, init], [out])

    def transp(out, a):
        rec("V", lambda e: e.transpose(real(out), real(a)), [a], [out])

    def quant(q, z, a):
        rec("V", lambda e: e.quantize_mx(real(q), real(z), real(a)), [a], [q, z])

    def quant_run(q, z, tile, a, b):
        quant(A(q, s_[:, a:b]), A(z, s_[:, a:b]), A(tile, s_[:, 4 * a:4 * b]))

    def act(out, a, func, bias=None, scale=None, accum=None):
        def call(e):
            kw = {}
            if bias is not None:
                kw["bias"] = real(bias)
            if scale is not None:
                kw["scale"] = scale
            if accum is not None:
                kw["accum_out"] = real(accum)
            return e.activation(real(out), real(a), func, **kw)
        rec("A", call, [a, bias], [out] + ([accum] if accum is not None else []))

    def acopy(out, a):
        act(out, a, Act.Copy)

    def lin(out, a, scale, bias):
        act(out, a, Act.Identity, bias, scale)

    def fill(out, n, c, p0=0, p1=128):
        lin(out, A("one", s_[p0:p1, 0:n]), 0.0, c)

    def const(name, a, b, c, p0=0, p1=128):
        fill(A(name, s_[p0:p1, a:b]), b - a, c, p0, p1)

    def mm(bank, lq, lz, lo, rq, rz, a, b):
        out = A("ps%d" % bank, s_[:, 0:b - a])
        l, ls = A(lq, s_[:, lo:lo + 128]), A(lz, s_[:, lo:lo + 128])
        m, ms = A(rq, s_[:, a:b]), A(rz, s_[:, a:b])
        rec("P", lambda e: e.matmul_mx(real(out), real(l), real(ls), real(m), real(ms), True, True), [l, ls, m, ms], [out])

    def iota(out, pattern, base, cm, small=True):
        if small:
            rec("G", lambda e: e.iota(real(out), pattern, base, cm, allow_small_or_imprecise_dtypes=True), [], [out])
        else:
            rec("G", lambda e: e.iota(real(out), pattern, base, cm), [], [out])

    def select(out, a, pattern, op, c, base, cm):
        rec("G", lambda e: e.affine_select(real(out), real(a), pattern, op, c, base, cm), [a], [out])

    def dst(to):
        rid, pid = topo.addr(to, core)
        return DstId(rid=rid, pnc=pid)

    def shared_engines(a, others):
        return [e for e in topo.engines(T.cores[a], T.cores[others[0]])
                if all(e in topo.engines(T.cores[a], T.cores[o]) for o in others)]

    def share(a):
        return len(shared_engines(a, neighbours(a))) // len(neighbours(a))

    def send(sem, transfers):
        rec("G", lambda e: e.remote_dma_fused(
            [RemoteDMATransfer(dst_ids=[dst(c) for c, d in to], dma_engine_mask=as_mask(es), remote_sem=T.sem[sem],
                               src=real(src), dsts=[real(d) for c, d in to]) for es, src, to in transfers],
            local_sem=T.sem.sent), [src for es, src, to in transfers], [], "remote", None,
            sum(len(es) for es, src, to in transfers))

    def send_pair(sem, pieces):
        es, n = shared_engines(r, neighbours(r)), share(r)
        send(sem, [(es[n * k:n * k + n], pieces[o][0], [(T.cores[o], pieces[o][1])]) for k, o in enumerate(neighbours(r))])

    def arrival(sem, count, writes):
        rec("R", None, [], writes, "arrival", sem, count)

    others = sorted((o for o in range(N) if o != r), key=lambda o: abs(2 * o - N + 1))
    wl = L * sent_strips(r - 1) if r > 0 else 0
    wr = L * sent_strips(r + 1) if r + 1 < N else 0
    ws_ = L * sent_strips(r)
    cap = wl + C + wr
    hb = cap + 2 * L

    def places_at(o):
        return (32 if o > 0 else 19), (19 if o + 1 == N else 34 if o > 0 else 32)
    h0 = halo_at(r)[0]
    hend = max(PADC, h0 + 128)
    pend = 32 + 2 * len(neighbours(r))
    low = 2 * r < N
    lo, hi = (min(0, r - 1), r + 1) if low else (r - 1, max(N - 1, r + 1))
    first = 0 if low else 4
    blocks = list(range(max(lo, 0), min(hi, N - 1) + 1))
    extra = [b for b in blocks if not first <= b < first + 4]
    nh = 1 + len(extra)
    nrow = S * (hi - lo + 1)
    win = S * (r - lo) - 16

    def slot(o, at):
        return 0 if o == at else 4 + o - (1 if o > at else 0)

    dma("A", A("us"), A("u"))
    for a, b in LOADS:
        dma("S", A("xs", s_[:, 4 * a:4 * b]), A("x", s_[:, 4 * a:4 * b]))

    iota(A("p16"), [[0, 8]], 0, 16, False)
    iota(A("jp"), [[1, 128]], 0, -1)
    iota(A("c16"), [[16, 24], [0, 4]], 0, 0)
    iota(A("row"), [[1, 96]], 0, 0)
    iota(A("lb", s_[:, :, 2:80:3]), [[0, 16], [1, 13]], -1, 0)
    iota(A("dm"), [[0, 4], [1, 16]], 0, 0)
    JJ, S4, U2, Q4 = range(4)
    memset(A("one"), 1.0)
    memset(A("idt"), 0.0)
    memset(col("vt", 256, 256), 0.0)
    ts(A("p7"), A("p16"), 127, Op.bitwise_and)
    for c, (sh, mask) in enumerate(((4, 15), (4, 3), (5, 1), (6, 3))):
        ts(col("ints", c), col("p16", 0), sh, Op.arith_shift_right, mask, Op.bitwise_and)
    copy(A("ul"), A("p7"))
    ts(A("idt", s_[:, 3:515:4]), A("jp"), 0.0, Op.is_equal)
    copy(col("fc", 0, 4), col("ints", 0, 4))
    for b in range(4):
        quant(col("idq", 128 * b, 128), col("idz", 128 * b, 128), col("idt", 3 - b, 512))
    quant(A("uq"), A("uz"), A("us"))
    jj = col("fc", JJ)
    A1, A2, B1, B3, JH, TQ, JK = range(7)
    ts(col("cc", A1), col("fc", S4), 3.0, Op.is_lt, 0.5, Op.mult)
    ts(col("cc", A2), col("fc", S4), 3.0, Op.is_lt)
    copy(A("uq2", None, "u32"), ind(A("uq", None, "u32"), A("ul")))

    def beside(s, w):
        acopy(A("lb", s_[:, s, 4 + 39 * w:40 + 39 * w:3]), A("lb", s_[:, s, 8 + 39 * w:42 + 39 * w:3]))

    def behind(s, w, by):
        by(A("lb", s_[:, s, 6 + 39 * w:42 + 39 * w:3]), A("lb", s_[:, s, 2 + 39 * w:38 + 39 * w:3]))

    def across(s):
        for w in range(min(s, 2)):
            behind(s, w, copy)

    fill(A("tt", s_[:, :, 0:48:2]), 168, 0.0)
    fill(A("mm", s_[:, :, 1:5:2]), 16, BIG)
    fill(A("mm", s_[:, :, 53:60:2]), 32, BIG)
    fill(A("zl", s_[:, :, 0:36:3]), 84, 0.0)
    const("z0", 0, 90, BIG)
    const("z1", 0, 78, BIG)
    const("zo", 78, 90, BIG)
    fill(A("lb", s_[:, :, 80]), 8, 0.0)
    const("st", 2 * r, 2 * r + 2, 0.0)
    for a in range(4):
        const("st", 16, 18, float(slot(first + a, r)), 32 * a, 32 * a + 32)
    fill(A("z0", s_[:, 0:78:3]), 26, 0.0)
    fill(A("z1", s_[:, 1:78:3]), 26, 0.0)
    if r > 0:
        lin(col("st", 0, 2 * r), A("c16", s_[:, 0:4 * r:2]), 0.0625, 4.0)
    if r + 1 < N:
        lin(col("st", 2 * r + 2, 14 - 2 * r), A("c16", s_[:, 4 * r + 4:32:2]), 0.0625, 3.0)
    for k, c in enumerate((places_at(r)[0], 19, places_at(r)[1])):
        lin(col("st", 18 + 2 * k, 2), col("row", 0, 2), 1.0, float(c - 8))
    lin(A("pcr"), col("row", 0, 96), float(L), float(wl - C))
    for t in range(R):
        const("land%d" % t, 1, 4, 0.0)
    lin(col("cc", JH), jj, 1.0, 0.5)
    lin(col("cc", TQ), col("fc", Q4), 16.0, 0.5)
    lin(col("cc", B3), col("fc", S4), 64.0, 31.0)
    lin(col("cc", JK), jj, -1.0, float(L - 1 + 16 * L - wl + hb))
    lin(A("hk"), col("row", 0, 64), 1.0, float(hb))
    acopy(A("uz2"), ind(A("uz"), A("ul")))
    for w in range(2):
        beside(w, w)
        behind(w, w, acopy)
    lin(col("cc", B3), col("fc", U2), -63.0, col("cc", B3))
    lin(col("thr", 0, 6), col("row", 0, 6), 64.0, col("cc", TQ))
    const("c12", 0, nrow, float(L if low else -L))
    if hi - lo + 1 > len(blocks):
        const("fb", 0, nrow, 1.0)

    def tile_constants(s):
        if s == 5:
            for b in range(4):
                const("fw%d" % b, cap, hb, 0.0)
            const("tp", 0, 8, 0.0)
            const("d0", 0, 1, 0.0)
        if s == 6:
            lin(A("cn"), A("c16"), 1.0, jj)
            lin(A("cge"), A("c16"), 1.0, col("cc", JH))
            const("ck", 0, 160, 0.0)
        if s == 7:
            fill(A("cn", s_[:, 3:96:4]), 24, 0.0)
            fill(A("cge", s_[:, 3:96:4]), 24, -1.0e9)
            lin(A("ck", s_[:, 0:96:4]), A("c16", s_[:, 0:96:4]), -1.0, col("cc", JK))

    def rank_constants(h, b):
        iota(col("ne%d" % h, 256), [[0, 1]], N * S - 1 - 2 * S * b, -2)
        select(A("m%d" % h), A("one"), [[1, 258]], Op.not_equal, -1.0, -S * b, -1)

    def late_constants():
        ts(A("pcr"), A("pcr"), 0.0, Op.max, float(cap + L), Op.min)
        ts(col("cc", B1), col("fc", S4), 39.0, Op.add, col("cc", A2), Op.mult)
        ts(A("dm"), A("dm"), jj, Op.is_equal, BIG, Op.mult)
        copy(A("cl"), A("st"))
        transp(A("pc"), A("pcr"))

    for a, b in LOADS:
        quant_run("tq0", "tz0", "xs", a, b)
    for t in range(R):
        tq, tz, hq, hz, land, pw = ("%s%d" % (n, t) for n in ("tq", "tz", "hq", "hz", "land", "pw"))
        mm(0, "uq2", "uz2", 0, tq, tz, 0, C)
        for b in range(4):
            mm(4 + b, "idq", "idz", 128 * b, tq, tz, 0, C)
        edge = {r - 1: 0, r + 1: C - ws_}
        half = ws_ // 2
        for x in neighbours(r):
            mine = [(h, edge[o] + k * half, es) for h, o, k, es in relays(T, topo, r) if o == x]
            send("plane%d" % t, [(es, col(tz, a, half), [(h, col("viz%d" % t, 0, half))]) for h, a, es in mine])
            send("halo%d" % t, [(es, A(tq, s_[:, a:a + half], "u8"), [(h, A("via%d" % t, s_[:, 0:half], "u8"))])
                                for h, a, es in mine])
        if t == 0:
            late_constants()
            for h, b in enumerate([first] + extra):
                rank_constants(h, b)
        for i in range(L):
            transp(A("et", s_[:, i, :]), A("ps0", s_[:, i:C:L]))

        def own(k):
            b, a = k // 2, k % 2 * (C // 2)
            acopy(col("fw%d" % b, wl + a, C // 2), col("ps%d" % (4 + b), a, C // 2))
        for k in range(2):
            own(k)
        act(A("z0", s_[:, 7:78:3]), A("et", s_[:, :, 0:8:7]), Act.Abs)
        act(A("z0", s_[:, 14:78:3]), A("et", s_[:, 0:11, 0:8:7]), Act.Abs)
        act(A("z1", s_[:, 0:70:3]), A("et", s_[:, :, 0:8:7]), Act.Abs)
        act(A("z1", s_[:, 8:78:3]), A("et", s_[:, :, 1:7:5]), Act.Abs)

        def m_at(s, j, n, lanes):
            if s < 2:
                a = 6 * j + 7 + s
                return A("zo" if s else "z0", s_[:, a:a + 6 * n - (2 if lanes == 2 else 5):6 // lanes])
            return A("mm", s_[:, s, 4 * j + 5:4 * j + 4 * n + (4 if lanes == 2 else 2):4 // lanes])

        def sides(s):
            tt(A("zl", s_[:, s, 1:36:3]), m_at(s, 1, 12, 1), A("tt", s_[:, s, 1:46:4]), Op.is_lt)
            tt(A("zl", s_[:, s, 2:36:3]), A("tt", s_[:, s, 5:50:4]), m_at(s, -1, 12, 1), Op.is_lt)

        def carry(s):
            for w in range(min(s + 1, 2)):
                p = 32 * ((s - w) // 2 + 1)
                scan(A("lb", s_[0:p, s + 1, 3 + 39 * w:39 + 39 * w]), A("zl", s_[0:p, s, :]),
                     A("lb", s_[0:p, s, 4 + 39 * w:40 + 39 * w]), 0.0, Op.mult, Op.max)
                if s < 6:
                    beside(s + 1, w)

        def step_scan(s):
            if s == 0:
                scan(col("zo", 0, 78), col("z0", 0, 78), A("z1"), 0.0, Op.min, Op.max)
            else:
                scan(A("mm", s_[:, s + 1, 4:52]), A("tt", s_[:, s, 0:48]), A("mm", s_[:, s, 9:57]), 0.0, Op.min, Op.max)

        def cost(s):
            red(col(land, 0), A("meet"), Op.min)
            send("cost%d" % t, [(shared_engines(r, others), col(land, 0),
                                 [(T.cores[o], col(land, slot(r, o))) for o in others])])
        for s in range(7):
            if s == 3:
                tt(col("meet", 0, 24), A("mm", s_[:, 3, 5:53:2]), A("mm", s_[:, 3, 7:55:2]), Op.max)
                tt(col("meet", 24, 12), A("mm", s_[:, 3, 5:53:4]), A("mm", s_[:, 3, 11:59:4]), Op.max)
            tt(A("tt", s_[:, s, 1:56:2]), m_at(s, -1, 14, 2), m_at(s, 0, 14, 2), Op.min)
            if s == 1:
                acopy(A("mm", s_[:, 1, 5:53:2]), m_at(1, 0, 12, 2))
            else:
                k = max(s, 1)
                far = 6 - k if k < 3 else k + 9
                act(A("mm", s_[:, k, 10:58:2]), A("et", s_[:, :, k + 1:far + 1:far - k - 1]), Act.Abs)
            if s < 5:
                own(2 + s)
            elif t == 0:
                tile_constants(s)
            for what, k in STEPS[s]:
                {"scan": step_scan, "cost": cost, "sides": sides, "carry": carry, "across": across}[what](k)
        ts(col("pm", 0, 12), A("mm", s_[:, 7, 5:53:4]), col(land, 0), Op.is_gt)
        carry(6)
        own(7)
        back = A("pm", s_[:, 11::-1])
        scan(col(pw, 8, 12), back, A("lb", s_[:, 7, 38:4:-3]), 0.0, Op.mult, Op.max)
        scan(A(pw, s_[:, 31:19:-1]), back, A("lb", s_[:, 7, 77:43:-3]), 0.0, Op.mult, Op.max)
        at = {o: places_at(o)[1 if o < r else 0] for o in neighbours(r)}
        send_pair("place%d" % t, {o: (col(pw, 19, 2), col(pw, at[o], 2)) for o in neighbours(r)})
        if t == 0:
            tile_constants(7)
            if hend > PADC:
                for k in range(R):
                    quant(col("hq%d" % k, PADC, 128), col("hz%d" % k, PADC, 128), col("xs", 0, 512))
            dma("S", A("wq", None, "u8"), A("wc"), col(pw, 19, 2))
            dma("S", A("wz"), A("ws"))
        arrival("halo%d" % t, sum(2 * len(topo.engines(h, core)) for o in neighbours(r)
                                  for h, x, k, es in relays(T, topo, o) if x == r), [A(hq, s_[:, h0:PADC]), A(hz, s_[:, h0:PADC])])
        for b in range(4):
            mm(b, "idq", "idz", 128 * b, hq, hz, h0, hend)

        def unpack(when):
            for b in UNPACK[t].get(when, ()):
                if wl:
                    acopy(col("fw%d" % b, 0, wl), col("ps%d" % b, 0, wl))
                if wr:
                    acopy(col("fw%d" % b, wl + C, wr), col("ps%d" % b, wl, wr))
        unpack("costs")
        arrival("cost%d" % t, sum(len(shared_engines(o, [x for x in range(N) if x != o])) for o in others),
                [col(land, 4, 7)])
        for k in range(4):
            (acopy if k % 2 else copy)(col("cg", 64 * k, 64), ind(col(land, 0, 11), col("cl", 4 * k, 4)))
        copy(col("cg", 256, 16), ind(col(land, 0, 11), col("cl", 16, 1)))
        for k in range(4):
            transp(col("ct", 64 * k, 64), col("cg", 64 * k, 64))
        sel = [col("cg", 256)] + [col("cg", S * b) for b in extra]
        for h in range(nh):
            for k in range(2):
                ts(col("ne%d" % h, 128 * k, 128), col("ct", 128 * k, 128), sel[h], Op.not_equal, -1.0, Op.mult)
                act(col("sj%d" % h, 128 * k, 128), col("ct", 128 * k, 128), Act.Sign, sel[h], -1.0, col("sg", 2 * h + k))
        for h in range(nh):
            const("th%d" % h, 0, 32, col("sg", 2 * h + 1))
        for h in range(nh):
            scan(col("sc%d" % h, 0, 257), col("m%d" % h, 0, 257), col("ne%d" % h, 0, 257), col("sg", 2 * h), Op.mult, Op.add)
        for b in sorted(blocks, key=lambda b: b in extra):
            h, a = (1, 0) if b in extra else (0, b - first)
            act(A("fb", s_[0:32, S * (b - lo):S * (b - lo) + S]), A("th%d" % h, s_[32 * a:32 * a + 32, :]), Act.Sign,
                A("sc%d" % h, s_[32 * a:32 * a + 32, 256:257]), -1.0)
        unpack("sigma")
        arrival("place%d" % t, sum(share(o) for o in neighbours(r)), [A(pw, s_[:, 32:pend])])
        tt(A("pb"), ind(col(pw, 8, pend - 8), col("cl", 18, 6)), A("pc"), Op.add)
        if t == R - 1:
            quant(A("vq"), A("vz"), A("vs"))
        transp(A("prow"), A("pb"))
        for a in range(4):
            transp(A("fr", s_[32 * a:32 * a + 32, 0:nrow]), A("fb", s_[0:32, 0:nrow]))
        scan(A("dg"), A("dm"), col("prow", 16, 64), BIG, Op.add, Op.min)
        if low:
            scan(col("sx", 1, win + 63), col("c12", 0, win + 63), col("fr", 0, win + 63), float(-C * r + (L - 1) * S * lo),
                 Op.add, Op.subtract)
        else:
            down = s_[:, nrow - 1:win - 2:-1]
            scan(A("sx", down), A("c12", down), A("fr", down), float(C * (N - r) + (L - 1) * S * (hi - N + 1)),
                 Op.add, Op.add)
        start, sig = col("sx", win, 64), col("fr", win, 64)
        before, sigb = col("sx", win - 1), col("fr", win - 1, 64)
        vo = col("vo", 0, 4)
        nq, nz = "tq%d" % (t + 1), "tz%d" % (t + 1)

        def rows(k):
            lin(A("fh"), sig, -0.25, 0.75 + 16 * L - wl + L)
            lin(col("mw", 0, 64), sig, -1.0, 0.0)
            lin(col("kw", 64, 63), col("fr", win, 63), -1.0, 0.0)
            acopy(col("mw", 127, 64), sig)

        def counts(k):
            for n in range(3 * k, 3 * k + 3):
                act(A("cmp", s_[:, n, :]), start, Act.Sign, col("thr", n), -1.0, col("cnt", n))

        def lists(k):
            ts(col("l3", 4 * k, 3), col("cnt", 3 * k, 3), 0.5, Op.mult, col("cc", B3), Op.add)
            ts(col("l1", 4 * k, 3), col("cnt", 3 * k, 3), col("cc", A1), Op.mult, col("cc", B1), Op.add)

        def seam_parts(b, by):
            by(A("vt", s_[:, b:256:4]), ind(col("fw%d" % b, 0, hb), vo))

        def layer_of_seams(k):
            quant(A("vtq"), A("vtz"), A("vt"))
            for b in range(4):
                mm(4 + b, "wq", "wz", 128 * b, "vtq", "vtz", 0, 128)

        def seams_made(k):
            for b in range(4):
                act(col("fw%d" % b, hb, 64), col("ps%d" % (4 + b), 0, 64), Act.Relu, None, 0.03125)

        def beside_the_tile(k):
            if t == 0:
                dma("S", A("vs"), A("v"), col("eo", 0, 12))
            if t == R - 1:
                ts(A("olb"), col("prow", 32, 32), float(-wl), Op.add)
                dma("S", A("ol"), A("olb", s_[0:128:16, :]))

        def part(k, e, by):
            a, b = PIECES[k]
            by(A("ee", s_[:, 4 * a + e:4 * b:4]), ind(col("fw%d" % e, 0, hb + 64), A("eo", s_[:, a // 16:b // 16])))

        def second(name, k, at):
            return A(name, s_[:, 96 * k + at:96 * k + at + 95:2])
        step = {
            "rows": rows, "counts": counts, "lists": lists, "qv": layer_of_seams, "h": seams_made, "out": beside_the_tile,
            "unpack": lambda k: unpack("counts"),
            "vo": lambda k: copy(vo, A("dg", s_[:, 15:64:16])),
            "tau": lambda k: tt(col("mw", 64, 63), col("fr", win, 63), col("fr", win + 1, 63), Op.mult),
            "zz": lambda k: tt(A("zz"), col("prow", 16, 64), A("fh"), Op.add),
            "fp": lambda k: scan(A("fp"), col("ck", 96, 64), sigb, before, Op.add, Op.subtract),
            "kw": lambda k: scan(col("kw", 0, 64), col("one", 0, 64), sigb, before, Op.add, Op.subtract),
            "hk": lambda k: tt(col("kw", 127, 64), sig, A("hk"), Op.mult),
            "tp": lambda k: tt(col("tp", 8, 64), A("zz"), A("fp"), Op.add),
            "vv": lambda k: seam_parts(k, copy), "va": lambda k: seam_parts(k, acopy),
            "signs": lambda k: acopy(second("d0", k, 1), ind(col("mw", 0, 191), col("l3", 4 * k, 3))),
            "terms": lambda k: tt(second("d1", k, 0), ind(col("kw", 0, 191), col("l3", 4 * k, 3)), col("ck", 48 * k, 48), Op.add),
            "passed": lambda k: tt(second("d1", k, 1), ind(A("tp"), col("l1", 4 * k, 3)), col("cge", 48 * k, 48), Op.is_le),
            "other": lambda k: tt(second("d0", k, 2), ind(A("tp"), col("l1", 4 * k, 3)), col("cn", 48 * k, 48), Op.not_equal),
            "sum": lambda k: scan(col("hs", 96 * k, 96), col("d0", 96 * k, 96), col("d1", 96 * k, 96), 0.0, Op.mult, Op.add),
            "list": lambda k: copy(col("eo", 12 * k, 12), A("hs", s_[:, 96 * k + 7:96 * k + 96:8])),
            "ev": lambda k: part(k // 4, k % 4, copy), "ea": lambda k: part(k // 4, k % 4, acopy),
            "qe": lambda k: quant_run("eq8", "ez", "ee", *PIECES[k]),
        }
        for name in ORDER.split():
            step[name[:-1]](int(name[-1]))

        def pack(k):
            a, b = PIECES[k]
            quant_run(nq, nz, "xn", a, b)
            if t == R - 1:
                dma("S", A("oc", s_[:, 4 * a:4 * b]), A(nq, s_[:, a:b], "u8"))
        for k, (a, b) in enumerate(PIECES):
            for e in range(5):
                if e < 4:
                    mm(e, "wq", "wz", 128 * e, "eq8", "ez", a, b)
                if e > 0:
                    mm(3 + e, "idq", "idz", 128 * (e - 1), "eq8", "ez", a, b)
            for e in range(4):
                rl = col("rl", C * e + a, b - a)
                act(rl, col("ps%d" % e, 0, b - a), Act.Relu, None, 0.015625)
                tt(A("xn", s_[:, 4 * a + e:4 * b:4]), col("ps%d" % (4 + e), 0, b - a), rl, Op.add)
                if k > 0 and e == (0 if t == R - 1 else 3):
                    pack(k - 1)
        pack(len(PIECES) - 1)

    tq, tz = "tq%d" % R, "tz%d" % R
    for k, (a, b) in enumerate(PIECES):
        mm(k, "vq", "vz", 0, tq, tz, a, b)
        if k == len(PIECES) - 1:
            for j in range(4):
                dma("S" if j < 2 else "A", A("osc", s_[4 * j:4 * j + 4, :]), A(tz, s_[32 * j:32 * j + 4, :]))
            copy(col("ys", a, b - a), col("ps%d" % k, 0, b - a))
        else:
            acopy(col("ys", a, b - a), col("ps%d" % k, 0, b - a))
        dma("A", A("y", s_[:, a:b]), col("ys", a, b - a))
    emit()
